import numpy as np
import ml_dtypes


def mxq(x, axis, fmt="e4m3"):
    dtype, down = {"e4m3": (ml_dtypes.float8_e4m3fn, 7), "e5m2": (ml_dtypes.float8_e5m2, 14)}[fmt]
    v = np.moveaxis(np.asarray(x, np.float32).astype(ml_dtypes.bfloat16).astype(np.float64), axis, -1)
    blocks = v.reshape(v.shape[:-1] + (-1, 32))
    amax = np.abs(blocks).max(-1, keepdims=True)
    byte = np.maximum(np.where(amax > 0, np.frexp(amax)[1] - 1 + 127, 0) - down, 1)
    scale = np.exp2(byte - 127.0)
    codes = (blocks / scale).astype(np.float32).astype(dtype).astype(np.float64)
    return np.moveaxis((codes * scale).reshape(v.shape), -1, axis)


WIDE = False


def mx_kscale(k):
    if not WIDE:
        return np.ones(k)
    levels = np.array([10, -10, 5, -5, 0])
    if k % 512:
        return np.exp2(np.random.permutation(np.resize(levels, k // 32))).repeat(32)
    a = np.empty((k // 512, 16))
    for p in range(k // 512):
        a[p, :8] = np.random.permutation(np.resize(levels, 8))
        for g in range(8):
            far = levels[np.abs(levels - a[p, g]) >= 10]
            a[p, g + 8] = far[np.random.randint(len(far))]
    return np.exp2(a.ravel()).repeat(32)


def f64(x):
    return np.asarray(x).astype(np.float64)


def striped(idx):
    return np.tile(idx.reshape(-1, 16).T, (8, 1)).astype(np.uint16)


def unstriped(offs):
    return offs[:16].T.reshape(-1).astype(np.int64)


def pack_weight(w):
    k, n = w.shape
    w = f64(np.asarray(w, np.float32).astype(ml_dtypes.bfloat16)).reshape(k // 32, 32, n)
    amax = np.abs(w).max(1)
    byte = np.clip(np.where(amax > 0, np.frexp(amax)[1] - 1 + 127 - 7, 1), 1, 254)
    scaled = (w * np.exp2(127.0 - byte)[:, None, :]).reshape(k, n).astype(np.float32)
    words = np.ascontiguousarray(scaled.reshape(k // 512, 128, 4, n).transpose(0, 1, 3, 2)).astype(ml_dtypes.float8_e4m3fn).view(np.uint8)
    return words, np.ascontiguousarray(byte.astype(np.uint8).reshape(k // 512, 16, n))


def unpack_weight(words, scales):
    g, p, n, _ = words.shape
    vals = np.ascontiguousarray(words).view(ml_dtypes.float8_e4m3fn).astype(np.float64) * np.repeat(np.exp2(scales.astype(np.float64) - 127.0), 8, axis=1)[..., None]
    return vals.transpose(0, 1, 3, 2).reshape(g * 512, n)


def planes(y):
    n, m = y.shape
    v = y.astype(np.float32).astype(ml_dtypes.bfloat16).astype(np.float64).reshape(n // 32, 32, m)
    top = np.abs(v).max(1)
    byte = np.clip(np.where(top > 0, np.frexp(top)[1] - 1 + 127 - 7, 1), 1, 254)
    codes = (v * np.exp2(127.0 - byte)[:, None, :]).reshape(n, m).astype(np.float32).astype(ml_dtypes.float8_e4m3fn).view(np.uint8)
    words = codes.reshape(n // 512, 128, 4, m).transpose(0, 1, 3, 2)
    return np.ascontiguousarray(words), np.ascontiguousarray(byte.astype(np.uint8).reshape(n // 512, 16, m))


K, T, S, N, D = 512, 1024, 512, 512, 2
P = 2 ** 7


def setup_inputs():
    n = np.random.standard_normal
    s = mx_kscale(K)[:, None]
    packed_xT = pack_weight(n((K, T)) * s)
    return {
        "x_words": packed_xT[0],
        "x_scales": packed_xT[1],
        "w1": (n((K, N)) / np.sqrt(K) / s).astype(np.float32),
        "gate": (np.tile(np.random.uniform(0.3, 0.6, (D, 1, S)), (1, P, 1))).astype(np.float32),
        "coef": (0.6 * n((N, 3)) + 0.3).astype(np.float32),
        "offs": striped(np.random.permutation(T)[:S]),
        "pos1": striped(np.random.permutation(S)[:S]),
        "pos2": striped(np.random.permutation(S)[:S]),
    }


def reference(x_words, x_scales, w1, gate, coef, offs, pos1, pos2):
    xq = unpack_weight(x_words, x_scales)[:, unstriped(offs)]
    h = mxq(f64(w1), 0, "e4m3").T @ xq
    gg = h[:, unstriped(pos1)] * f64(gate)[0, :1] + h[:, unstriped(pos2)] * f64(gate)[1, :1]
    ee = gg[:, unstriped(pos1)] * f64(gate)[0, :1] + gg[:, unstriped(pos2)] * f64(gate)[1, :1]
    out_0 = f64(coef)[:, 0:1] * h + f64(coef)[:, 1:2] * gg + f64(coef)[:, 2:3] * ee
    return (out_0,) + planes(out_0)

@@ -1,0 +1,207 @@
+from contextlib import ExitStack
+
+import concourse.mybir as mybir
+from concourse.masks import make_identity
+
+K, T, S, N = 512, 1024, 512, 512
+FLOPS = 2 * K * S * N
+
+F32 = mybir.dt.float32
+BF16 = mybir.dt.bfloat16
+I32 = mybir.dt.int32
+U32 = mybir.dt.uint32
+U16 = mybir.dt.uint16
+U8 = mybir.dt.uint8
+FP8X4 = mybir.dt.float8_e4m3fn_x4
+MULT = mybir.AluOpType.mult
+ADD = mybir.AluOpType.add
+COPY = mybir.ActivationFunctionType.Copy
+
+P = 128
+PACK = 4
+SPARE = 8
+BLOCKS = S // P
+CHUNKS = ((0, 256), (256, 384))
+LAST = 384
+
+
+def tile_picked_ygpr_none_po_kernel(
+    tc, x_words, x_scales, w1, gate, coef, offs, pos1, pos2, out_0, out_1, out_2
+):
+    nc = tc.nc
+    with ExitStack() as ctx:
+        sb = ctx.enter_context(tc.tile_pool(name="sb", bufs=1))
+        ps = ctx.enter_context(tc.psum_pool(name="ps", bufs=1))
+
+        def bank(tag, name):
+            return ps.tile([P, S], F32, tag=tag, name=name)
+
+        def turn(out, in_, start, stop):
+            nc.tensor.matmul(out, lhsT=in_, rhs=ident[:], start=start, stop=stop, is_transpose=True)
+
+        def block(b):
+            return slice(b * P, (b + 1) * P)
+
+        picks = sb.tile([P, S // 16], U16, name="picks")
+        nc.sync.dma_start(picks[:], offs)
+        xs = sb.tile([P, T], U8, name="xs")
+        nc.gpsimd.memset(xs[:].bitcast(I32), 0)
+        for q in range(4):
+            nc.sync.dma_start(xs[32 * q : 32 * q + 4, :].bitcast(I32), x_scales[0, 4 * q : 4 * q + 4, :].bitcast(I32))
+        w_rows = w1.rearrange("(p j) c -> p j c", j=PACK)
+        w_raw = [sb.tile([P, PACK, N // 2], F32, name=f"w_raw{u}") for u in range(2)]
+        for u in range(2):
+            nc.sync.dma_start(w_raw[u][:], w_rows[:, :, u * (N // 2) : (u + 1) * (N // 2)])
+        xw = sb.tile([P, T], I32, name="xw")
+        nc.sync.dma_start(xw[:], x_words[0].rearrange("p n t -> p (n t)").bitcast(I32))
+        lists = [sb.tile([P, S // 16], U16, name=f"list{d}") for d in range(2)]
+        nc.sync.dma_start(lists[0][:], pos1)
+        nc.sync.dma_start(lists[1][:], pos2)
+        gates = [sb.tile([P, S], F32, name=f"gate{d}") for d in range(2)]
+        for d in range(2):
+            nc.sync.dma_start(gates[d][:], gate[d])
+        cf = sb.tile([P, PACK * 3], F32, name="cf")
+        nc.sync.dma_start(cf[:], coef.rearrange("(p t) c -> p (t c)", t=PACK))
+
+        def c(t, depth):
+            return cf[:, 3 * t + depth : 3 * t + depth + 1]
+
+        ident = sb.tile([P, P], F32, name="ident")
+        make_identity(nc, ident[:])
+        h = [sb.tile([P, S + SPARE], F32, name=f"h{t}") for t in range(PACK)]
+        for t in range(PACK):
+            nc.gpsimd.memset(h[t][:, S:], 0.0)
+
+        xq_scale = sb.tile([P, S], U8, name="xq_scale", align_bytes=64)
+        nc.vector.tensor_copy(xq_scale[:], xs[:].indirect(picks[:]))
+
+        wb = sb.tile([P, PACK, P, PACK], BF16, name="wb", align_bytes=64)
+        wq = sb.tile([P, N], U32, name="wq", align_bytes=64)
+        ws = sb.tile([P, N], U8, name="ws", align_bytes=64)
+        for u, copy in enumerate((nc.scalar.copy, nc.vector.tensor_copy)):
+            copy(
+                wb[:, :, 64 * u : 64 * u + 64, :].rearrange("p t m j -> p m t j"),
+                w_raw[u][:].rearrange("p j (m t) -> p m t j", t=PACK),
+            )
+        nc.vector.quantize_mx(out=wq[:].bitcast(FP8X4), scales=ws[:], in_=wb[:].rearrange("p t m j -> p (t m j)"))
+        xq = sb.tile([P, S], U32, name="xq", tag="wb", align_bytes=64)
+
+        def project(t, acc, cols):
+            nc.tensor.matmul_mx(
+                out=acc[:, cols], lhsT=wq[:, block(t)].bitcast(FP8X4), lhsT_scale=ws[:, block(t)],
+                rhs=xq[:, cols].bitcast(FP8X4), rhs_scale=xq_scale[:, cols], start=True, stop=True,
+            )
+            nc.scalar.copy(h[t][:, cols], acc[:, cols])
+
+        for u in range(2):
+            cols = slice(u * 256, (u + 1) * 256)
+            nc.vector.tensor_copy(xq[:, cols], xw[:].bitcast(U32).indirect(picks[:, u * 16 : (u + 1) * 16]))
+            project(0, bank(f"back{u}", f"h_ps0_{u}"), cols)
+        for t in range(1, PACK):
+            project(t, bank(f"acc{t}", f"h_ps{t}"), slice(0, S))
+        h0 = [sb.tile([P, S], F32, name=f"h_c0_{t}") for t in range(PACK)]
+        for t in range(PACK):
+            nc.scalar.activation(h0[t][:], h[t][:, :S], COPY, scale=c(t, 0))
+
+        sums = [bank(f"acc{b}", f"sum{b}") for b in range(BLOCKS)]
+        g1 = [sb.tile([P, S], F32, name=f"gg_c1_{t}") for t in range(PACK)]
+        g2 = [sb.tile([P, S], F32, name=f"gg_c2_{t}") for t in range(PACK)]
+
+        def first_gather(t):
+            fwd = bank(f"fwd{t % 2}", f"fwd{t}")
+            for d in range(2):
+                m = sb.tile([P, S], F32, name=f"m{t}_{d}")
+                nc.vector.tensor_tensor(m[:], h[t][:].indirect(lists[d][:]), gates[d][:], MULT)
+                for b in range(BLOCKS):
+                    turn(fwd[:, block(b)], m[:, block(b)], d == 0 and b == 0, d == 1 and b == BLOCKS - 1)
+            return fwd
+
+        def first_back(t, fwd):
+            turned = sb.tile([P, S], F32, name=f"gg_turned{t}")
+            nc.scalar.copy(turned[:], fwd[:])
+            back = bank(f"back{t % 2}", f"back{t}")
+            for b in range(BLOCKS):
+                turn(back[:, block(b)], turned[:, block(b)], True, True)
+            nc.scalar.activation(g2[t][:], back[:], COPY, scale=c(t, 2))
+            nc.scalar.activation(g1[t][:], back[:], COPY, scale=c(t, 1))
+
+        def add_term(term, t, blocks, start, stop):
+            for b in blocks:
+                turn(sums[b][:, block(t)], term[t][:, block(b)], start, stop and b == BLOCKS - 1)
+
+        fwd = first_gather(0)
+        for t in range(PACK):
+            nxt = first_gather(t + 1) if t + 1 < PACK else None
+            first_back(t, fwd)
+            add_term(h0, t, range(BLOCKS), t == 0, False)
+            if t > 0:
+                add_term(g1, t - 1, range(BLOCKS), False, False)
+            fwd = nxt
+
+        y_rows = out_0.rearrange("(p t) n -> p t n", t=PACK)
+        yb = sb.tile([P, S, PACK], BF16, name="yb", align_bytes=64)
+        yq = sb.tile([P, S], U32, name="yq", align_bytes=64)
+        ys = sb.tile([P, S], U8, name="ys", align_bytes=64)
+        words_out = out_1[0].rearrange("p n t -> p (n t)").bitcast(I32)
+
+        def turn_back(b):
+            turned = sb.tile([P, S], F32, name=f"y_turned{b}")
+            nc.scalar.copy(turned[:], sums[b][:])
+            back = bank(f"back{b % 2}", f"y_back{b}")
+            for t in range(PACK):
+                turn(back[:, block(t)], turned[:, block(t)], True, True)
+            y = sb.tile([P, PACK, P], F32, name=f"y{b}")
+            nc.scalar.copy(y[:], back[:].rearrange("p (t n) -> p t n", t=PACK))
+            return back, y
+
+        def finish(b):
+            back, y = turn_back(b)
+            nc.sync.dma_start(y_rows[:, :, block(b)], y[:])
+            nc.scalar.copy(yb[:, block(b), :], back[:].rearrange("p (t n) -> p n t", t=PACK))
+
+        def quantise(lo, hi):
+            nc.vector.quantize_mx(
+                out=yq[:, lo:hi].bitcast(FP8X4), scales=ys[:, lo:hi], in_=yb[:, lo:hi, :].rearrange("p n t -> p (n t)")
+            )
+
+        base = None
+        for lo, hi in CHUNKS:
+            for t in range(PACK):
+                if t == PACK - 1 and lo == 0:
+                    add_term(g1, t, range(BLOCKS), False, True)
+                for d in range(2):
+                    if lo > 0 and t < 2:
+                        e = gates[d][:, block(t)]
+                    else:
+                        e = sb.tile([P, hi - lo], F32, name=f"e{lo}_{t}_{d}", tag=f"e{lo}_{t}_{d}")[:]
+                    nc.vector.tensor_tensor(e, g2[t][:].indirect(lists[d][:, lo // 16 : hi // 16]), gates[d][:, lo:hi], MULT)
+                    for b in range(lo // P, hi // P):
+                        turn(sums[b][:, block(t)], e[:, b * P - lo : (b + 1) * P - lo], False, t == PACK - 1 and d == 1)
+            if lo == 0:
+                base = turn_back(BLOCKS - 1)[1]
+            for b in range(lo // P, hi // P):
+                finish(b)
+
+        e_last = [sb.tile([P, PACK, P], F32, name=f"e_last{d}", tag=f"e0_3_{d}") for d in range(2)]
+        part = sb.tile([P, PACK, P], F32, name="part")
+        y_last = sb.tile([P, PACK, P], F32, name="y_last")
+        for d in range(2):
+            for t in range(PACK):
+                nc.vector.tensor_tensor(e_last[d][:, t, :], g2[t][:].indirect(lists[d][:, LAST // 16 :]), gates[d][:, LAST:], MULT)
+                if d == 1 and t == 0:
+                    nc.vector.tensor_tensor(part[:], e_last[0][:], base[:], ADD)
+        quantise(0, 256)
+        for u in range(2):
+            cols = slice(64 * u, 64 * u + 64)
+            nc.vector.tensor_tensor(y_last[:, :, cols], part[:, :, cols], e_last[1][:, :, cols], ADD)
+        nc.scalar.dma_start(y_rows[:, :, LAST:], y_last[:])
+        for u in range(2):
+            cols = slice(64 * u, 64 * u + 64)
+            nc.vector.tensor_copy(yb[:, LAST + 64 * u : LAST + 64 * u + 64, :], y_last[:, :, cols].rearrange("p t n -> p n t"))
+        quantise(256, 384)
+        nc.sync.dma_start(words_out[:, :LAST], yq[:, :LAST].bitcast(I32))
+        quantise(LAST, S)
+        nc.sync.dma_start(words_out[:, LAST:], yq[:, LAST:].bitcast(I32))
+        for q in range(4):
+            eng = nc.sync if q % 2 else nc.scalar
+            eng.dma_start(out_2[0, 4 * q : 4 * q + 4, :].bitcast(I32), ys[32 * q : 32 * q + 4, :].bitcast(I32))

@@ -49,7 +49,7 @@ def tile_picked_ygpr_none_po_kernel(
         for q in range(4):
             nc.sync.dma_start(xs[32 * q : 32 * q + 4, :].bitcast(I32), x_scales[0, 4 * q : 4 * q + 4, :].bitcast(I32))
         w_rows = w1.rearrange("(p j) c -> p j c", j=PACK)
-        w_raw = [sb.tile([P, PACK, N // 2], F32, name=f"w_raw{u}") for u in range(2)]
+        w_raw = [sb.tile([P, PACK, N // 2], F32, name=f"w_raw{u}", align_bytes=64) for u in range(2)]
         for u in range(2):
             nc.sync.dma_start(w_raw[u][:], w_rows[:, :, u * (N // 2) : (u + 1) * (N // 2)])
         xw = sb.tile([P, T], I32, name="xw")
@@ -78,13 +78,24 @@ def tile_picked_ygpr_none_po_kernel(
         wb = sb.tile([P, PACK, P, PACK], BF16, name="wb", align_bytes=64)
         wq = sb.tile([P, N], U32, name="wq", align_bytes=64)
         ws = sb.tile([P, N], U8, name="ws", align_bytes=64)
-        for u, copy in enumerate((nc.scalar.copy, nc.vector.tensor_copy)):
+        for u, lo, hi, copy in (
+            (0, 0, 64, nc.vector.tensor_copy),
+            (1, 0, 20, nc.scalar.copy),
+            (1, 20, 64, nc.vector.tensor_copy),
+        ):
             copy(
-                wb[:, :, 64 * u : 64 * u + 64, :].rearrange("p t m j -> p m t j"),
-                w_raw[u][:].rearrange("p j (m t) -> p m t j", t=PACK),
+                wb[:, :, 64 * u + lo : 64 * u + hi, :].rearrange("p t m j -> p m t j"),
+                w_raw[u][:].rearrange("p j (m t) -> p m t j", t=PACK)[:, lo:hi],
             )
-        nc.vector.quantize_mx(out=wq[:].bitcast(FP8X4), scales=ws[:], in_=wb[:].rearrange("p t m j -> p (t m j)"))
-        xq = sb.tile([P, S], U32, name="xq", tag="wb", align_bytes=64)
+
+        def quantise_weights(lo, hi):
+            nc.vector.quantize_mx(
+                out=wq[:, lo * P : hi * P].bitcast(FP8X4), scales=ws[:, lo * P : hi * P],
+                in_=wb[:, lo:hi].rearrange("p t m j -> p (t m j)"),
+            )
+
+        quantise_weights(0, 1)
+        xq = sb.tile([P, S], U32, name="xq", tag="w_raw1", align_bytes=64)
 
         def project(t, acc, cols):
             nc.tensor.matmul_mx(
@@ -93,10 +104,11 @@ def tile_picked_ygpr_none_po_kernel(
             )
             nc.scalar.copy(h[t][:, cols], acc[:, cols])
 
-        for u in range(2):
-            cols = slice(u * 256, (u + 1) * 256)
-            nc.vector.tensor_copy(xq[:, cols], xw[:].bitcast(U32).indirect(picks[:, u * 16 : (u + 1) * 16]))
-            project(0, bank(f"back{u}", f"h_ps0_{u}"), cols)
+        for u, (lo, hi) in enumerate(((0, 256), (256, 384), (384, 512))):
+            nc.vector.tensor_copy(xq[:, lo:hi], xw[:].bitcast(U32).indirect(picks[:, lo // 16 : hi // 16]))
+            project(0, bank(("back0", "back1", "fwd1")[u], f"h_ps0_{u}"), slice(lo, hi))
+        quantise_weights(1, 2)
+        quantise_weights(2, 4)
         for t in range(1, PACK):
             project(t, bank(f"acc{t}", f"h_ps{t}"), slice(0, S))
         h0 = [sb.tile([P, S], F32, name=f"h_c0_{t}") for t in range(PACK)]
@@ -107,36 +119,49 @@ def tile_picked_ygpr_none_po_kernel(
         g1 = [sb.tile([P, S], F32, name=f"gg_c1_{t}") for t in range(PACK)]
         g2 = [sb.tile([P, S], F32, name=f"gg_c2_{t}") for t in range(PACK)]
 
-        def first_gather(t):
+        m = [[sb.tile([P, S], F32, name=f"m{t}_{d}") for d in range(2)] for t in range(PACK)]
+
+        def first_gather(t, d):
+            nc.vector.tensor_tensor(m[t][d][:], h[t][:].indirect(lists[d][:]), gates[d][:], MULT)
+
+        def scale_gg(t, gg):
+            nc.scalar.activation(g2[t][:], gg, COPY, scale=c(t, 2))
+            nc.scalar.activation(g1[t][:], gg, COPY, scale=c(t, 1))
+
+        def sum_on_tensor(t):
             fwd = bank(f"fwd{t % 2}", f"fwd{t}")
             for d in range(2):
-                m = sb.tile([P, S], F32, name=f"m{t}_{d}")
-                nc.vector.tensor_tensor(m[:], h[t][:].indirect(lists[d][:]), gates[d][:], MULT)
+                first_gather(t, d)
                 for b in range(BLOCKS):
-                    turn(fwd[:, block(b)], m[:, block(b)], d == 0 and b == 0, d == 1 and b == BLOCKS - 1)
-            return fwd
-
-        def first_back(t, fwd):
+                    turn(fwd[:, block(b)], m[t][d][:, block(b)], d == 0 and b == 0, d == 1 and b == BLOCKS - 1)
             turned = sb.tile([P, S], F32, name=f"gg_turned{t}")
             nc.scalar.copy(turned[:], fwd[:])
             back = bank(f"back{t % 2}", f"back{t}")
             for b in range(BLOCKS):
                 turn(back[:, block(b)], turned[:, block(b)], True, True)
-            nc.scalar.activation(g2[t][:], back[:], COPY, scale=c(t, 2))
-            nc.scalar.activation(g1[t][:], back[:], COPY, scale=c(t, 1))
+            scale_gg(t, back[:])
+
+        def sum_on_vector(t):
+            gg = sb.tile([P, S], F32, name=f"gg{t}")
+            nc.vector.tensor_tensor(gg[:], m[t][0][:], m[t][1][:], ADD)
+            scale_gg(t, gg[:])
 
         def add_term(term, t, blocks, start, stop):
             for b in blocks:
                 turn(sums[b][:, block(t)], term[t][:, block(b)], start, stop and b == BLOCKS - 1)
 
-        fwd = first_gather(0)
-        for t in range(PACK):
-            nxt = first_gather(t + 1) if t + 1 < PACK else None
-            first_back(t, fwd)
-            add_term(h0, t, range(BLOCKS), t == 0, False)
-            if t > 0:
-                add_term(g1, t - 1, range(BLOCKS), False, False)
-            fwd = nxt
+        for t in range(2):
+            sum_on_tensor(t)
+            for tt in (2 * t, 2 * t + 1):
+                add_term(h0, tt, range(BLOCKS), tt == 0, False)
+        for t in range(2):
+            add_term(g1, t, range(BLOCKS), False, False)
+        first_gather(2, 0)
+        first_gather(2, 1)
+        first_gather(3, 0)
+        sum_on_vector(2)
+        add_term(g1, 2, range(BLOCKS), False, False)
+        first_gather(3, 1)
 
         y_rows = out_0.rearrange("(p t) n -> p t n", t=PACK)
         yb = sb.tile([P, S, PACK], BF16, name="yb", align_bytes=64)
@@ -167,8 +192,6 @@ def tile_picked_ygpr_none_po_kernel(
         base = None
         for lo, hi in CHUNKS:
             for t in range(PACK):
-                if t == PACK - 1 and lo == 0:
-                    add_term(g1, t, range(BLOCKS), False, True)
                 for d in range(2):
                     if lo > 0 and t < 2:
                         e = gates[d][:, block(t)]
@@ -177,6 +200,9 @@ def tile_picked_ygpr_none_po_kernel(
                     nc.vector.tensor_tensor(e, g2[t][:].indirect(lists[d][:, lo // 16 : hi // 16]), gates[d][:, lo:hi], MULT)
                     for b in range(lo // P, hi // P):
                         turn(sums[b][:, block(t)], e[:, b * P - lo : (b + 1) * P - lo], False, t == PACK - 1 and d == 1)
+                    if lo == 0 and t == 0 and d == 0:
+                        sum_on_vector(PACK - 1)
+                        add_term(g1, PACK - 1, range(BLOCKS), False, True)
             if lo == 0:
                 base = turn_back(BLOCKS - 1)[1]
             for b in range(lo // P, hi // P):

@@ -21,7 +21,6 @@ P = 128
 PACK = 4
 SPARE = 8
 BLOCKS = S // P
-CHUNKS = ((0, 256), (256, 384))
 LAST = 384
 
 
@@ -42,17 +41,17 @@ def tile_picked_ygpr_none_po_kernel(
         def block(b):
             return slice(b * P, (b + 1) * P)
 
+        w_rows = w1.rearrange("(p j) c -> p j c", j=PACK)
+        w_raw = [sb.tile([P, PACK, N // 2], F32, name=f"w_raw{u}", align_bytes=64) for u in range(2)]
+        nc.sync.dma_start(w_raw[0][:], w_rows[:, :, : N // 2])
         picks = sb.tile([P, S // 16], U16, name="picks")
         nc.sync.dma_start(picks[:], offs)
         xs = sb.tile([P, T], U8, name="xs")
         nc.gpsimd.memset(xs[:].bitcast(I32), 0)
         for q in range(4):
             nc.sync.dma_start(xs[32 * q : 32 * q + 4, :].bitcast(I32), x_scales[0, 4 * q : 4 * q + 4, :].bitcast(I32))
-        w_rows = w1.rearrange("(p j) c -> p j c", j=PACK)
-        w_raw = [sb.tile([P, PACK, N // 2], F32, name=f"w_raw{u}", align_bytes=64) for u in range(2)]
-        for u in range(2):
-            nc.sync.dma_start(w_raw[u][:], w_rows[:, :, u * (N // 2) : (u + 1) * (N // 2)])
-        xw = sb.tile([P, T], I32, name="xw")
+        nc.sync.dma_start(w_raw[1][:], w_rows[:, :, N // 2 :])
+        xw = sb.tile([P, T], I32, name="xw", align_bytes=64)
         nc.sync.dma_start(xw[:], x_words[0].rearrange("p n t -> p (n t)").bitcast(I32))
         lists = [sb.tile([P, S // 16], U16, name=f"list{d}") for d in range(2)]
         nc.sync.dma_start(lists[0][:], pos1)
@@ -76,12 +75,17 @@ def tile_picked_ygpr_none_po_kernel(
         nc.vector.tensor_copy(xq_scale[:], xs[:].indirect(picks[:]))
 
         wb = sb.tile([P, PACK, P, PACK], BF16, name="wb", align_bytes=64)
-        wq = sb.tile([P, N], U32, name="wq", align_bytes=64)
+        wq = [sb.tile([P, P], U32, name="wq_first", align_bytes=64)]
+
+        def codes(lo, hi):
+            return wq[0][:] if lo == 0 else wq[1][:, (lo - 1) * P : (hi - 1) * P]
+
         ws = sb.tile([P, N], U8, name="ws", align_bytes=64)
         for u, lo, hi, copy in (
-            (0, 0, 64, nc.vector.tensor_copy),
-            (1, 0, 20, nc.scalar.copy),
-            (1, 20, 64, nc.vector.tensor_copy),
+            (0, 0, 32, nc.scalar.copy),
+            (0, 32, 64, nc.vector.tensor_copy),
+            (1, 0, 24, nc.scalar.copy),
+            (1, 24, 64, nc.vector.tensor_copy),
         ):
             copy(
                 wb[:, :, 64 * u + lo : 64 * u + hi, :].rearrange("p t m j -> p m t j"),
@@ -90,7 +94,7 @@ def tile_picked_ygpr_none_po_kernel(
 
         def quantise_weights(lo, hi):
             nc.vector.quantize_mx(
-                out=wq[:, lo * P : hi * P].bitcast(FP8X4), scales=ws[:, lo * P : hi * P],
+                out=codes(lo, hi).bitcast(FP8X4), scales=ws[:, lo * P : hi * P],
                 in_=wb[:, lo:hi].rearrange("p t m j -> p (t m j)"),
             )
 
@@ -99,7 +103,7 @@ def tile_picked_ygpr_none_po_kernel(
 
         def project(t, acc, cols):
             nc.tensor.matmul_mx(
-                out=acc[:, cols], lhsT=wq[:, block(t)].bitcast(FP8X4), lhsT_scale=ws[:, block(t)],
+                out=acc[:, cols], lhsT=codes(t, t + 1).bitcast(FP8X4), lhsT_scale=ws[:, block(t)],
                 rhs=xq[:, cols].bitcast(FP8X4), rhs_scale=xq_scale[:, cols], start=True, stop=True,
             )
             nc.scalar.copy(h[t][:, cols], acc[:, cols])
@@ -107,6 +111,7 @@ def tile_picked_ygpr_none_po_kernel(
         for u, (lo, hi) in enumerate(((0, 256), (256, 384), (384, 512))):
             nc.vector.tensor_copy(xq[:, lo:hi], xw[:].bitcast(U32).indirect(picks[:, lo // 16 : hi // 16]))
             project(0, bank(("back0", "back1", "fwd1")[u], f"h_ps0_{u}"), slice(lo, hi))
+        wq.append(sb.tile([P, 3 * P], U32, name="wq_rest", tag="xw", align_bytes=64))
         quantise_weights(1, 2)
         quantise_weights(2, 4)
         for t in range(1, PACK):
@@ -116,8 +121,9 @@ def tile_picked_ygpr_none_po_kernel(
             nc.scalar.activation(h0[t][:], h[t][:, :S], COPY, scale=c(t, 0))
 
         sums = [bank(f"acc{b}", f"sum{b}") for b in range(BLOCKS)]
-        g1 = [sb.tile([P, S], F32, name=f"gg_c1_{t}") for t in range(PACK)]
-        g2 = [sb.tile([P, S], F32, name=f"gg_c2_{t}") for t in range(PACK)]
+        g1, g2 = [], []
+        g1_tags = ("gg_c1_0", "gg_c1_1", "m1_1", "gg_c1_1")
+        g2_tags = ("gg_c2_0", "gg_c2_1", "gg_turned1", "gg2")
 
         m = [[sb.tile([P, S], F32, name=f"m{t}_{d}") for d in range(2)] for t in range(PACK)]
 
@@ -125,6 +131,8 @@ def tile_picked_ygpr_none_po_kernel(
             nc.vector.tensor_tensor(m[t][d][:], h[t][:].indirect(lists[d][:]), gates[d][:], MULT)
 
         def scale_gg(t, gg):
+            g2.append(sb.tile([P, S], F32, name=f"gg_c2_{t}", tag=g2_tags[t]))
+            g1.append(sb.tile([P, S], F32, name=f"gg_c1_{t}", tag=g1_tags[t]))
             nc.scalar.activation(g2[t][:], gg, COPY, scale=c(t, 2))
             nc.scalar.activation(g1[t][:], gg, COPY, scale=c(t, 1))
 
@@ -148,14 +156,21 @@ def tile_picked_ygpr_none_po_kernel(
 
         def add_term(term, t, blocks, start, stop):
             for b in blocks:
-                turn(sums[b][:, block(t)], term[t][:, block(b)], start, stop and b == BLOCKS - 1)
+                turn(sums[b][:, block(t)], term[t][:, block(b)], start, stop)
+
+        def sum_cols(b, t):
+            if b == 2 and t == PACK - 1:
+                return late_sum[:, :P]
+            return sums[b][:, block(t)]
 
         for t in range(2):
             sum_on_tensor(t)
             for tt in (2 * t, 2 * t + 1):
-                add_term(h0, tt, range(BLOCKS), tt == 0, False)
+                add_term(h0, tt, [b for b in range(BLOCKS) if (b, tt) != (2, 3)], tt == 0, False)
         for t in range(2):
             add_term(g1, t, range(BLOCKS), False, False)
+        late_sum = bank("fwd0", "late_sum")
+        turn(late_sum[:, :P], h0[3][:, block(2)], True, False)
         first_gather(2, 0)
         first_gather(2, 1)
         first_gather(3, 0)
@@ -169,18 +184,28 @@ def tile_picked_ygpr_none_po_kernel(
         ys = sb.tile([P, S], U8, name="ys", align_bytes=64)
         words_out = out_1[0].rearrange("p n t -> p (n t)").bitcast(I32)
 
-        def turn_back(b):
+        def second_gather(e, t, d, lo, hi):
+            nc.vector.tensor_tensor(e, g2[t][:].indirect(lists[d][:, lo // 16 : hi // 16]), gates[d][:, lo:hi], MULT)
+
+        def turn_back(b, tag):
             turned = sb.tile([P, S], F32, name=f"y_turned{b}")
-            nc.scalar.copy(turned[:], sums[b][:])
-            back = bank(f"back{b % 2}", f"y_back{b}")
-            for t in range(PACK):
-                turn(back[:, block(t)], turned[:, block(t)], True, True)
-            y = sb.tile([P, PACK, P], F32, name=f"y{b}")
-            nc.scalar.copy(y[:], back[:].rearrange("p (t n) -> p t n", t=PACK))
-            return back, y
+            back = bank(tag, f"y_back{b}")
+            if b == 2:
+                nc.scalar.copy(turned[:, : 3 * P], sums[b][:, : 3 * P])
+                for t in range(3):
+                    turn(back[:, block(t)], turned[:, block(t)], True, True)
+                nc.scalar.copy(turned[:, 3 * P :], late_sum[:, :P])
+                turn(back[:, block(3)], turned[:, block(3)], True, True)
+            else:
+                nc.scalar.copy(turned[:], sums[b][:])
+                for t in range(PACK):
+                    turn(back[:, block(t)], turned[:, block(t)], True, True)
+            return back
 
         def finish(b):
-            back, y = turn_back(b)
+            back = turn_back(b, f"back{b % 2}")
+            y = sb.tile([P, PACK, P], F32, name=f"y{b}")
+            nc.scalar.copy(y[:], back[:].rearrange("p (t n) -> p t n", t=PACK))
             nc.sync.dma_start(y_rows[:, :, block(b)], y[:])
             nc.scalar.copy(yb[:, block(b), :], back[:].rearrange("p (t n) -> p n t", t=PACK))
 
@@ -189,45 +214,49 @@ def tile_picked_ygpr_none_po_kernel(
                 out=yq[:, lo:hi].bitcast(FP8X4), scales=ys[:, lo:hi], in_=yb[:, lo:hi, :].rearrange("p n t -> p (n t)")
             )
 
-        base = None
-        for lo, hi in CHUNKS:
-            for t in range(PACK):
-                for d in range(2):
-                    if lo > 0 and t < 2:
-                        e = gates[d][:, block(t)]
-                    else:
-                        e = sb.tile([P, hi - lo], F32, name=f"e{lo}_{t}_{d}", tag=f"e{lo}_{t}_{d}")[:]
-                    nc.vector.tensor_tensor(e, g2[t][:].indirect(lists[d][:, lo // 16 : hi // 16]), gates[d][:, lo:hi], MULT)
-                    for b in range(lo // P, hi // P):
-                        turn(sums[b][:, block(t)], e[:, b * P - lo : (b + 1) * P - lo], False, t == PACK - 1 and d == 1)
-                    if lo == 0 and t == 0 and d == 0:
-                        sum_on_vector(PACK - 1)
-                        add_term(g1, PACK - 1, range(BLOCKS), False, True)
-            if lo == 0:
-                base = turn_back(BLOCKS - 1)[1]
-            for b in range(lo // P, hi // P):
-                finish(b)
-
-        e_last = [sb.tile([P, PACK, P], F32, name=f"e_last{d}", tag=f"e0_3_{d}") for d in range(2)]
-        part = sb.tile([P, PACK, P], F32, name="part")
+        for t in range(PACK):
+            for d in range(2):
+                e = sb.tile([P, P], F32, name=f"e0_{t}_{d}")
+                second_gather(e[:], t, d, 0, P)
+                turn(sums[0][:, block(t)], e[:], False, t == PACK - 1 and d == 1)
+                if t == 0 and d == 0:
+                    sum_on_vector(PACK - 1)
+                    for b in range(BLOCKS):
+                        turn(sum_cols(b, 3), g1[3][:, block(b)], False, False)
+        finish(0)
+        rest = sb.tile([P, 24 * P], F32, name="e_rest", tag="gg3")
+        for t in range(PACK):
+            for d in range(2):
+                e = rest[:, block(2 * t + d)]
+                second_gather(e, t, d, P, 2 * P)
+                turn(sums[1][:, block(t)], e, False, t == PACK - 1 and d == 1)
+        finish(1)
+        for t in range(PACK):
+            second_gather(rest[:, (8 + 2 * t) * P : (10 + 2 * t) * P], t, 0, 2 * P, S)
+            turn(sums[3][:, block(t)], rest[:, block(9 + 2 * t)], False, t == PACK - 1)
+            turn(sum_cols(2, t), rest[:, block(8 + 2 * t)], False, False)
+        base = turn_back(3, "fwd1")
+        for t in range(PACK):
+            second_gather(rest[:, block(16 + t)], t, 1, 2 * P, LAST)
+            turn(sum_cols(2, t), rest[:, block(16 + t)], False, t >= 2)
+        finish(2)
+        for t in range(PACK):
+            second_gather(rest[:, block(20 + t)], t, 1, LAST, S)
+        e_last = rest[:, 20 * P :].rearrange("p (t n) -> p t n", t=PACK)
+        base_t = base[:].rearrange("p (t n) -> p t n", t=PACK)
         y_last = sb.tile([P, PACK, P], F32, name="y_last")
-        for d in range(2):
-            for t in range(PACK):
-                nc.vector.tensor_tensor(e_last[d][:, t, :], g2[t][:].indirect(lists[d][:, LAST // 16 :]), gates[d][:, LAST:], MULT)
-                if d == 1 and t == 0:
-                    nc.vector.tensor_tensor(part[:], e_last[0][:], base[:], ADD)
         quantise(0, 256)
+        nc.sync.dma_start(words_out[:, :256], yq[:, :256].bitcast(I32))
         for u in range(2):
             cols = slice(64 * u, 64 * u + 64)
-            nc.vector.tensor_tensor(y_last[:, :, cols], part[:, :, cols], e_last[1][:, :, cols], ADD)
-        nc.scalar.dma_start(y_rows[:, :, LAST:], y_last[:])
+            nc.vector.tensor_tensor(y_last[:, :, cols], e_last[:, :, cols], base_t[:, :, cols], ADD)
+        nc.sync.dma_start(y_rows[:, :, LAST:], y_last[:])
         for u in range(2):
             cols = slice(64 * u, 64 * u + 64)
             nc.vector.tensor_copy(yb[:, LAST + 64 * u : LAST + 64 * u + 64, :], y_last[:, :, cols].rearrange("p t n -> p n t"))
-        quantise(256, 384)
-        nc.sync.dma_start(words_out[:, :LAST], yq[:, :LAST].bitcast(I32))
         quantise(LAST, S)
-        nc.sync.dma_start(words_out[:, LAST:], yq[:, LAST:].bitcast(I32))
+        quantise(256, 384)
+        nc.sync.dma_start(words_out[:, 256:], yq[:, 256:].bitcast(I32))
         for q in range(4):
             eng = nc.sync if q % 2 else nc.scalar
             eng.dma_start(out_2[0, 4 * q : 4 * q + 4, :].bitcast(I32), ys[32 * q : 32 * q + 4, :].bitcast(I32))

@@ -41,18 +41,18 @@ def tile_picked_ygpr_none_po_kernel(
         def block(b):
             return slice(b * P, (b + 1) * P)
 
-        w_rows = w1.rearrange("(p j) c -> p j c", j=PACK)
-        w_raw = [sb.tile([P, PACK, N // 2], F32, name=f"w_raw{u}", align_bytes=64) for u in range(2)]
-        nc.sync.dma_start(w_raw[0][:], w_rows[:, :, : N // 2])
+        xw = sb.tile([P, T], I32, name="xw")
+        nc.sync.dma_start(xw[:], x_words[0].rearrange("p n t -> p (n t)").bitcast(I32))
         picks = sb.tile([P, S // 16], U16, name="picks")
         nc.sync.dma_start(picks[:], offs)
         xs = sb.tile([P, T], U8, name="xs")
         nc.gpsimd.memset(xs[:].bitcast(I32), 0)
         for q in range(4):
             nc.sync.dma_start(xs[32 * q : 32 * q + 4, :].bitcast(I32), x_scales[0, 4 * q : 4 * q + 4, :].bitcast(I32))
-        nc.sync.dma_start(w_raw[1][:], w_rows[:, :, N // 2 :])
-        xw = sb.tile([P, T], I32, name="xw", align_bytes=64)
-        nc.sync.dma_start(xw[:], x_words[0].rearrange("p n t -> p (n t)").bitcast(I32))
+        w_rows = w1.rearrange("(p j) c -> p j c", j=PACK)
+        w_raw = [sb.tile([P, PACK, N // 2], F32, name=f"w_raw{u}") for u in range(2)]
+        for u in range(2):
+            nc.sync.dma_start(w_raw[u][:], w_rows[:, :, u * (N // 2) : (u + 1) * (N // 2)])
         lists = [sb.tile([P, S // 16], U16, name=f"list{d}") for d in range(2)]
         nc.sync.dma_start(lists[0][:], pos1)
         nc.sync.dma_start(lists[1][:], pos2)
@@ -61,6 +61,10 @@ def tile_picked_ygpr_none_po_kernel(
             nc.sync.dma_start(gates[d][:], gate[d])
         cf = sb.tile([P, PACK * 3], F32, name="cf")
         nc.sync.dma_start(cf[:], coef.rearrange("(p t) c -> p (t c)", t=PACK))
+
+        cf_half = [sb.tile([P, 3], F32, name=f"cf_half{u}") for u in range(2)]
+        for u in range(2):
+            nc.sync.dma_start(cf_half[u][:], coef.rearrange("(u p t) c -> u t p c", u=2, t=PACK)[u, 0:2])
 
         def c(t, depth):
             return cf[:, 3 * t + depth : 3 * t + depth + 1]
@@ -71,59 +75,59 @@ def tile_picked_ygpr_none_po_kernel(
         for t in range(PACK):
             nc.gpsimd.memset(h[t][:, S:], 0.0)
 
+        xq = sb.tile([P, S], U32, name="xq", align_bytes=64)
+        nc.vector.tensor_copy(xq[:], xw[:].bitcast(U32).indirect(picks[:]))
         xq_scale = sb.tile([P, S], U8, name="xq_scale", align_bytes=64)
         nc.vector.tensor_copy(xq_scale[:], xs[:].indirect(picks[:]))
 
-        wb = sb.tile([P, PACK, P, PACK], BF16, name="wb", align_bytes=64)
-        wq = [sb.tile([P, P], U32, name="wq_first", align_bytes=64)]
-
-        def codes(lo, hi):
-            return wq[0][:] if lo == 0 else wq[1][:, (lo - 1) * P : (hi - 1) * P]
-
+        wb_high = sb.tile([P, 2, P, PACK], BF16, name="wb_high", align_bytes=64)
+        wq = sb.tile([P, N], U32, name="wq", align_bytes=64)
         ws = sb.tile([P, N], U8, name="ws", align_bytes=64)
-        for u, lo, hi, copy in (
-            (0, 0, 32, nc.scalar.copy),
-            (0, 32, 64, nc.vector.tensor_copy),
-            (1, 0, 24, nc.scalar.copy),
-            (1, 24, 64, nc.vector.tensor_copy),
-        ):
+
+        def round_low(u, copy):
+            wb_low = sb.tile([P, P, PACK], BF16, name=f"wb_low{u}", tag="wb_low", align_bytes=64)
             copy(
-                wb[:, :, 64 * u + lo : 64 * u + hi, :].rearrange("p t m j -> p m t j"),
-                w_raw[u][:].rearrange("p j (m t) -> p m t j", t=PACK)[:, lo:hi],
+                wb_low[:].rearrange("p (t m) j -> p m t j", t=2),
+                w_raw[u][:].rearrange("p j (m t) -> p m t j", t=PACK)[:, :, 0:2],
+            )
+            quantise_weights(u, u + 1, wb_low[:].rearrange("p m j -> p (m j)"))
+
+        def round_high(u, copy):
+            copy(
+                wb_high[:, :, 64 * u : 64 * u + 64, :].rearrange("p t m j -> p m t j"),
+                w_raw[u][:].rearrange("p j (m t) -> p m t j", t=PACK)[:, :, 2:4],
             )
 
-        def quantise_weights(lo, hi):
+        def quantise_weights(lo, hi, rounded):
             nc.vector.quantize_mx(
-                out=codes(lo, hi).bitcast(FP8X4), scales=ws[:, lo * P : hi * P],
-                in_=wb[:, lo:hi].rearrange("p t m j -> p (t m j)"),
+                out=wq[:, lo * P : hi * P].bitcast(FP8X4), scales=ws[:, lo * P : hi * P],
+                in_=rounded,
             )
-
-        quantise_weights(0, 1)
-        xq = sb.tile([P, S], U32, name="xq", tag="w_raw1", align_bytes=64)
 
         def project(t, acc, cols):
             nc.tensor.matmul_mx(
-                out=acc[:, cols], lhsT=codes(t, t + 1).bitcast(FP8X4), lhsT_scale=ws[:, block(t)],
+                out=acc[:, cols], lhsT=wq[:, block(t)].bitcast(FP8X4), lhsT_scale=ws[:, block(t)],
                 rhs=xq[:, cols].bitcast(FP8X4), rhs_scale=xq_scale[:, cols], start=True, stop=True,
             )
             nc.scalar.copy(h[t][:, cols], acc[:, cols])
 
-        for u, (lo, hi) in enumerate(((0, 256), (256, 384), (384, 512))):
-            nc.vector.tensor_copy(xq[:, lo:hi], xw[:].bitcast(U32).indirect(picks[:, lo // 16 : hi // 16]))
-            project(0, bank(("back0", "back1", "fwd1")[u], f"h_ps0_{u}"), slice(lo, hi))
-        wq.append(sb.tile([P, 3 * P], U32, name="wq_rest", tag="xw", align_bytes=64))
-        quantise_weights(1, 2)
-        quantise_weights(2, 4)
+        round_low(0, nc.scalar.copy)
+        round_high(0, nc.scalar.copy)
+        for u in range(2):
+            project(0, bank(f"back{u}", f"h_ps0_{u}"), slice(256 * u, 256 * u + 256))
+        round_low(1, nc.vector.tensor_copy)
+        round_high(1, nc.scalar.copy)
+        quantise_weights(2, 4, wb_high[:].rearrange("p t m j -> p (t m j)"))
         for t in range(1, PACK):
             project(t, bank(f"acc{t}", f"h_ps{t}"), slice(0, S))
         h0 = [sb.tile([P, S], F32, name=f"h_c0_{t}") for t in range(PACK)]
         for t in range(PACK):
-            nc.scalar.activation(h0[t][:], h[t][:, :S], COPY, scale=c(t, 0))
+            nc.scalar.activation(h0[t][:], h[t][:, :S], COPY, scale=cf_half[t][:, 0:1] if t < 2 else c(t, 0))
 
         sums = [bank(f"acc{b}", f"sum{b}") for b in range(BLOCKS)]
-        g1, g2 = [], []
-        g1_tags = ("gg_c1_0", "gg_c1_1", "m1_1", "gg_c1_1")
-        g2_tags = ("gg_c2_0", "gg_c2_1", "gg_turned1", "gg2")
+        ggs, g1, g2 = [], [], []
+        g1_tags = ("gg_c1_0", "gg_c1_1", "gg_c1_1", "gg2")
+        g2_tags = ("gg_c2_0", "gg_c2_1", "gg_turned1", "gg_c1_0")
 
         m = [[sb.tile([P, S], F32, name=f"m{t}_{d}") for d in range(2)] for t in range(PACK)]
 
@@ -132,21 +136,27 @@ def tile_picked_ygpr_none_po_kernel(
 
         def scale_gg(t, gg):
             g2.append(sb.tile([P, S], F32, name=f"gg_c2_{t}", tag=g2_tags[t]))
-            g1.append(sb.tile([P, S], F32, name=f"gg_c1_{t}", tag=g1_tags[t]))
             nc.scalar.activation(g2[t][:], gg, COPY, scale=c(t, 2))
-            nc.scalar.activation(g1[t][:], gg, COPY, scale=c(t, 1))
+            ggs.append(gg)
 
-        def sum_on_tensor(t):
-            fwd = bank(f"fwd{t % 2}", f"fwd{t}")
+        def scale_middle(t):
+            g1.append(sb.tile([P, S], F32, name=f"gg_c1_{t}", tag=g1_tags[t]))
+            nc.scalar.activation(g1[t][:], ggs[t], COPY, scale=c(t, 1))
+
+        turned = sb.tile([P, 2, BLOCKS, 2, 64], F32, name="gg_turned1")
+
+        def sum_half(u):
+            fwd = bank(f"fwd{u}", f"fwd{u}")
             for d in range(2):
-                first_gather(t, d)
+                first_gather(u, d)
                 for b in range(BLOCKS):
-                    turn(fwd[:, block(b)], m[t][d][:, block(b)], d == 0 and b == 0, d == 1 and b == BLOCKS - 1)
-            turned = sb.tile([P, S], F32, name=f"gg_turned{t}")
-            nc.scalar.copy(turned[:], fwd[:])
-            back = bank(f"back{t % 2}", f"back{t}")
+                    turn(fwd[:, block(b)], m[u][d][:, block(b)], d == 0 and b == 0, d == 1 and b == BLOCKS - 1)
+            nc.scalar.copy(turned[:, :, :, u, :], fwd[:].rearrange("n (b t p) -> n t b p", b=BLOCKS, t=2))
+
+        def turn_sum_back(t):
+            back = bank(f"back{t}", f"back{t}")
             for b in range(BLOCKS):
-                turn(back[:, block(b)], turned[:, block(b)], True, True)
+                turn(back[:, block(b)], turned[:, t, b].rearrange("n u p -> n (u p)"), True, True)
             scale_gg(t, back[:])
 
         def sum_on_vector(t):
@@ -159,23 +169,33 @@ def tile_picked_ygpr_none_po_kernel(
                 turn(sums[b][:, block(t)], term[t][:, block(b)], start, stop)
 
         def sum_cols(b, t):
-            if b == 2 and t == PACK - 1:
-                return late_sum[:, :P]
+            if t == PACK - 1 and b < BLOCKS - 1:
+                return late_sums[b][:, :P]
             return sums[b][:, block(t)]
 
+        for u in range(2):
+            sum_half(u)
+            for b in range(BLOCKS):
+                turn(sums[b][:].rearrange("n (t u p) -> n u t p", t=PACK, u=2)[:, u, 0:2], h0[u][:, block(b)], u == 0, False)
         for t in range(2):
-            sum_on_tensor(t)
-            for tt in (2 * t, 2 * t + 1):
-                add_term(h0, tt, [b for b in range(BLOCKS) if (b, tt) != (2, 3)], tt == 0, False)
-        for t in range(2):
-            add_term(g1, t, range(BLOCKS), False, False)
-        late_sum = bank("fwd0", "late_sum")
-        turn(late_sum[:, :P], h0[3][:, block(2)], True, False)
+            turn_sum_back(t)
+        add_term(h0, 2, range(BLOCKS), False, False)
+        add_term(h0, 3, [BLOCKS - 1], False, False)
+        late_sums = []
+
+        def open_late(b):
+            late_sums.append(bank(f"fwd{b % 2}", f"late_sum{b}"))
+            turn(sum_cols(b, 3), h0[3][:, block(b)], True, False)
+
+        for b in range(2):
+            open_late(b)
         first_gather(2, 0)
         first_gather(2, 1)
         first_gather(3, 0)
         sum_on_vector(2)
-        add_term(g1, 2, range(BLOCKS), False, False)
+        for t in range(2):
+            scale_middle(t)
+            add_term(g1, t, range(BLOCKS), False, False)
         first_gather(3, 1)
 
         y_rows = out_0.rearrange("(p t) n -> p t n", t=PACK)
@@ -190,20 +210,17 @@ def tile_picked_ygpr_none_po_kernel(
         def turn_back(b, tag):
             turned = sb.tile([P, S], F32, name=f"y_turned{b}")
             back = bank(tag, f"y_back{b}")
-            if b == 2:
-                nc.scalar.copy(turned[:, : 3 * P], sums[b][:, : 3 * P])
-                for t in range(3):
-                    turn(back[:, block(t)], turned[:, block(t)], True, True)
-                nc.scalar.copy(turned[:, 3 * P :], late_sum[:, :P])
-                turn(back[:, block(3)], turned[:, block(3)], True, True)
-            else:
-                nc.scalar.copy(turned[:], sums[b][:])
-                for t in range(PACK):
-                    turn(back[:, block(t)], turned[:, block(t)], True, True)
+            nc.scalar.copy(turned[:, : 3 * P], sums[b][:, : 3 * P])
+            for t in range(3):
+                turn(back[:, block(t)], turned[:, block(t)], True, True)
+            nc.scalar.copy(turned[:, 3 * P :], sum_cols(b, 3))
+            turn(back[:, block(3)], turned[:, block(3)], True, True)
+            if b == 0:
+                open_late(2)
+                turn(sum_cols(2, 3), g1[3][:, block(2)], False, False)
             return back
 
-        def finish(b):
-            back = turn_back(b, f"back{b % 2}")
+        def hand_out(b, back):
             y = sb.tile([P, PACK, P], F32, name=f"y{b}")
             nc.scalar.copy(y[:], back[:].rearrange("p (t n) -> p t n", t=PACK))
             nc.sync.dma_start(y_rows[:, :, block(b)], y[:])
@@ -214,42 +231,56 @@ def tile_picked_ygpr_none_po_kernel(
                 out=yq[:, lo:hi].bitcast(FP8X4), scales=ys[:, lo:hi], in_=yb[:, lo:hi, :].rearrange("p n t -> p (n t)")
             )
 
+        def fetch(b, t, d):
+            if b == 0:
+                e = sb.tile([P, P], F32, name=f"e{t}_{d}")[:]
+            else:
+                e = rest[0][:, block(8 * (b - 1) + 4 * d + t)]
+            second_gather(e, t, d, b * P, (b + 1) * P)
+            return e
+
+        backs = []
+        rest = []
+        for b in range(2):
+            for t in range(PACK):
+                for d in range(2):
+                    turn(sum_cols(b, t), fetch(b, t, d), False, d == 1 and t >= 2)
+                    if b == 0 and t == 0 and d == 0:
+                        sum_on_vector(PACK - 1)
+                        scale_middle(2)
+                        add_term(g1, 2, range(BLOCKS), False, False)
+                        scale_middle(3)
+                        rest.append(sb.tile([P, 24 * P], F32, name="e_rest", tag="gg3"))
+                        for bb in (0, 1, 3):
+                            turn(sum_cols(bb, 3), g1[3][:, block(bb)], False, False)
+            backs.append(turn_back(b, f"back{b}"))
+        hand_out(0, backs[0])
         for t in range(PACK):
-            for d in range(2):
-                e = sb.tile([P, P], F32, name=f"e0_{t}_{d}")
-                second_gather(e[:], t, d, 0, P)
-                turn(sums[0][:, block(t)], e[:], False, t == PACK - 1 and d == 1)
-                if t == 0 and d == 0:
-                    sum_on_vector(PACK - 1)
-                    for b in range(BLOCKS):
-                        turn(sum_cols(b, 3), g1[3][:, block(b)], False, False)
-        finish(0)
-        rest = sb.tile([P, 24 * P], F32, name="e_rest", tag="gg3")
+            e = rest[0][:, (8 + 2 * t) * P : (10 + 2 * t) * P]
+            second_gather(e, t, 0, 2 * P, S)
+            turn(sum_cols(3, t), e[:, block(1)], False, t == PACK - 1)
+            turn(sum_cols(2, t), e[:, block(0)], False, False)
+        hand_out(1, backs[1])
+        base = bank("acc0", "base")
+        base_turned = sb.tile([P, S], F32, name="base_turned")
+        nc.scalar.copy(base_turned[:], sums[3][:])
         for t in range(PACK):
-            for d in range(2):
-                e = rest[:, block(2 * t + d)]
-                second_gather(e, t, d, P, 2 * P)
-                turn(sums[1][:, block(t)], e, False, t == PACK - 1 and d == 1)
-        finish(1)
+            turn(base[:, block(t)], base_turned[:, block(t)], True, True)
         for t in range(PACK):
-            second_gather(rest[:, (8 + 2 * t) * P : (10 + 2 * t) * P], t, 0, 2 * P, S)
-            turn(sums[3][:, block(t)], rest[:, block(9 + 2 * t)], False, t == PACK - 1)
-            turn(sum_cols(2, t), rest[:, block(8 + 2 * t)], False, False)
-        base = turn_back(3, "fwd1")
+            e = rest[0][:, block(16 + t)]
+            second_gather(e, t, 1, 2 * P, LAST)
+            turn(sum_cols(2, t), e, False, t >= 2)
+        hand_out(2, turn_back(2, "back0"))
         for t in range(PACK):
-            second_gather(rest[:, block(16 + t)], t, 1, 2 * P, LAST)
-            turn(sum_cols(2, t), rest[:, block(16 + t)], False, t >= 2)
-        finish(2)
-        for t in range(PACK):
-            second_gather(rest[:, block(20 + t)], t, 1, LAST, S)
-        e_last = rest[:, 20 * P :].rearrange("p (t n) -> p t n", t=PACK)
-        base_t = base[:].rearrange("p (t n) -> p t n", t=PACK)
+            fetch(3, t, 1)
         y_last = sb.tile([P, PACK, P], F32, name="y_last")
         quantise(0, 256)
         nc.sync.dma_start(words_out[:, :256], yq[:, :256].bitcast(I32))
+        e_all = rest[0][:, 20 * P :].rearrange("p (t n) -> p t n", t=PACK)
+        base_t = base[:].rearrange("p (t n) -> p t n", t=PACK)
         for u in range(2):
             cols = slice(64 * u, 64 * u + 64)
-            nc.vector.tensor_tensor(y_last[:, :, cols], e_last[:, :, cols], base_t[:, :, cols], ADD)
+            nc.vector.tensor_tensor(y_last[:, :, cols], e_all[:, :, cols], base_t[:, :, cols], ADD)
         nc.sync.dma_start(y_rows[:, :, LAST:], y_last[:])
         for u in range(2):
             cols = slice(64 * u, 64 * u + 64)

@@ -21,7 +21,7 @@ P = 128
 PACK = 4
 SPARE = 8
 BLOCKS = S // P
-LAST = 384
+LAST = 256
 
 
 def tile_picked_ygpr_none_po_kernel(
@@ -135,8 +135,9 @@ def tile_picked_ygpr_none_po_kernel(
             nc.vector.tensor_tensor(m[t][d][:], h[t][:].indirect(lists[d][:]), gates[d][:], MULT)
 
         def scale_gg(t, gg):
-            g2.append(sb.tile([P, S], F32, name=f"gg_c2_{t}", tag=g2_tags[t]))
-            nc.scalar.activation(g2[t][:], gg, COPY, scale=c(t, 2))
+            g2.append(sb.tile([P, S + SPARE], F32, name=f"gg_c2_{t}", tag=g2_tags[t]))
+            nc.gpsimd.memset(g2[t][:, S:], 0.0)
+            nc.scalar.activation(g2[t][:, :S], gg, COPY, scale=c(t, 2))
             ggs.append(gg)
 
         def scale_middle(t):
@@ -164,38 +165,32 @@ def tile_picked_ygpr_none_po_kernel(
             nc.vector.tensor_tensor(gg[:], m[t][0][:], m[t][1][:], ADD)
             scale_gg(t, gg[:])
 
-        def add_term(term, t, blocks, start, stop):
-            for b in blocks:
-                turn(sums[b][:, block(t)], term[t][:, block(b)], start, stop)
-
         def sum_cols(b, t):
-            if t == PACK - 1 and b < BLOCKS - 1:
-                return late_sums[b][:, :P]
-            return sums[b][:, block(t)]
+            if t < 2:
+                return sums[b // 2][:, block(2 * (b % 2) + t)]
+            return sums[t][:, block(b)]
+
+        def add_term(term, t, blocks, start, stop):
+            for b in range(blocks):
+                last = stop and (b == blocks - 1)
+                turn(sum_cols(b, t), term[:, block(b)], start and b == 0, last)
 
         for u in range(2):
             sum_half(u)
             for b in range(BLOCKS):
-                turn(sums[b][:].rearrange("n (t u p) -> n u t p", t=PACK, u=2)[:, u, 0:2], h0[u][:, block(b)], u == 0, False)
+                pair = sums[b // 2][:].rearrange("n (b t u p) -> n b u t p", b=2, t=2, u=2)
+                turn(pair[:, b % 2, u], h0[u][:, block(b)], u == 0 and b % 2 == 0, False)
         for t in range(2):
             turn_sum_back(t)
-        add_term(h0, 2, range(BLOCKS), False, False)
-        add_term(h0, 3, [BLOCKS - 1], False, False)
-        late_sums = []
-
-        def open_late(b):
-            late_sums.append(bank(f"fwd{b % 2}", f"late_sum{b}"))
-            turn(sum_cols(b, 3), h0[3][:, block(b)], True, False)
-
-        for b in range(2):
-            open_late(b)
+        for t in (2, 3):
+            add_term(h0[t], t, BLOCKS, True, False)
         first_gather(2, 0)
         first_gather(2, 1)
         first_gather(3, 0)
         sum_on_vector(2)
         for t in range(2):
             scale_middle(t)
-            add_term(g1, t, range(BLOCKS), False, False)
+            add_term(g1[t], t, BLOCKS, False, False)
         first_gather(3, 1)
 
         y_rows = out_0.rearrange("(p t) n -> p t n", t=PACK)
@@ -207,87 +202,73 @@ def tile_picked_ygpr_none_po_kernel(
         def second_gather(e, t, d, lo, hi):
             nc.vector.tensor_tensor(e, g2[t][:].indirect(lists[d][:, lo // 16 : hi // 16]), gates[d][:, lo:hi], MULT)
 
-        def turn_back(b, tag):
-            turned = sb.tile([P, S], F32, name=f"y_turned{b}")
-            back = bank(tag, f"y_back{b}")
-            nc.scalar.copy(turned[:, : 3 * P], sums[b][:, : 3 * P])
-            for t in range(3):
-                turn(back[:, block(t)], turned[:, block(t)], True, True)
-            nc.scalar.copy(turned[:, 3 * P :], sum_cols(b, 3))
-            turn(back[:, block(3)], turned[:, block(3)], True, True)
-            if b == 0:
-                open_late(2)
-                turn(sum_cols(2, 3), g1[3][:, block(2)], False, False)
-            return back
-
-        def hand_out(b, back):
-            y = sb.tile([P, PACK, P], F32, name=f"y{b}")
-            nc.scalar.copy(y[:], back[:].rearrange("p (t n) -> p t n", t=PACK))
-            nc.sync.dma_start(y_rows[:, :, block(b)], y[:])
-            nc.scalar.copy(yb[:, block(b), :], back[:].rearrange("p (t n) -> p n t", t=PACK))
-
         def quantise(lo, hi):
             nc.vector.quantize_mx(
                 out=yq[:, lo:hi].bitcast(FP8X4), scales=ys[:, lo:hi], in_=yb[:, lo:hi, :].rearrange("p n t -> p (n t)")
             )
 
-        def fetch(b, t, d):
-            if b == 0:
-                e = sb.tile([P, P], F32, name=f"e{t}_{d}")[:]
-            else:
-                e = rest[0][:, block(8 * (b - 1) + 4 * d + t)]
-            second_gather(e, t, d, b * P, (b + 1) * P)
-            return e
+        y = sb.tile([P, PACK, S], F32, name="y")
+        backs = [None] * PACK
 
-        backs = []
-        rest = []
-        for b in range(2):
-            for t in range(PACK):
-                for d in range(2):
-                    turn(sum_cols(b, t), fetch(b, t, d), False, d == 1 and t >= 2)
-                    if b == 0 and t == 0 and d == 0:
-                        sum_on_vector(PACK - 1)
-                        scale_middle(2)
-                        add_term(g1, 2, range(BLOCKS), False, False)
-                        scale_middle(3)
-                        rest.append(sb.tile([P, 24 * P], F32, name="e_rest", tag="gg3"))
-                        for bb in (0, 1, 3):
-                            turn(sum_cols(bb, 3), g1[3][:, block(bb)], False, False)
-            backs.append(turn_back(b, f"back{b}"))
-        hand_out(0, backs[0])
+        def come_back(t, staged, blocks):
+            for b in blocks:
+                turn(backs[t][:, block(b)], staged(b), True, True)
+
         for t in range(PACK):
-            e = rest[0][:, (8 + 2 * t) * P : (10 + 2 * t) * P]
-            second_gather(e, t, 0, 2 * P, S)
-            turn(sum_cols(3, t), e[:, block(1)], False, t == PACK - 1)
-            turn(sum_cols(2, t), e[:, block(0)], False, False)
-        hand_out(1, backs[1])
-        base = bank("acc0", "base")
-        base_turned = sb.tile([P, S], F32, name="base_turned")
-        nc.scalar.copy(base_turned[:], sums[3][:])
+            e0 = sb.tile([P, S], F32, name=f"e{t}_0")
+            second_gather(e0[:], t, 0, 0, S)
+            if t == 0:
+                sum_on_vector(PACK - 1)
+                scale_middle(2)
+                add_term(g1[2], 2, BLOCKS, False, False)
+                scale_middle(3)
+            if t == PACK - 1:
+                add_term(g1[t], t, BLOCKS, False, False)
+            add_term(e0, t, BLOCKS, False, t == 1)
+            e1 = sb.tile([P, LAST], F32, name=f"e{t}_1")
+            second_gather(e1[:], t, 1, 0, LAST)
+            add_term(e1, t, LAST // P, False, t > 0)
+            if t == 1:
+                staged = sb.tile([P, 2, S], F32, name="y_turned_pair")
+                for half in (1, 0):
+                    nc.scalar.copy(staged[:, half, :], sums[half][:])
+                for tt in range(2):
+                    backs[tt] = bank(f"back{tt}", f"y_back{tt}")
+                    come_back(tt, lambda b: staged[:, b // 2, block(2 * (b % 2) + tt)], range(BLOCKS))
+                    nc.scalar.copy(y[:, tt, :LAST], backs[tt][:, :LAST])
+                nc.sync.dma_start(y_rows[:, :2, :LAST], y[:, :2, :LAST])
+            if t > 1:
+                staged_t = sb.tile([P, S], F32, name=f"y_turned{t}")
+                backs[t] = bank(f"fwd{t - 2}", f"y_back{t}")
+                for cols in ((slice(0, S),), (slice(0, LAST), slice(LAST, S)))[t == PACK - 1]:
+                    nc.scalar.copy(staged_t[:, cols], sums[t][:, cols])
+                    come_back(t, lambda b: staged_t[:, block(b)], range(cols.start // P, cols.stop // P))
+                nc.scalar.copy(y[:, t, :LAST], backs[t][:, :LAST])
+
+        def round_block(b, copy):
+            copy(yb[:, block(b), :], y[:, :, block(b)].rearrange("p t n -> p n t"))
+
+        for b in range(LAST // P):
+            round_block(b, nc.scalar.copy)
+        e_last = sb.tile([P, PACK, S - LAST], F32, name="e_last", tag="gg3")
+
+        def finish(t):
+            nc.vector.tensor_tensor(y[:, t, LAST:], e_last[:, t, :], backs[t][:, LAST:], ADD)
+            if t == 1:
+                nc.sync.dma_start(y_rows[:, :2, LAST:], y[:, :2, LAST:])
+            if t > 1:
+                nc.sync.dma_start(y_rows[:, t, :], y[:, t, :])
+
         for t in range(PACK):
-            turn(base[:, block(t)], base_turned[:, block(t)], True, True)
-        for t in range(PACK):
-            e = rest[0][:, block(16 + t)]
-            second_gather(e, t, 1, 2 * P, LAST)
-            turn(sum_cols(2, t), e, False, t >= 2)
-        hand_out(2, turn_back(2, "back0"))
-        for t in range(PACK):
-            fetch(3, t, 1)
-        y_last = sb.tile([P, PACK, P], F32, name="y_last")
-        quantise(0, 256)
-        nc.sync.dma_start(words_out[:, :256], yq[:, :256].bitcast(I32))
-        e_all = rest[0][:, 20 * P :].rearrange("p (t n) -> p t n", t=PACK)
-        base_t = base[:].rearrange("p (t n) -> p t n", t=PACK)
-        for u in range(2):
-            cols = slice(64 * u, 64 * u + 64)
-            nc.vector.tensor_tensor(y_last[:, :, cols], e_all[:, :, cols], base_t[:, :, cols], ADD)
-        nc.sync.dma_start(y_rows[:, :, LAST:], y_last[:])
-        for u in range(2):
-            cols = slice(64 * u, 64 * u + 64)
-            nc.vector.tensor_copy(yb[:, LAST + 64 * u : LAST + 64 * u + 64, :], y_last[:, :, cols].rearrange("p t n -> p n t"))
+            second_gather(e_last[:, t, :], t, 1, LAST, S)
+            if t > 0:
+                finish(t - 1)
+        finish(PACK - 1)
+        for b in range(LAST // P, BLOCKS):
+            round_block(b, nc.vector.tensor_copy)
+        quantise(0, LAST)
         quantise(LAST, S)
-        quantise(256, 384)
-        nc.sync.dma_start(words_out[:, 256:], yq[:, 256:].bitcast(I32))
+        nc.sync.dma_start(words_out, yq[:].bitcast(I32))
         for q in range(4):
             eng = nc.sync if q % 2 else nc.scalar
             eng.dma_start(out_2[0, 4 * q : 4 * q + 4, :].bitcast(I32), ys[32 * q : 32 * q + 4, :].bitcast(I32))

@@ -120,16 +120,16 @@ def tile_picked_ygpr_none_po_kernel(
         quantise_weights(2, 4, wb_high[:].rearrange("p t m j -> p (t m j)"))
         for t in range(1, PACK):
             project(t, bank(f"acc{t}", f"h_ps{t}"), slice(0, S))
-        h0 = [sb.tile([P, S], F32, name=f"h_c0_{t}") for t in range(PACK)]
-        for t in range(PACK):
-            nc.scalar.activation(h0[t][:], h[t][:, :S], COPY, scale=cf_half[t][:, 0:1] if t < 2 else c(t, 0))
+        h0 = [sb.tile([P, S], F32, name=f"h_c0_{t}") for t in range(2)]
+        for t in range(2):
+            nc.scalar.activation(h0[t][:], h[t][:, :S], COPY, scale=cf_half[t][:, 0:1])
 
         sums = [bank(f"acc{b}", f"sum{b}") for b in range(BLOCKS)]
         ggs, g1, g2 = [], [], []
         g1_tags = ("gg_c1_0", "gg_c1_1", "gg_c1_1", "gg2")
         g2_tags = ("gg_c2_0", "gg_c2_1", "gg_turned1", "gg_c1_0")
 
-        m = [[sb.tile([P, S], F32, name=f"m{t}_{d}") for d in range(2)] for t in range(PACK)]
+        m = [[sb.tile([P, S], F32, name=f"m{t}_{d}", tag=f"m{t}_{d}") for d in range(2)] for t in range(PACK)]
 
         def first_gather(t, d):
             nc.vector.tensor_tensor(m[t][d][:], h[t][:].indirect(lists[d][:]), gates[d][:], MULT)
@@ -182,8 +182,10 @@ def tile_picked_ygpr_none_po_kernel(
                 turn(pair[:, b % 2, u], h0[u][:, block(b)], u == 0 and b % 2 == 0, False)
         for t in range(2):
             turn_sum_back(t)
+        h0_late = sb.tile([P, 2, S], F32, name="h_c0_late", tag="m1_1")
         for t in (2, 3):
-            add_term(h0[t], t, BLOCKS, True, False)
+            nc.scalar.activation(h0_late[:, t - 2, :], h[t][:, :S], COPY, scale=c(t, 0))
+            add_term(h0_late[:, t - 2, :], t, BLOCKS, True, False)
         first_gather(2, 0)
         first_gather(2, 1)
         first_gather(3, 0)

@@ -19,6 +19,7 @@ COPY = mybir.ActivationFunctionType.Copy
 
 P = 128
 PACK = 4
+HALF = N // 2
 SPARE = 8
 BLOCKS = S // P
 LAST = 256
@@ -46,13 +47,13 @@ def tile_picked_ygpr_none_po_kernel(
         picks = sb.tile([P, S // 16], U16, name="picks")
         nc.sync.dma_start(picks[:], offs)
         xs = sb.tile([P, T], U8, name="xs")
-        nc.gpsimd.memset(xs[:].bitcast(I32), 0)
+        nc.vector.memset(xs[:].bitcast(I32), 0)
         for q in range(4):
             nc.sync.dma_start(xs[32 * q : 32 * q + 4, :].bitcast(I32), x_scales[0, 4 * q : 4 * q + 4, :].bitcast(I32))
         w_rows = w1.rearrange("(p j) c -> p j c", j=PACK)
-        w_raw = [sb.tile([P, PACK, N // 2], F32, name=f"w_raw{u}") for u in range(2)]
+        w_raw = [sb.tile([P, PACK, HALF], F32, name=f"w_raw{u}") for u in range(2)]
         for u in range(2):
-            nc.sync.dma_start(w_raw[u][:], w_rows[:, :, u * (N // 2) : (u + 1) * (N // 2)])
+            nc.sync.dma_start(w_raw[u][:], w_rows[:, :, u * HALF : (u + 1) * HALF])
         lists = [sb.tile([P, S // 16], U16, name=f"list{d}") for d in range(2)]
         nc.sync.dma_start(lists[0][:], pos1)
         nc.sync.dma_start(lists[1][:], pos2)
@@ -61,10 +62,10 @@ def tile_picked_ygpr_none_po_kernel(
             nc.sync.dma_start(gates[d][:], gate[d])
         cf = sb.tile([P, PACK * 3], F32, name="cf")
         nc.sync.dma_start(cf[:], coef.rearrange("(p t) c -> p (t c)", t=PACK))
-
-        cf_half = [sb.tile([P, 3], F32, name=f"cf_half{u}") for u in range(2)]
-        for u in range(2):
-            nc.sync.dma_start(cf_half[u][:], coef.rearrange("(u p t) c -> u t p c", u=2, t=PACK)[u, 0:2])
+        cf_half = [sb.tile([P, 1], F32, name=f"cf_half{u}") for u in range(2)]
+        with nc.allow_non_contiguous_dma(reason="one coefficient a partition"):
+            for u in range(2):
+                nc.sync.dma_start(cf_half[u][:], coef.rearrange("(u m t) c -> u t m c", u=2, t=PACK)[u, 0:2, :, 0:1])
 
         def c(t, depth):
             return cf[:, 3 * t + depth : 3 * t + depth + 1]
@@ -73,7 +74,7 @@ def tile_picked_ygpr_none_po_kernel(
         make_identity(nc, ident[:])
         h = [sb.tile([P, S + SPARE], F32, name=f"h{t}") for t in range(PACK)]
         for t in range(PACK):
-            nc.gpsimd.memset(h[t][:, S:], 0.0)
+            nc.vector.memset(h[t][:, S:], 0.0)
 
         xq = sb.tile([P, S], U32, name="xq", align_bytes=64)
         nc.vector.tensor_copy(xq[:], xw[:].bitcast(U32).indirect(picks[:]))
@@ -84,7 +85,12 @@ def tile_picked_ygpr_none_po_kernel(
         wq = sb.tile([P, N], U32, name="wq", align_bytes=64)
         ws = sb.tile([P, N], U8, name="ws", align_bytes=64)
 
-        def round_low(u, copy):
+        def quantise_weights(lo, hi, rounded):
+            nc.vector.quantize_mx(
+                out=wq[:, lo * P : hi * P].bitcast(FP8X4), scales=ws[:, lo * P : hi * P], in_=rounded
+            )
+
+        def make_half_weights(u, copy):
             wb_low = sb.tile([P, P, PACK], BF16, name=f"wb_low{u}", tag="wb_low", align_bytes=64)
             copy(
                 wb_low[:].rearrange("p (t m) j -> p m t j", t=2),
@@ -92,16 +98,10 @@ def tile_picked_ygpr_none_po_kernel(
             )
             quantise_weights(u, u + 1, wb_low[:].rearrange("p m j -> p (m j)"))
 
-        def round_high(u, copy):
-            copy(
+        def round_high(u):
+            nc.scalar.copy(
                 wb_high[:, :, 64 * u : 64 * u + 64, :].rearrange("p t m j -> p m t j"),
                 w_raw[u][:].rearrange("p j (m t) -> p m t j", t=PACK)[:, :, 2:4],
-            )
-
-        def quantise_weights(lo, hi, rounded):
-            nc.vector.quantize_mx(
-                out=wq[:, lo * P : hi * P].bitcast(FP8X4), scales=ws[:, lo * P : hi * P],
-                in_=rounded,
             )
 
         def project(t, acc, cols):
@@ -111,59 +111,59 @@ def tile_picked_ygpr_none_po_kernel(
             )
             nc.scalar.copy(h[t][:, cols], acc[:, cols])
 
-        round_low(0, nc.scalar.copy)
-        round_high(0, nc.scalar.copy)
-        for u in range(2):
-            project(0, bank(f"back{u}", f"h_ps0_{u}"), slice(256 * u, 256 * u + 256))
-        round_low(1, nc.vector.tensor_copy)
-        round_high(1, nc.scalar.copy)
+        make_half_weights(0, nc.scalar.copy)
+        round_high(0)
+        for part in range(2):
+            project(0, bank(f"back{part}", f"h_ps0_{part}"), slice(part * S // 2, (part + 1) * S // 2))
+        make_half_weights(1, nc.vector.tensor_copy)
+        round_high(1)
         quantise_weights(2, 4, wb_high[:].rearrange("p t m j -> p (t m j)"))
         for t in range(1, PACK):
             project(t, bank(f"acc{t}", f"h_ps{t}"), slice(0, S))
-        h0 = [sb.tile([P, S], F32, name=f"h_c0_{t}") for t in range(2)]
-        for t in range(2):
-            nc.scalar.activation(h0[t][:], h[t][:, :S], COPY, scale=cf_half[t][:, 0:1])
+        h_c0 = [sb.tile([P, S], F32, name=f"h_c0_{u}") for u in range(2)]
+        for u in range(2):
+            nc.scalar.activation(h_c0[u][:], h[u][:, :S], COPY, scale=cf_half[u][:, 0:1])
 
         sums = [bank(f"acc{b}", f"sum{b}") for b in range(BLOCKS)]
-        ggs, g1, g2 = [], [], []
-        g1_tags = ("gg_c1_0", "gg_c1_1", "gg_c1_1", "gg2")
-        g2_tags = ("gg_c2_0", "gg_c2_1", "gg_turned1", "gg_c1_0")
+        gg, gg_c1, gg_c2 = [], [], []
+        c1_tags = ("gg_c1_0", "gg_c1_1", "gg_c1_1", "gg2")
+        c2_tags = ("gg_c2_0", "gg_c2_1", "gg_turned", "gg_c1_0")
 
-        m = [[sb.tile([P, S], F32, name=f"m{t}_{d}", tag=f"m{t}_{d}") for d in range(2)] for t in range(PACK)]
+        terms = [[sb.tile([P, S], F32, name=f"term{t}_{d}", tag=f"term{t}_{d}") for d in range(2)] for t in range(PACK)]
 
         def first_gather(t, d):
-            nc.vector.tensor_tensor(m[t][d][:], h[t][:].indirect(lists[d][:]), gates[d][:], MULT)
+            nc.vector.tensor_tensor(terms[t][d][:], h[t][:].indirect(lists[d][:]), gates[d][:], MULT)
 
-        def scale_gg(t, gg):
-            g2.append(sb.tile([P, S + SPARE], F32, name=f"gg_c2_{t}", tag=g2_tags[t]))
-            nc.gpsimd.memset(g2[t][:, S:], 0.0)
-            nc.scalar.activation(g2[t][:, :S], gg, COPY, scale=c(t, 2))
-            ggs.append(gg)
+        def make_window(t, summed):
+            gg_c2.append(sb.tile([P, S + SPARE], F32, name=f"gg_c2_{t}", tag=c2_tags[t]))
+            nc.gpsimd.memset(gg_c2[t][:, S:], 0.0)
+            nc.scalar.activation(gg_c2[t][:, :S], summed, COPY, scale=c(t, 2))
+            gg.append(summed)
 
         def scale_middle(t):
-            g1.append(sb.tile([P, S], F32, name=f"gg_c1_{t}", tag=g1_tags[t]))
-            nc.scalar.activation(g1[t][:], ggs[t], COPY, scale=c(t, 1))
+            gg_c1.append(sb.tile([P, S], F32, name=f"gg_c1_{t}", tag=c1_tags[t]))
+            nc.scalar.activation(gg_c1[t][:], gg[t], COPY, scale=c(t, 1))
 
-        turned = sb.tile([P, 2, BLOCKS, 2, 64], F32, name="gg_turned1")
+        turned = sb.tile([P, 2, BLOCKS, 2, 64], F32, name="gg_turned")
 
         def sum_half(u):
             fwd = bank(f"fwd{u}", f"fwd{u}")
             for d in range(2):
                 first_gather(u, d)
                 for b in range(BLOCKS):
-                    turn(fwd[:, block(b)], m[u][d][:, block(b)], d == 0 and b == 0, d == 1 and b == BLOCKS - 1)
-            nc.scalar.copy(turned[:, :, :, u, :], fwd[:].rearrange("n (b t p) -> n t b p", b=BLOCKS, t=2))
+                    turn(fwd[:, block(b)], terms[u][d][:, block(b)], d == 0 and b == 0, d == 1 and b == BLOCKS - 1)
+            nc.scalar.copy(turned[:, :, :, u, :], fwd[:].rearrange("n (b t m) -> n t b m", b=BLOCKS, t=2))
 
         def turn_sum_back(t):
             back = bank(f"back{t}", f"back{t}")
             for b in range(BLOCKS):
-                turn(back[:, block(b)], turned[:, t, b].rearrange("n u p -> n (u p)"), True, True)
-            scale_gg(t, back[:])
+                turn(back[:, block(b)], turned[:, t, b].rearrange("n u m -> n (u m)"), True, True)
+            make_window(t, back[:])
 
         def sum_on_vector(t):
-            gg = sb.tile([P, S], F32, name=f"gg{t}")
-            nc.vector.tensor_tensor(gg[:], m[t][0][:], m[t][1][:], ADD)
-            scale_gg(t, gg[:])
+            summed = sb.tile([P, S], F32, name=f"gg{t}")
+            nc.vector.tensor_tensor(summed[:], terms[t][0][:], terms[t][1][:], ADD)
+            make_window(t, summed[:])
 
         def sum_cols(b, t):
             if t < 2:
@@ -172,105 +172,108 @@ def tile_picked_ygpr_none_po_kernel(
 
         def add_term(term, t, blocks, start, stop):
             for b in range(blocks):
-                last = stop and (b == blocks - 1)
-                turn(sum_cols(b, t), term[:, block(b)], start and b == 0, last)
+                turn(sum_cols(b, t), term[:, block(b)], start and b == 0, stop and b == blocks - 1)
 
         for u in range(2):
             sum_half(u)
             for b in range(BLOCKS):
-                pair = sums[b // 2][:].rearrange("n (b t u p) -> n b u t p", b=2, t=2, u=2)
-                turn(pair[:, b % 2, u], h0[u][:, block(b)], u == 0 and b % 2 == 0, False)
+                pair = sums[b // 2][:].rearrange("n (b t u m) -> n b u t m", b=2, t=2, u=2)
+                turn(pair[:, b % 2, u], h_c0[u][:, block(b)], u == 0 and b % 2 == 0, False)
         for t in range(2):
             turn_sum_back(t)
-        h0_late = sb.tile([P, 2, S], F32, name="h_c0_late", tag="m1_1")
+        h_c0_late = sb.tile([P, 2, S], F32, name="h_c0_late", tag="term1_1")
         for t in (2, 3):
-            nc.scalar.activation(h0_late[:, t - 2, :], h[t][:, :S], COPY, scale=c(t, 0))
-            add_term(h0_late[:, t - 2, :], t, BLOCKS, True, False)
+            nc.scalar.activation(h_c0_late[:, t - 2, :], h[t][:, :S], COPY, scale=c(t, 0))
+            add_term(h_c0_late[:, t - 2, :], t, BLOCKS, True, False)
         first_gather(2, 0)
         first_gather(2, 1)
         first_gather(3, 0)
         sum_on_vector(2)
         for t in range(2):
             scale_middle(t)
-            add_term(g1[t], t, BLOCKS, False, False)
+            add_term(gg_c1[t], t, BLOCKS, False, False)
         first_gather(3, 1)
 
         y_rows = out_0.rearrange("(p t) n -> p t n", t=PACK)
         yb = sb.tile([P, S, PACK], BF16, name="yb", align_bytes=64)
         yq = sb.tile([P, S], U32, name="yq", align_bytes=64)
         ys = sb.tile([P, S], U8, name="ys", align_bytes=64)
-        words_out = out_1[0].rearrange("p n t -> p (n t)").bitcast(I32)
+        y = sb.tile([P, PACK, S], F32, name="y")
+        y_back = [None] * PACK
 
-        def second_gather(e, t, d, lo, hi):
-            nc.vector.tensor_tensor(e, g2[t][:].indirect(lists[d][:, lo // 16 : hi // 16]), gates[d][:, lo:hi], MULT)
-
-        def quantise(lo, hi):
-            nc.vector.quantize_mx(
-                out=yq[:, lo:hi].bitcast(FP8X4), scales=ys[:, lo:hi], in_=yb[:, lo:hi, :].rearrange("p n t -> p (n t)")
+        def second_gather(term, t, d, lo, hi):
+            nc.vector.tensor_tensor(
+                term, gg_c2[t][:].indirect(lists[d][:, lo // 16 : hi // 16]), gates[d][:, lo:hi], MULT
             )
 
-        y = sb.tile([P, PACK, S], F32, name="y")
-        backs = [None] * PACK
+        def bring_back_pair():
+            staged = sb.tile([P, 2, S], F32, name="y_turned_pair")
+            for half in (1, 0):
+                nc.scalar.copy(staged[:, half, :], sums[half][:])
+            for t in range(2):
+                y_back[t] = bank(f"back{t}", f"y_back{t}")
+                for b in range(BLOCKS):
+                    turn(y_back[t][:, block(b)], staged[:, b // 2, block(2 * (b % 2) + t)], True, True)
+                nc.scalar.copy(y[:, t, :LAST], y_back[t][:, :LAST])
+            nc.sync.dma_start(y_rows[:, :2, :LAST], y[:, :2, :LAST])
 
-        def come_back(t, staged, blocks):
-            for b in blocks:
-                turn(backs[t][:, block(b)], staged(b), True, True)
+        def bring_back(t, pieces):
+            staged = sb.tile([P, S], F32, name=f"y_turned{t}")
+            y_back[t] = bank(f"fwd{t - 2}", f"y_back{t}")
+            for lo, hi in pieces:
+                nc.scalar.copy(staged[:, lo:hi], sums[t][:, lo:hi])
+                for b in range(lo // P, hi // P):
+                    turn(y_back[t][:, block(b)], staged[:, block(b)], True, True)
+            nc.scalar.copy(y[:, t, :LAST], y_back[t][:, :LAST])
 
         for t in range(PACK):
-            e0 = sb.tile([P, S], F32, name=f"e{t}_0")
-            second_gather(e0[:], t, 0, 0, S)
+            term0 = sb.tile([P, S], F32, name=f"ee{t}_0")
+            second_gather(term0[:], t, 0, 0, S)
             if t == 0:
-                sum_on_vector(PACK - 1)
+                sum_on_vector(3)
                 scale_middle(2)
-                add_term(g1[2], 2, BLOCKS, False, False)
+                add_term(gg_c1[2], 2, BLOCKS, False, False)
                 scale_middle(3)
-            if t == PACK - 1:
-                add_term(g1[t], t, BLOCKS, False, False)
-            add_term(e0, t, BLOCKS, False, t == 1)
-            e1 = sb.tile([P, LAST], F32, name=f"e{t}_1")
-            second_gather(e1[:], t, 1, 0, LAST)
-            add_term(e1, t, LAST // P, False, t > 0)
+            if t == 3:
+                add_term(gg_c1[3], 3, BLOCKS, False, False)
+            add_term(term0, t, BLOCKS, False, t == 1)
+            term1 = sb.tile([P, LAST], F32, name=f"ee{t}_1")
+            second_gather(term1[:], t, 1, 0, LAST)
+            add_term(term1, t, LAST // P, False, t > 0)
             if t == 1:
-                staged = sb.tile([P, 2, S], F32, name="y_turned_pair")
-                for half in (1, 0):
-                    nc.scalar.copy(staged[:, half, :], sums[half][:])
-                for tt in range(2):
-                    backs[tt] = bank(f"back{tt}", f"y_back{tt}")
-                    come_back(tt, lambda b: staged[:, b // 2, block(2 * (b % 2) + tt)], range(BLOCKS))
-                    nc.scalar.copy(y[:, tt, :LAST], backs[tt][:, :LAST])
-                nc.sync.dma_start(y_rows[:, :2, :LAST], y[:, :2, :LAST])
-            if t > 1:
-                staged_t = sb.tile([P, S], F32, name=f"y_turned{t}")
-                backs[t] = bank(f"fwd{t - 2}", f"y_back{t}")
-                for cols in ((slice(0, S),), (slice(0, LAST), slice(LAST, S)))[t == PACK - 1]:
-                    nc.scalar.copy(staged_t[:, cols], sums[t][:, cols])
-                    come_back(t, lambda b: staged_t[:, block(b)], range(cols.start // P, cols.stop // P))
-                nc.scalar.copy(y[:, t, :LAST], backs[t][:, :LAST])
+                bring_back_pair()
+            if t == 2:
+                bring_back(t, ((0, S),))
+            if t == 3:
+                bring_back(t, ((0, LAST), (LAST, S)))
 
         def round_block(b, copy):
             copy(yb[:, block(b), :], y[:, :, block(b)].rearrange("p t n -> p n t"))
 
         for b in range(LAST // P):
             round_block(b, nc.scalar.copy)
-        e_last = sb.tile([P, PACK, S - LAST], F32, name="e_last", tag="gg3")
+
+        term_last = sb.tile([P, PACK, S - LAST], F32, name="ee_last", tag="gg3")
 
         def finish(t):
-            nc.vector.tensor_tensor(y[:, t, LAST:], e_last[:, t, :], backs[t][:, LAST:], ADD)
+            nc.vector.tensor_tensor(y[:, t, LAST:], term_last[:, t, :], y_back[t][:, LAST:], ADD)
             if t == 1:
                 nc.sync.dma_start(y_rows[:, :2, LAST:], y[:, :2, LAST:])
             if t > 1:
                 nc.sync.dma_start(y_rows[:, t, :], y[:, t, :])
 
         for t in range(PACK):
-            second_gather(e_last[:, t, :], t, 1, LAST, S)
+            second_gather(term_last[:, t, :], t, 1, LAST, S)
             if t > 0:
                 finish(t - 1)
         finish(PACK - 1)
         for b in range(LAST // P, BLOCKS):
             round_block(b, nc.vector.tensor_copy)
-        quantise(0, LAST)
-        quantise(LAST, S)
-        nc.sync.dma_start(words_out, yq[:].bitcast(I32))
+        for lo, hi in ((0, LAST), (LAST, S)):
+            nc.vector.quantize_mx(
+                out=yq[:, lo:hi].bitcast(FP8X4), scales=ys[:, lo:hi], in_=yb[:, lo:hi, :].rearrange("p n t -> p (n t)")
+            )
+        nc.sync.dma_start(out_1[0].rearrange("p n t -> p (n t)").bitcast(I32), yq[:].bitcast(I32))
         for q in range(4):
-            eng = nc.sync if q % 2 else nc.scalar
-            eng.dma_start(out_2[0, 4 * q : 4 * q + 4, :].bitcast(I32), ys[32 * q : 32 * q + 4, :].bitcast(I32))
+            queue = nc.sync if q % 2 else nc.scalar
+            queue.dma_start(out_2[0, 4 * q : 4 * q + 4, :].bitcast(I32), ys[32 * q : 32 * q + 4, :].bitcast(I32))

@@ -47,7 +47,7 @@ def tile_picked_ygpr_none_po_kernel(
         picks = sb.tile([P, S // 16], U16, name="picks")
         nc.sync.dma_start(picks[:], offs)
         xs = sb.tile([P, T], U8, name="xs")
-        nc.vector.memset(xs[:].bitcast(I32), 0)
+        nc.gpsimd.memset(xs[:].bitcast(I32), 0)
         for q in range(4):
             nc.sync.dma_start(xs[32 * q : 32 * q + 4, :].bitcast(I32), x_scales[0, 4 * q : 4 * q + 4, :].bitcast(I32))
         w_rows = w1.rearrange("(p j) c -> p j c", j=PACK)
@@ -74,7 +74,7 @@ def tile_picked_ygpr_none_po_kernel(
         make_identity(nc, ident[:])
         h = [sb.tile([P, S + SPARE], F32, name=f"h{t}") for t in range(PACK)]
         for t in range(PACK):
-            nc.vector.memset(h[t][:, S:], 0.0)
+            nc.gpsimd.memset(h[t][:, S:], 0.0)
 
         xq = sb.tile([P, S], U32, name="xq", align_bytes=64)
         nc.vector.tensor_copy(xq[:], xw[:].bitcast(U32).indirect(picks[:]))
@@ -275,5 +275,4 @@ def tile_picked_ygpr_none_po_kernel(
             )
         nc.sync.dma_start(out_1[0].rearrange("p n t -> p (n t)").bitcast(I32), yq[:].bitcast(I32))
         for q in range(4):
-            queue = nc.sync if q % 2 else nc.scalar
-            queue.dma_start(out_2[0, 4 * q : 4 * q + 4, :].bitcast(I32), ys[32 * q : 32 * q + 4, :].bitcast(I32))
+            nc.scalar.dma_start(out_2[0, 4 * q : 4 * q + 4, :].bitcast(I32), ys[32 * q : 32 * q + 4, :].bitcast(I32))

@@ -93,15 +93,15 @@ def tile_picked_ygpr_none_po_kernel(
         def make_half_weights(u, copy):
             wb_low = sb.tile([P, P, PACK], BF16, name=f"wb_low{u}", tag="wb_low", align_bytes=64)
             copy(
-                wb_low[:].rearrange("p (t m) j -> p m t j", t=2),
-                w_raw[u][:].rearrange("p j (m t) -> p m t j", t=PACK)[:, :, 0:2],
+                wb_low[:].rearrange("p (t m) j -> p m j t", t=2),
+                w_raw[u][:].rearrange("p j (m t) -> p m j t", t=PACK)[:, :, :, 0:2],
             )
             quantise_weights(u, u + 1, wb_low[:].rearrange("p m j -> p (m j)"))
 
         def round_high(u):
             nc.scalar.copy(
-                wb_high[:, :, 64 * u : 64 * u + 64, :].rearrange("p t m j -> p m t j"),
-                w_raw[u][:].rearrange("p j (m t) -> p m t j", t=PACK)[:, :, 2:4],
+                wb_high[:, :, 64 * u : 64 * u + 64, :].rearrange("p t m j -> p m j t"),
+                w_raw[u][:].rearrange("p j (m t) -> p m j t", t=PACK)[:, :, :, 2:4],
             )
 
         def project(t, acc, cols):
@@ -136,9 +136,12 @@ def tile_picked_ygpr_none_po_kernel(
 
         def make_window(t, summed):
             gg_c2.append(sb.tile([P, S + SPARE], F32, name=f"gg_c2_{t}", tag=c2_tags[t]))
-            nc.gpsimd.memset(gg_c2[t][:, S:], 0.0)
-            nc.scalar.activation(gg_c2[t][:, :S], summed, COPY, scale=c(t, 2))
-            gg.append(summed)
+            if t < 2:
+                nc.gpsimd.memset(gg_c2[t][:, S:], 0.0)
+                nc.scalar.activation(gg_c2[t][:, :S], summed, COPY, scale=c(t, 2))
+            else:
+                nc.scalar.activation(gg_c2[t][:], summed, COPY, scale=c(t, 2))
+            gg.append(summed[:, :S])
 
         def scale_middle(t):
             gg_c1.append(sb.tile([P, S], F32, name=f"gg_c1_{t}", tag=c1_tags[t]))
@@ -161,8 +164,9 @@ def tile_picked_ygpr_none_po_kernel(
             make_window(t, back[:])
 
         def sum_on_vector(t):
-            summed = sb.tile([P, S], F32, name=f"gg{t}")
-            nc.vector.tensor_tensor(summed[:], terms[t][0][:], terms[t][1][:], ADD)
+            summed = sb.tile([P, S + SPARE], F32, name=f"gg{t}")
+            nc.gpsimd.memset(summed[:, S:], 0.0)
+            nc.vector.tensor_tensor(summed[:, :S], terms[t][0][:], terms[t][1][:], ADD)
             make_window(t, summed[:])
 
         def sum_cols(b, t):
@@ -248,7 +252,10 @@ def tile_picked_ygpr_none_po_kernel(
                 bring_back(t, ((0, LAST), (LAST, S)))
 
         def round_block(b, copy):
-            copy(yb[:, block(b), :], y[:, :, block(b)].rearrange("p t n -> p n t"))
+            copy(
+                yb[:, block(b), :].rearrange("p (c i) t -> p c t i", i=4),
+                y[:, :, block(b)].rearrange("p t (c i) -> p c t i", i=4),
+            )
 
         for b in range(LAST // P):
             round_block(b, nc.scalar.copy)

@@ -62,10 +62,12 @@ def tile_picked_ygpr_none_po_kernel(
             nc.sync.dma_start(gates[d][:], gate[d])
         cf = sb.tile([P, PACK * 3], F32, name="cf")
         nc.sync.dma_start(cf[:], coef.rearrange("(p t) c -> p (t c)", t=PACK))
-        cf_half = [sb.tile([P, 1], F32, name=f"cf_half{u}") for u in range(2)]
-        with nc.allow_non_contiguous_dma(reason="one coefficient a partition"):
-            for u in range(2):
-                nc.sync.dma_start(cf_half[u][:], coef.rearrange("(u m t) c -> u t m c", u=2, t=PACK)[u, 0:2, :, 0:1])
+        cf_half = sb.tile([P, 2, 1], F32, name="cf_half")
+        with nc.allow_non_contiguous_dma(reason="single coefficients"):
+            for t in range(2):
+                nc.sync.dma_start(
+                    cf_half[64 * t : 64 * t + 64], coef.rearrange("(u m t) c -> t m u c", u=2, t=PACK)[t, :, :, 0:1]
+                )
 
         def c(t, depth):
             return cf[:, 3 * t + depth : 3 * t + depth + 1]
@@ -122,7 +124,7 @@ def tile_picked_ygpr_none_po_kernel(
             project(t, bank(f"acc{t}", f"h_ps{t}"), slice(0, S))
         h_c0 = [sb.tile([P, S], F32, name=f"h_c0_{u}") for u in range(2)]
         for u in range(2):
-            nc.scalar.activation(h_c0[u][:], h[u][:, :S], COPY, scale=cf_half[u][:, 0:1])
+            nc.scalar.activation(h_c0[u][:], h[u][:, :S], COPY, scale=cf_half[:, u, :])
 
         sums = [bank(f"acc{b}", f"sum{b}") for b in range(BLOCKS)]
         gg, gg_c1, gg_c2 = [], [], []

@@ -213,13 +213,16 @@ def tile_picked_ygpr_none_po_kernel(
             )
 
         def bring_back_pair():
-            staged = sb.tile([P, 2, S], F32, name="y_turned_pair")
+            staged = [sb.tile([P, S], F32, name=f"y_turned_pair{half}", tag=f"pair{half}") for half in range(2)]
             for half in (1, 0):
-                nc.scalar.copy(staged[:, half, :], sums[half][:])
+                nc.scalar.copy(staged[half][:], sums[half][:])
             for t in range(2):
                 y_back[t] = bank(f"back{t}", f"y_back{t}")
-                for b in range(BLOCKS):
-                    turn(y_back[t][:, block(b)], staged[:, b // 2, block(2 * (b % 2) + t)], True, True)
+            for half in (1, 0):
+                for t in range(2):
+                    for b in (2 * half, 2 * half + 1):
+                        turn(y_back[t][:, block(b)], staged[half][:, block(2 * (b % 2) + t)], True, True)
+            for t in range(2):
                 nc.scalar.copy(y[:, t, :LAST], y_back[t][:, :LAST])
             nc.sync.dma_start(y_rows[:, :2, :LAST], y[:, :2, :LAST])
 
@@ -233,8 +236,15 @@ def tile_picked_ygpr_none_po_kernel(
             nc.scalar.copy(y[:, t, :LAST], y_back[t][:, :LAST])
 
         for t in range(PACK):
-            term0 = sb.tile([P, S], F32, name=f"ee{t}_0")
-            second_gather(term0[:], t, 0, 0, S)
+            if t == 2:
+                rest = sb.tile([P, 2 * (S + LAST) + PACK * (S - LAST)], F32, name="ee_rest", tag="gg3")
+            if t >= 2:
+                term0 = rest[:, (t - 2) * (S + LAST) : (t - 2) * (S + LAST) + S]
+                term1 = rest[:, (t - 2) * (S + LAST) + S : (t - 1) * (S + LAST)]
+            else:
+                term0 = sb.tile([P, S], F32, name=f"ee{t}_0")[:]
+                term1 = sb.tile([P, LAST], F32, name=f"ee{t}_1")[:]
+            second_gather(term0, t, 0, 0, S)
             if t == 0:
                 sum_on_vector(3)
                 scale_middle(2)
@@ -243,8 +253,7 @@ def tile_picked_ygpr_none_po_kernel(
             if t == 3:
                 add_term(gg_c1[3], 3, BLOCKS, False, False)
             add_term(term0, t, BLOCKS, False, t == 1)
-            term1 = sb.tile([P, LAST], F32, name=f"ee{t}_1")
-            second_gather(term1[:], t, 1, 0, LAST)
+            second_gather(term1, t, 1, 0, LAST)
             add_term(term1, t, LAST // P, False, t > 0)
             if t == 1:
                 bring_back_pair()
@@ -262,7 +271,7 @@ def tile_picked_ygpr_none_po_kernel(
         for b in range(LAST // P):
             round_block(b, nc.scalar.copy)
 
-        term_last = sb.tile([P, PACK, S - LAST], F32, name="ee_last", tag="gg3")
+        term_last = rest[:, 2 * (S + LAST) :].rearrange("p (t n) -> p t n", t=PACK)
 
         def finish(t):
             nc.vector.tensor_tensor(y[:, t, LAST:], term_last[:, t, :], y_back[t][:, LAST:], ADD)
@@ -278,7 +287,7 @@ def tile_picked_ygpr_none_po_kernel(
         finish(PACK - 1)
         for b in range(LAST // P, BLOCKS):
             round_block(b, nc.vector.tensor_copy)
-        for lo, hi in ((0, LAST), (LAST, S)):
+        for lo, hi in ((LAST, LAST + P), (0, LAST), (LAST + P, S)):
             nc.vector.quantize_mx(
                 out=yq[:, lo:hi].bitcast(FP8X4), scales=ys[:, lo:hi], in_=yb[:, lo:hi, :].rearrange("p n t -> p (n t)")
             )

@@ -268,17 +268,19 @@ def tile_picked_ygpr_none_po_kernel(
                 y[:, :, block(b)].rearrange("p t (c i) -> p c t i", i=4),
             )
 
+        nc.sync.dma_start(y_rows[:, 2:, :LAST], y[:, 2:, :LAST])
         for b in range(LAST // P):
             round_block(b, nc.scalar.copy)
 
         term_last = rest[:, 2 * (S + LAST) :].rearrange("p (t n) -> p t n", t=PACK)
 
         def finish(t):
-            nc.vector.tensor_tensor(y[:, t, LAST:], term_last[:, t, :], y_back[t][:, LAST:], ADD)
+            for lo, hi in ((LAST, LAST + P), (LAST + P, S)) if t == PACK - 1 else ((LAST, S),):
+                nc.vector.tensor_tensor(y[:, t, lo:hi], term_last[:, t, lo - LAST : hi - LAST], y_back[t][:, lo:hi], ADD)
             if t == 1:
                 nc.sync.dma_start(y_rows[:, :2, LAST:], y[:, :2, LAST:])
-            if t > 1:
-                nc.sync.dma_start(y_rows[:, t, :], y[:, t, :])
+            if t == 3:
+                nc.sync.dma_start(y_rows[:, 2:, LAST:], y[:, 2:, LAST:])
 
         for t in range(PACK):
             second_gather(term_last[:, t, :], t, 1, LAST, S)
@@ -293,4 +295,4 @@ def tile_picked_ygpr_none_po_kernel(
             )
         nc.sync.dma_start(out_1[0].rearrange("p n t -> p (n t)").bitcast(I32), yq[:].bitcast(I32))
         for q in range(4):
-            nc.scalar.dma_start(out_2[0, 4 * q : 4 * q + 4, :].bitcast(I32), ys[32 * q : 32 * q + 4, :].bitcast(I32))
+            (nc.sync if q == 3 else nc.scalar).dma_start(out_2[0, 4 * q : 4 * q + 4, :].bitcast(I32), ys[32 * q : 32 * q + 4, :].bitcast(I32))

@@ -22,7 +22,7 @@ PACK = 4
 HALF = N // 2
 SPARE = 8
 BLOCKS = S // P
-LAST = 256
+MID = S // 2
 
 
 def tile_picked_ygpr_none_po_kernel(
@@ -33,14 +33,26 @@ def tile_picked_ygpr_none_po_kernel(
         sb = ctx.enter_context(tc.tile_pool(name="sb", bufs=1))
         ps = ctx.enter_context(tc.psum_pool(name="ps", bufs=1))
 
-        def bank(tag, name):
-            return ps.tile([P, S], F32, tag=tag, name=name)
+        def bank(n, name):
+            return ps.tile([P, S], F32, tag=f"bank{n}", name=name)
 
-        def turn(out, in_, start, stop):
-            nc.tensor.matmul(out, lhsT=in_, rhs=ident[:], start=start, stop=stop, is_transpose=True)
+        def plain(name):
+            return sb.tile([P, S], F32, name=name)
+
+        def window(name):
+            w = sb.tile([P, S + SPARE], F32, name=name)
+            nc.gpsimd.memset(w[:, S:], 0.0)
+            return w
 
         def block(b):
             return slice(b * P, (b + 1) * P)
+
+        def turn(out, in_, start, stop, blocks=BLOCKS):
+            for b in range(blocks):
+                nc.tensor.matmul(
+                    out[:, block(b)], lhsT=in_[:, block(b)], rhs=ident[:],
+                    start=start and b == 0, stop=stop and b == blocks - 1, is_transpose=True,
+                )
 
         xw = sb.tile([P, T], I32, name="xw")
         nc.sync.dma_start(xw[:], x_words[0].rearrange("p n t -> p (n t)").bitcast(I32))
@@ -60,23 +72,22 @@ def tile_picked_ygpr_none_po_kernel(
         gates = [sb.tile([P, S], F32, name=f"gate{d}") for d in range(2)]
         for d in range(2):
             nc.sync.dma_start(gates[d][:], gate[d])
-        cf = sb.tile([P, PACK * 3], F32, name="cf")
-        nc.sync.dma_start(cf[:], coef.rearrange("(p t) c -> p (t c)", t=PACK))
-        cf_half = sb.tile([P, 2, 1], F32, name="cf_half")
-        with nc.allow_non_contiguous_dma(reason="single coefficients"):
-            for t in range(2):
-                nc.sync.dma_start(
-                    cf_half[64 * t : 64 * t + 64], coef.rearrange("(u m t) c -> t m u c", u=2, t=PACK)[t, :, :, 0:1]
-                )
+        cf_half = [sb.tile([P, 3], F32, name=f"cf_half{u}") for u in range(2)]
+        cf = sb.tile([P, 6], F32, name="cf")
+        with nc.allow_non_contiguous_dma(reason="a few coefficients a partition"):
+            for u in range(2):
+                nc.sync.dma_start(cf_half[u][:], coef.rearrange("(u m t) c -> u m t c", u=2, t=PACK)[u, :, 0:2, :])
+            nc.sync.dma_start(cf[:], coef.rearrange("(p t) c -> p (t c)", t=PACK)[:, 6:12])
 
         def c(t, depth):
-            return cf[:, 3 * t + depth : 3 * t + depth + 1]
+            if t < 2:
+                return cf_half[t][:, depth : depth + 1]
+            return cf[:, 3 * (t - 2) + depth : 3 * (t - 2) + depth + 1]
 
         ident = sb.tile([P, P], F32, name="ident")
         make_identity(nc, ident[:])
-        h = [sb.tile([P, S + SPARE], F32, name=f"h{t}") for t in range(PACK)]
-        for t in range(PACK):
-            nc.gpsimd.memset(h[t][:, S:], 0.0)
+        h = [window(f"h{t}") for t in range(PACK)]
+        second = [window(f"second{t}") for t in range(PACK)]
 
         xq = sb.tile([P, S], U32, name="xq", align_bytes=64)
         nc.vector.tensor_copy(xq[:], xw[:].bitcast(U32).indirect(picks[:]))
@@ -95,7 +106,7 @@ def tile_picked_ygpr_none_po_kernel(
         def make_half_weights(u, copy):
             wb_low = sb.tile([P, P, PACK], BF16, name=f"wb_low{u}", tag="wb_low", align_bytes=64)
             copy(
-                wb_low[:].rearrange("p (t m) j -> p m j t", t=2),
+                wb_low[:].rearrange("p (m t) j -> p m j t", t=2),
                 w_raw[u][:].rearrange("p j (m t) -> p m j t", t=PACK)[:, :, :, 0:2],
             )
             quantise_weights(u, u + 1, wb_low[:].rearrange("p m j -> p (m j)"))
@@ -106,161 +117,135 @@ def tile_picked_ygpr_none_po_kernel(
                 w_raw[u][:].rearrange("p j (m t) -> p m j t", t=PACK)[:, :, :, 2:4],
             )
 
-        def project(t, acc, cols):
+        def multiply(t, acc, cols):
             nc.tensor.matmul_mx(
                 out=acc[:, cols], lhsT=wq[:, block(t)].bitcast(FP8X4), lhsT_scale=ws[:, block(t)],
                 rhs=xq[:, cols].bitcast(FP8X4), rhs_scale=xq_scale[:, cols], start=True, stop=True,
             )
-            nc.scalar.copy(h[t][:, cols], acc[:, cols])
 
         make_half_weights(0, nc.scalar.copy)
         round_high(0)
         for part in range(2):
-            project(0, bank(f"back{part}", f"h_ps0_{part}"), slice(part * S // 2, (part + 1) * S // 2))
+            cols = slice(part * MID, (part + 1) * MID)
+            acc = bank(part, f"h_ps0_{part}")
+            multiply(0, acc, cols)
+            nc.scalar.copy(h[0][:, cols], acc[:, cols])
         make_half_weights(1, nc.vector.tensor_copy)
         round_high(1)
         quantise_weights(2, 4, wb_high[:].rearrange("p t m j -> p (t m j)"))
+        h_ps = [None] + [bank(t + 1, f"h_ps{t}") for t in range(1, PACK)]
         for t in range(1, PACK):
-            project(t, bank(f"acc{t}", f"h_ps{t}"), slice(0, S))
-        h_c0 = [sb.tile([P, S], F32, name=f"h_c0_{u}") for u in range(2)]
-        for u in range(2):
-            nc.scalar.activation(h_c0[u][:], h[u][:, :S], COPY, scale=cf_half[:, u, :])
+            multiply(t, h_ps[t], slice(0, S))
 
-        sums = [bank(f"acc{b}", f"sum{b}") for b in range(BLOCKS)]
-        gg, gg_c1, gg_c2 = [], [], []
-        c1_tags = ("gg_c1_0", "gg_c1_1", "gg_c1_1", "gg2")
-        c2_tags = ("gg_c2_0", "gg_c2_1", "gg_turned", "gg_c1_0")
+        def copy_h(t):
+            nc.scalar.copy(h[t][:, :S], h_ps[t][:])
 
-        terms = [[sb.tile([P, S], F32, name=f"term{t}_{d}", tag=f"term{t}_{d}") for d in range(2)] for t in range(PACK)]
+        gate_t = sb.tile([P, 2, BLOCKS], F32, name="gate_t")
+        for d in range(2):
+            g_ps = bank(5 + d, f"gate_ps{d}")
+            turn(g_ps, gates[d], True, True)
+            nc.vector.tensor_copy(gate_t[:, d, :], g_ps[:].rearrange("n (b j) -> n b j", b=BLOCKS)[:, :, 0])
 
-        def first_gather(t, d):
-            nc.vector.tensor_tensor(terms[t][d][:], h[t][:].indirect(lists[d][:]), gates[d][:], MULT)
+        def fused(out, win, d, lo=0, hi=S):
+            nc.vector.tensor_tensor(out[:, lo:hi], win[:].indirect(lists[d][:, lo // 16 : hi // 16]), gates[d][:, lo:hi], MULT)
 
-        def make_window(t, summed):
-            gg_c2.append(sb.tile([P, S + SPARE], F32, name=f"gg_c2_{t}", tag=c2_tags[t]))
-            if t < 2:
-                nc.gpsimd.memset(gg_c2[t][:, S:], 0.0)
-                nc.scalar.activation(gg_c2[t][:, :S], summed, COPY, scale=c(t, 2))
-            else:
-                nc.scalar.activation(gg_c2[t][:], summed, COPY, scale=c(t, 2))
-            gg.append(summed[:, :S])
+        def scaled(out, in_, t, depth):
+            nc.scalar.activation(out, in_, COPY, scale=c(t, depth))
 
-        def scale_middle(t):
-            gg_c1.append(sb.tile([P, S], F32, name=f"gg_c1_{t}", tag=c1_tags[t]))
-            nc.scalar.activation(gg_c1[t][:], gg[t], COPY, scale=c(t, 1))
-
-        turned = sb.tile([P, 2, BLOCKS, 2, 64], F32, name="gg_turned")
-
-        def sum_half(u):
-            fwd = bank(f"fwd{u}", f"fwd{u}")
-            for d in range(2):
-                first_gather(u, d)
-                for b in range(BLOCKS):
-                    turn(fwd[:, block(b)], terms[u][d][:, block(b)], d == 0 and b == 0, d == 1 and b == BLOCKS - 1)
-            nc.scalar.copy(turned[:, :, :, u, :], fwd[:].rearrange("n (b t m) -> n t b m", b=BLOCKS, t=2))
-
-        def turn_sum_back(t):
-            back = bank(f"back{t}", f"back{t}")
-            for b in range(BLOCKS):
-                turn(back[:, block(b)], turned[:, t, b].rearrange("n u m -> n (u m)"), True, True)
-            make_window(t, back[:])
-
-        def sum_on_vector(t):
-            summed = sb.tile([P, S + SPARE], F32, name=f"gg{t}")
-            nc.gpsimd.memset(summed[:, S:], 0.0)
-            nc.vector.tensor_tensor(summed[:, :S], terms[t][0][:], terms[t][1][:], ADD)
-            make_window(t, summed[:])
-
-        def sum_cols(b, t):
-            if t < 2:
-                return sums[b // 2][:, block(2 * (b % 2) + t)]
-            return sums[t][:, block(b)]
-
-        def add_term(term, t, blocks, start, stop):
-            for b in range(blocks):
-                turn(sum_cols(b, t), term[:, block(b)], start and b == 0, stop and b == blocks - 1)
-
-        for u in range(2):
-            sum_half(u)
-            for b in range(BLOCKS):
-                pair = sums[b // 2][:].rearrange("n (b t u m) -> n b u t m", b=2, t=2, u=2)
-                turn(pair[:, b % 2, u], h_c0[u][:, block(b)], u == 0 and b % 2 == 0, False)
-        for t in range(2):
-            turn_sum_back(t)
-        h_c0_late = sb.tile([P, 2, S], F32, name="h_c0_late", tag="term1_1")
-        for t in (2, 3):
-            nc.scalar.activation(h_c0_late[:, t - 2, :], h[t][:, :S], COPY, scale=c(t, 0))
-            add_term(h_c0_late[:, t - 2, :], t, BLOCKS, True, False)
-        first_gather(2, 0)
-        first_gather(2, 1)
-        first_gather(3, 0)
-        sum_on_vector(2)
-        for t in range(2):
-            scale_middle(t)
-            add_term(gg_c1[t], t, BLOCKS, False, False)
-        first_gather(3, 1)
+        def mix(out, in0, t, depth, in1):
+            nc.vector.scalar_tensor_tensor(out, in0, c(t, depth), in1, MULT, ADD)
 
         y_rows = out_0.rearrange("(p t) n -> p t n", t=PACK)
+        y_half_rows = out_0.rearrange("(u m t) n -> u m t n", u=2, t=PACK)
+        y = sb.tile([P, PACK, S], F32, name="y")
+        y_half = [plain(f"y_half{u}") for u in range(2)]
+
+        def hand_on_half(u):
+            nc.sync.dma_start(y[64 * u : 64 * u + 64, 0:2, :], y_half[u][:])
+            nc.sync.dma_start(y_half_rows[u, :, 0:2, :], y_half[u][:])
+
+        a = [[plain(f"a{t}_{d}") for d in range(2)] for t in range(PACK)]
+        h_c0 = [plain(f"h_c0_{t}") for t in range(PACK)]
+        ee = [None] * PACK
+
+        for t in range(1, PACK):
+            copy_h(t)
+        for t in range(2):
+            scaled(h_c0[t][:], h[t][:, :S], t, 0)
+
+        def first_sum(t, lo=0, hi=S):
+            nc.vector.tensor_tensor(second[t][:, lo:hi], a[t][0][:, lo:hi], a[t][1][:, lo:hi], ADD)
+
+        def low_terms(out, t):
+            mix(out, second[t][:, :S], t, 1, h_c0[t][:])
+
+        swing = sb.tile([P, 2, S], F32, name="swing")
+        got_second = plain("got_second")
+        gated_second = plain("gated_second")
+        low_late = sb.tile([P, 2 * S], F32, name="low_late")
+
+        def second_round_on_scalar(t, banks, blocks):
+            nodes = blocks * P
+            fwd = [bank(banks[d], f"fwd{t}_{d}") for d in range(2)]
+            ee[t] = bank(banks[2], f"ee{t}")
+            got = (swing[:, t % 2, :], got_second[:])
+            gated = (swing[:, (t + 1) % 2, :], low_late[:, 64 : 64 + S] if t == 1 else gated_second[:])
+            for d in range(2):
+                nc.scalar.activation(got[d][:, :nodes], second[t][:].indirect(lists[d][:, : nodes // 16]), COPY)
+                turn(fwd[d], got[d], True, True, blocks)
+            for d in range(2):
+                for b in range(blocks):
+                    nc.scalar.activation(gated[d][:, block(b)], fwd[d][:, block(b)], COPY, scale=gate_t[:, d, b : b + 1])
+                turn(ee[t], gated[d], d == 0, d == 1, blocks)
+
+        low = [plain(f"low{u}") for u in range(2)]
+
+        def finish_half(u):
+            mix(y_half[u][:], ee[u][:], u, 2, low[u][:])
+            hand_on_half(u)
+
+        fused(a[0][0], h[0], 0)
+        for part in range(2):
+            fused(a[0][1], h[0], 1, part * MID, (part + 1) * MID)
+        for part in range(2):
+            first_sum(0, part * MID, (part + 1) * MID)
+        second_round_on_scalar(0, (7, 0, 1), BLOCKS)
+        fused(a[1][0], h[1], 0)
+        fused(a[1][1], h[1], 1)
+        fused(a[2][0], h[2], 0)
+        first_sum(1)
+        second_round_on_scalar(1, (2, 3, 4), BLOCKS)
+        fused(a[2][1], h[2], 1)
+        fused(a[3][0], h[3], 0)
+        first_sum(2)
+        second_round_on_scalar(2, (5, 6, 7), BLOCKS)
+        fused(a[3][1], h[3], 1)
+        low_terms(low[0][:], 0)
+        first_sum(3)
+        second_round_on_scalar(3, (0, 2, 3), BLOCKS // 2)
+        low_terms(low[1][:], 1)
+        for t in (2, 3):
+            nc.vector.tensor_scalar(h_c0[t][:], h[t][:, :S], c(t, 0), None, MULT)
+        finish_half(0)
+        finish_half(1)
+
+        low2, low3 = low_late[:, :S], low_late[:, S:]
+        low_terms(low2, 2)
+        last = [low[1][:, d * MID : (d + 1) * MID] for d in range(2)]
+        for d in range(2):
+            nc.vector.tensor_tensor(last[d], second[3][:].indirect(lists[d][:, MID // 16 :]), gates[d][:, MID:], MULT)
+        low_terms(low3, 3)
+        ee3_high = low[0][:, :MID]
+        nc.vector.tensor_tensor(ee3_high, last[0], last[1], ADD)
+        mix(y[:, 2, :], ee[2][:], 2, 2, low2)
+        nc.sync.dma_start(y_rows[:, 2, :], y[:, 2, :])
+        mix(y[:, 3, MID:], ee3_high, 3, 2, low3[:, MID:])
+        mix(y[:, 3, :MID], ee[3][:, :MID], 3, 2, low3[:, :MID])
+        nc.sync.dma_start(y_rows[:, 3, :], y[:, 3, :])
+
         yb = sb.tile([P, S, PACK], BF16, name="yb", align_bytes=64)
         yq = sb.tile([P, S], U32, name="yq", align_bytes=64)
         ys = sb.tile([P, S], U8, name="ys", align_bytes=64)
-        y = sb.tile([P, PACK, S], F32, name="y")
-        y_back = [None] * PACK
-
-        def second_gather(term, t, d, lo, hi):
-            nc.vector.tensor_tensor(
-                term, gg_c2[t][:].indirect(lists[d][:, lo // 16 : hi // 16]), gates[d][:, lo:hi], MULT
-            )
-
-        def bring_back_pair():
-            staged = [sb.tile([P, S], F32, name=f"y_turned_pair{half}", tag=f"pair{half}") for half in range(2)]
-            for half in (1, 0):
-                nc.scalar.copy(staged[half][:], sums[half][:])
-            for t in range(2):
-                y_back[t] = bank(f"back{t}", f"y_back{t}")
-            for half in (1, 0):
-                for t in range(2):
-                    for b in (2 * half, 2 * half + 1):
-                        turn(y_back[t][:, block(b)], staged[half][:, block(2 * (b % 2) + t)], True, True)
-            for t in range(2):
-                nc.scalar.copy(y[:, t, :LAST], y_back[t][:, :LAST])
-            nc.sync.dma_start(y_rows[:, :2, :LAST], y[:, :2, :LAST])
-
-        def bring_back(t, pieces):
-            staged = sb.tile([P, S], F32, name=f"y_turned{t}")
-            y_back[t] = bank(f"fwd{t - 2}", f"y_back{t}")
-            for lo, hi in pieces:
-                nc.scalar.copy(staged[:, lo:hi], sums[t][:, lo:hi])
-                for b in range(lo // P, hi // P):
-                    turn(y_back[t][:, block(b)], staged[:, block(b)], True, True)
-            nc.scalar.copy(y[:, t, :LAST], y_back[t][:, :LAST])
-
-        for t in range(PACK):
-            if t == 2:
-                rest = sb.tile([P, 2 * (S + LAST) + PACK * (S - LAST)], F32, name="ee_rest", tag="gg3")
-            if t >= 2:
-                term0 = rest[:, (t - 2) * (S + LAST) : (t - 2) * (S + LAST) + S]
-                term1 = rest[:, (t - 2) * (S + LAST) + S : (t - 1) * (S + LAST)]
-            else:
-                term0 = sb.tile([P, S], F32, name=f"ee{t}_0")[:]
-                term1 = sb.tile([P, LAST], F32, name=f"ee{t}_1")[:]
-            second_gather(term0, t, 0, 0, S)
-            if t == 0:
-                sum_on_vector(3)
-                scale_middle(2)
-                add_term(gg_c1[2], 2, BLOCKS, False, False)
-                scale_middle(3)
-            if t == 3:
-                add_term(gg_c1[3], 3, BLOCKS, False, False)
-            add_term(term0, t, BLOCKS, False, t == 1)
-            second_gather(term1, t, 1, 0, LAST)
-            add_term(term1, t, LAST // P, False, t > 0)
-            if t == 1:
-                bring_back_pair()
-            if t == 2:
-                bring_back(t, ((0, S),))
-            if t == 3:
-                bring_back(t, ((0, LAST), (LAST, S)))
 
         def round_block(b, copy):
             copy(
@@ -268,31 +253,17 @@ def tile_picked_ygpr_none_po_kernel(
                 y[:, :, block(b)].rearrange("p t (c i) -> p c t i", i=4),
             )
 
-        nc.sync.dma_start(y_rows[:, 2:, :LAST], y[:, 2:, :LAST])
-        for b in range(LAST // P):
-            round_block(b, nc.scalar.copy)
-
-        term_last = rest[:, 2 * (S + LAST) :].rearrange("p (t n) -> p t n", t=PACK)
-
-        def finish(t):
-            for lo, hi in ((LAST, LAST + P), (LAST + P, S)) if t == PACK - 1 else ((LAST, S),):
-                nc.vector.tensor_tensor(y[:, t, lo:hi], term_last[:, t, lo - LAST : hi - LAST], y_back[t][:, lo:hi], ADD)
-            if t == 1:
-                nc.sync.dma_start(y_rows[:, :2, LAST:], y[:, :2, LAST:])
-            if t == 3:
-                nc.sync.dma_start(y_rows[:, 2:, LAST:], y[:, 2:, LAST:])
-
-        for t in range(PACK):
-            second_gather(term_last[:, t, :], t, 1, LAST, S)
-            if t > 0:
-                finish(t - 1)
-        finish(PACK - 1)
-        for b in range(LAST // P, BLOCKS):
-            round_block(b, nc.vector.tensor_copy)
-        for lo, hi in ((LAST, LAST + P), (0, LAST), (LAST + P, S)):
+        def quantise(lo, hi):
             nc.vector.quantize_mx(
                 out=yq[:, lo:hi].bitcast(FP8X4), scales=ys[:, lo:hi], in_=yb[:, lo:hi, :].rearrange("p n t -> p (n t)")
             )
+
+        round_block(3, nc.scalar.copy)
+        round_block(2, nc.vector.tensor_copy)
+        round_block(0, nc.scalar.copy)
+        round_block(1, nc.vector.tensor_copy)
+        quantise(MID, S)
+        quantise(0, MID)
         nc.sync.dma_start(out_1[0].rearrange("p n t -> p (n t)").bitcast(I32), yq[:].bitcast(I32))
         for q in range(4):
             (nc.sync if q == 3 else nc.scalar).dma_start(out_2[0, 4 * q : 4 * q + 4, :].bitcast(I32), ys[32 * q : 32 * q + 4, :].bitcast(I32))

@@ -170,7 +170,7 @@ def tile_picked_ygpr_none_po_kernel(
 
         for t in range(1, PACK):
             copy_h(t)
-        for t in range(2):
+        for t in range(3):
             scaled(h_c0[t][:], h[t][:, :S], t, 0)
 
         def first_sum(t, lo=0, hi=S):
@@ -179,24 +179,36 @@ def tile_picked_ygpr_none_po_kernel(
         def low_terms(out, t):
             mix(out, second[t][:, :S], t, 1, h_c0[t][:])
 
-        swing = sb.tile([P, 2, S], F32, name="swing")
-        got_second = plain("got_second")
-        gated_second = plain("gated_second")
+        got = sb.tile([P, 2, S], F32, name="got")
+        gated = sb.tile([P, 2, S], F32, name="gated")
         low_late = sb.tile([P, 2 * S], F32, name="low_late")
+        fwd = {}
 
-        def second_round_on_scalar(t, banks, blocks):
-            nodes = blocks * P
-            fwd = [bank(banks[d], f"fwd{t}_{d}") for d in range(2)]
-            ee[t] = bank(banks[2], f"ee{t}")
-            got = (swing[:, t % 2, :], got_second[:])
-            gated = (swing[:, (t + 1) % 2, :], low_late[:, 64 : 64 + S] if t == 1 else gated_second[:])
-            for d in range(2):
-                nc.scalar.activation(got[d][:, :nodes], second[t][:].indirect(lists[d][:, : nodes // 16]), COPY)
-                turn(fwd[d], got[d], True, True, blocks)
-            for d in range(2):
-                for b in range(blocks):
-                    nc.scalar.activation(gated[d][:, block(b)], fwd[d][:, block(b)], COPY, scale=gate_t[:, d, b : b + 1])
-                turn(ee[t], gated[d], d == 0, d == 1, blocks)
+        def blocks_on_scalar(t):
+            return BLOCKS // 2 if t == PACK - 1 else BLOCKS
+
+        def fetch(t, d):
+            nodes = blocks_on_scalar(t) * P
+            fwd[t, d] = bank((7, 0, 2, 6)[(2 * t + d) % 4], f"fwd{t}_{d}")
+            nc.scalar.activation(got[:, d, :nodes], second[t][:].indirect(lists[d][:, : nodes // 16]), COPY)
+            turn(fwd[t, d], got[:, d, :], True, True, blocks_on_scalar(t))
+
+        def weigh(t, d):
+            if d == 0:
+                ee[t] = bank((1, 3, 4, 5)[t], f"ee{t}")
+            out = low_late[:, 64 : 64 + S] if (t, d) == (1, 1) else gated[:, d, :]
+            for b in range(blocks_on_scalar(t)):
+                nc.scalar.activation(out[:, block(b)], fwd[t, d][:, block(b)], COPY, scale=gate_t[:, d, b : b + 1])
+            turn(ee[t], out, d == 0, d == 1, blocks_on_scalar(t))
+
+        def second_round_step(t):
+            fetch(t, 0)
+            if t > 0:
+                weigh(t - 1, 1)
+            fetch(t, 1)
+            weigh(t, 0)
+            if t == PACK - 1:
+                weigh(t, 1)
 
         low = [plain(f"low{u}") for u in range(2)]
 
@@ -204,28 +216,24 @@ def tile_picked_ygpr_none_po_kernel(
             mix(y_half[u][:], ee[u][:], u, 2, low[u][:])
             hand_on_half(u)
 
-        fused(a[0][0], h[0], 0)
-        for part in range(2):
-            fused(a[0][1], h[0], 1, part * MID, (part + 1) * MID)
-        for part in range(2):
-            first_sum(0, part * MID, (part + 1) * MID)
-        second_round_on_scalar(0, (7, 0, 1), BLOCKS)
-        fused(a[1][0], h[1], 0)
-        fused(a[1][1], h[1], 1)
+        for t in range(2):
+            fused(a[t][0], h[t], 0)
+            for part in range(2):
+                fused(a[t][1], h[t], 1, part * MID, (part + 1) * MID)
+            for part in range(2):
+                first_sum(t, part * MID, (part + 1) * MID)
+            second_round_step(t)
         fused(a[2][0], h[2], 0)
-        first_sum(1)
-        second_round_on_scalar(1, (2, 3, 4), BLOCKS)
         fused(a[2][1], h[2], 1)
         fused(a[3][0], h[3], 0)
         first_sum(2)
-        second_round_on_scalar(2, (5, 6, 7), BLOCKS)
+        second_round_step(2)
         fused(a[3][1], h[3], 1)
         low_terms(low[0][:], 0)
         first_sum(3)
-        second_round_on_scalar(3, (0, 2, 3), BLOCKS // 2)
+        second_round_step(3)
         low_terms(low[1][:], 1)
-        for t in (2, 3):
-            nc.vector.tensor_scalar(h_c0[t][:], h[t][:, :S], c(t, 0), None, MULT)
+        nc.vector.tensor_scalar(h_c0[3][:], h[3][:, :S], c(3, 0), None, MULT)
         finish_half(0)
         finish_half(1)
 

@@ -19,10 +19,10 @@ COPY = mybir.ActivationFunctionType.Copy
 
 P = 128
 PACK = 4
-HALF = N // 2
 SPARE = 8
 BLOCKS = S // P
 MID = S // 2
+HALF = N // 2
 
 
 def tile_picked_ygpr_none_po_kernel(
@@ -72,17 +72,11 @@ def tile_picked_ygpr_none_po_kernel(
         gates = [sb.tile([P, S], F32, name=f"gate{d}") for d in range(2)]
         for d in range(2):
             nc.sync.dma_start(gates[d][:], gate[d])
-        cf_half = [sb.tile([P, 3], F32, name=f"cf_half{u}") for u in range(2)]
-        cf = sb.tile([P, 6], F32, name="cf")
-        with nc.allow_non_contiguous_dma(reason="a few coefficients a partition"):
-            for u in range(2):
-                nc.sync.dma_start(cf_half[u][:], coef.rearrange("(u m t) c -> u m t c", u=2, t=PACK)[u, :, 0:2, :])
-            nc.sync.dma_start(cf[:], coef.rearrange("(p t) c -> p (t c)", t=PACK)[:, 6:12])
+        cf = sb.tile([P, PACK * 3], F32, name="cf")
+        nc.sync.dma_start(cf[:], coef.rearrange("(p t) c -> p (t c)", t=PACK))
 
         def c(t, depth):
-            if t < 2:
-                return cf_half[t][:, depth : depth + 1]
-            return cf[:, 3 * (t - 2) + depth : 3 * (t - 2) + depth + 1]
+            return cf[:, 3 * t + depth : 3 * t + depth + 1]
 
         ident = sb.tile([P, P], F32, name="ident")
         make_identity(nc, ident[:])
@@ -94,27 +88,20 @@ def tile_picked_ygpr_none_po_kernel(
         xq_scale = sb.tile([P, S], U8, name="xq_scale", align_bytes=64)
         nc.vector.tensor_copy(xq_scale[:], xs[:].indirect(picks[:]))
 
-        wb_high = sb.tile([P, 2, P, PACK], BF16, name="wb_high", align_bytes=64)
+        wb = sb.tile([P, PACK, P, PACK], BF16, name="wb", align_bytes=64)
         wq = sb.tile([P, N], U32, name="wq", align_bytes=64)
         ws = sb.tile([P, N], U8, name="ws", align_bytes=64)
 
-        def quantise_weights(lo, hi, rounded):
+        def quantise_weights(lo, hi):
             nc.vector.quantize_mx(
-                out=wq[:, lo * P : hi * P].bitcast(FP8X4), scales=ws[:, lo * P : hi * P], in_=rounded
+                out=wq[:, lo * P : hi * P].bitcast(FP8X4), scales=ws[:, lo * P : hi * P],
+                in_=wb[:, lo:hi].rearrange("p t m j -> p (t m j)"),
             )
 
-        def make_half_weights(u, copy):
-            wb_low = sb.tile([P, P, PACK], BF16, name=f"wb_low{u}", tag="wb_low", align_bytes=64)
+        def round_weights(u, lo, hi, copy):
             copy(
-                wb_low[:].rearrange("p (m t) j -> p m j t", t=2),
-                w_raw[u][:].rearrange("p j (m t) -> p m j t", t=PACK)[:, :, :, 0:2],
-            )
-            quantise_weights(u, u + 1, wb_low[:].rearrange("p m j -> p (m j)"))
-
-        def round_high(u):
-            nc.scalar.copy(
-                wb_high[:, :, 64 * u : 64 * u + 64, :].rearrange("p t m j -> p m j t"),
-                w_raw[u][:].rearrange("p j (m t) -> p m j t", t=PACK)[:, :, :, 2:4],
+                wb[:, lo:hi, 64 * u : 64 * u + 64, :].rearrange("p t m j -> p m j t"),
+                w_raw[u][:].rearrange("p j (m t) -> p m j t", t=PACK)[:, :, :, lo:hi],
             )
 
         def multiply(t, acc, cols):
@@ -123,16 +110,16 @@ def tile_picked_ygpr_none_po_kernel(
                 rhs=xq[:, cols].bitcast(FP8X4), rhs_scale=xq_scale[:, cols], start=True, stop=True,
             )
 
-        make_half_weights(0, nc.scalar.copy)
-        round_high(0)
+        round_weights(0, 0, PACK, nc.scalar.copy)
+        round_weights(1, 0, 2, nc.vector.tensor_copy)
+        round_weights(1, 2, PACK, nc.scalar.copy)
+        quantise_weights(0, 1)
         for part in range(2):
             cols = slice(part * MID, (part + 1) * MID)
             acc = bank(part, f"h_ps0_{part}")
             multiply(0, acc, cols)
             nc.scalar.copy(h[0][:, cols], acc[:, cols])
-        make_half_weights(1, nc.vector.tensor_copy)
-        round_high(1)
-        quantise_weights(2, 4, wb_high[:].rearrange("p t m j -> p (t m j)"))
+        quantise_weights(1, 4)
         h_ps = [None] + [bank(t + 1, f"h_ps{t}") for t in range(1, PACK)]
         for t in range(1, PACK):
             multiply(t, h_ps[t], slice(0, S))
@@ -141,8 +128,9 @@ def tile_picked_ygpr_none_po_kernel(
             nc.scalar.copy(h[t][:, :S], h_ps[t][:])
 
         gate_t = sb.tile([P, 2, BLOCKS], F32, name="gate_t")
-        for d in range(2):
-            g_ps = bank(5 + d, f"gate_ps{d}")
+
+        def turn_gate(d):
+            g_ps = bank(d, f"gate_ps{d}")
             turn(g_ps, gates[d], True, True)
             nc.vector.tensor_copy(gate_t[:, d, :], g_ps[:].rearrange("n (b j) -> n b j", b=BLOCKS)[:, :, 0])
 
@@ -156,13 +144,7 @@ def tile_picked_ygpr_none_po_kernel(
             nc.vector.scalar_tensor_tensor(out, in0, c(t, depth), in1, MULT, ADD)
 
         y_rows = out_0.rearrange("(p t) n -> p t n", t=PACK)
-        y_half_rows = out_0.rearrange("(u m t) n -> u m t n", u=2, t=PACK)
         y = sb.tile([P, PACK, S], F32, name="y")
-        y_half = [plain(f"y_half{u}") for u in range(2)]
-
-        def hand_on_half(u):
-            nc.sync.dma_start(y[64 * u : 64 * u + 64, 0:2, :], y_half[u][:])
-            nc.sync.dma_start(y_half_rows[u, :, 0:2, :], y_half[u][:])
 
         a = [[plain(f"a{t}_{d}") for d in range(2)] for t in range(PACK)]
         h_c0 = [plain(f"h_c0_{t}") for t in range(PACK)]
@@ -213,8 +195,8 @@ def tile_picked_ygpr_none_po_kernel(
         low = [plain(f"low{u}") for u in range(2)]
 
         def finish_half(u):
-            mix(y_half[u][:], ee[u][:], u, 2, low[u][:])
-            hand_on_half(u)
+            mix(y[:, u, :], ee[u][:], u, 2, low[u][:])
+            nc.sync.dma_start(y_rows[:, u, :], y[:, u, :])
 
         for t in range(2):
             fused(a[t][0], h[t], 0)
@@ -222,6 +204,9 @@ def tile_picked_ygpr_none_po_kernel(
                 fused(a[t][1], h[t], 1, part * MID, (part + 1) * MID)
             for part in range(2):
                 first_sum(t, part * MID, (part + 1) * MID)
+            if t == 0:
+                turn_gate(0)
+                turn_gate(1)
             second_round_step(t)
         fused(a[2][0], h[2], 0)
         fused(a[2][1], h[2], 1)

@@ -19,10 +19,10 @@ COPY = mybir.ActivationFunctionType.Copy
 
 P = 128
 PACK = 4
+HALF = N // 2
 SPARE = 8
 BLOCKS = S // P
 MID = S // 2
-HALF = N // 2
 
 
 def tile_picked_ygpr_none_po_kernel(
@@ -72,10 +72,16 @@ def tile_picked_ygpr_none_po_kernel(
         gates = [sb.tile([P, S], F32, name=f"gate{d}") for d in range(2)]
         for d in range(2):
             nc.sync.dma_start(gates[d][:], gate[d])
+        cf_half = [sb.tile([P, 2], F32, name=f"cf_half{u}") for u in range(2)]
+        with nc.allow_non_contiguous_dma(reason="two coefficients a partition"):
+            for u in range(2):
+                nc.sync.dma_start(cf_half[u][:], coef.rearrange("(u m t) c -> u m t c", u=2, t=PACK)[u, :, 0:2, 0:2])
         cf = sb.tile([P, PACK * 3], F32, name="cf")
         nc.sync.dma_start(cf[:], coef.rearrange("(p t) c -> p (t c)", t=PACK))
 
         def c(t, depth):
+            if t < 2 and depth < 2:
+                return cf_half[t][:, depth : depth + 1]
             return cf[:, 3 * t + depth : 3 * t + depth + 1]
 
         ident = sb.tile([P, P], F32, name="ident")
@@ -88,20 +94,27 @@ def tile_picked_ygpr_none_po_kernel(
         xq_scale = sb.tile([P, S], U8, name="xq_scale", align_bytes=64)
         nc.vector.tensor_copy(xq_scale[:], xs[:].indirect(picks[:]))
 
-        wb = sb.tile([P, PACK, P, PACK], BF16, name="wb", align_bytes=64)
+        wb_high = sb.tile([P, 2, P, PACK], BF16, name="wb_high", align_bytes=64)
         wq = sb.tile([P, N], U32, name="wq", align_bytes=64)
         ws = sb.tile([P, N], U8, name="ws", align_bytes=64)
 
-        def quantise_weights(lo, hi):
+        def quantise_weights(lo, hi, rounded):
             nc.vector.quantize_mx(
-                out=wq[:, lo * P : hi * P].bitcast(FP8X4), scales=ws[:, lo * P : hi * P],
-                in_=wb[:, lo:hi].rearrange("p t m j -> p (t m j)"),
+                out=wq[:, lo * P : hi * P].bitcast(FP8X4), scales=ws[:, lo * P : hi * P], in_=rounded
             )
 
-        def round_weights(u, lo, hi, copy):
+        def make_half_weights(u, copy):
+            wb_low = sb.tile([P, P, PACK], BF16, name=f"wb_low{u}", tag="wb_low", align_bytes=64)
             copy(
-                wb[:, lo:hi, 64 * u : 64 * u + 64, :].rearrange("p t m j -> p m j t"),
-                w_raw[u][:].rearrange("p j (m t) -> p m j t", t=PACK)[:, :, :, lo:hi],
+                wb_low[:].rearrange("p (m t) j -> p m j t", t=2),
+                w_raw[u][:].rearrange("p j (m t) -> p m j t", t=PACK)[:, :, :, 0:2],
+            )
+            quantise_weights(u, u + 1, wb_low[:].rearrange("p m j -> p (m j)"))
+
+        def round_high(u):
+            nc.scalar.copy(
+                wb_high[:, :, 64 * u : 64 * u + 64, :].rearrange("p t m j -> p m j t"),
+                w_raw[u][:].rearrange("p j (m t) -> p m j t", t=PACK)[:, :, :, 2:4],
             )
 
         def multiply(t, acc, cols):
@@ -110,16 +123,16 @@ def tile_picked_ygpr_none_po_kernel(
                 rhs=xq[:, cols].bitcast(FP8X4), rhs_scale=xq_scale[:, cols], start=True, stop=True,
             )
 
-        round_weights(0, 0, PACK, nc.scalar.copy)
-        round_weights(1, 0, 2, nc.vector.tensor_copy)
-        round_weights(1, 2, PACK, nc.scalar.copy)
-        quantise_weights(0, 1)
+        make_half_weights(0, nc.scalar.copy)
+        round_high(0)
         for part in range(2):
             cols = slice(part * MID, (part + 1) * MID)
             acc = bank(part, f"h_ps0_{part}")
             multiply(0, acc, cols)
-            nc.scalar.copy(h[0][:, cols], acc[:, cols])
-        quantise_weights(1, 4)
+            (nc.scalar.copy if part == 0 else nc.vector.tensor_copy)(h[0][:, cols], acc[:, cols])
+        make_half_weights(1, nc.vector.tensor_copy)
+        round_high(1)
+        quantise_weights(2, 4, wb_high[:].rearrange("p t m j -> p (t m j)"))
         h_ps = [None] + [bank(t + 1, f"h_ps{t}") for t in range(1, PACK)]
         for t in range(1, PACK):
             multiply(t, h_ps[t], slice(0, S))
@@ -130,7 +143,7 @@ def tile_picked_ygpr_none_po_kernel(
         gate_t = sb.tile([P, 2, BLOCKS], F32, name="gate_t")
 
         def turn_gate(d):
-            g_ps = bank(d, f"gate_ps{d}")
+            g_ps = bank(2 + d, f"gate_ps{d}")
             turn(g_ps, gates[d], True, True)
             nc.vector.tensor_copy(gate_t[:, d, :], g_ps[:].rearrange("n (b j) -> n b j", b=BLOCKS)[:, :, 0])
 
@@ -146,95 +159,115 @@ def tile_picked_ygpr_none_po_kernel(
         y_rows = out_0.rearrange("(p t) n -> p t n", t=PACK)
         y = sb.tile([P, PACK, S], F32, name="y")
 
-        a = [[plain(f"a{t}_{d}") for d in range(2)] for t in range(PACK)]
-        h_c0 = [plain(f"h_c0_{t}") for t in range(PACK)]
-        ee = [None] * PACK
+        terms = sb.tile([P, 5 * MID], F32, name="terms")
+        term1 = plain("term1")
+        a = [[terms[:, (PACK - 1 - t) * MID : (PACK + 1 - t) * MID], term1[:]] for t in range(PACK)]
+        h_c0 = [plain(f"h_c0_{t}")[:] for t in range(PACK)]
 
-        for t in range(1, PACK):
-            copy_h(t)
-        for t in range(3):
-            scaled(h_c0[t][:], h[t][:, :S], t, 0)
+        def scale_h(t):
+            scaled(h_c0[t], h[t][:, :S], t, 0)
 
-        def first_sum(t, lo=0, hi=S):
-            nc.vector.tensor_tensor(second[t][:, lo:hi], a[t][0][:, lo:hi], a[t][1][:, lo:hi], ADD)
+        def first_round(t):
+            fused(a[t][0], h[t], 0)
+            for lo in (0, MID):
+                fused(a[t][1], h[t], 1, lo, lo + MID)
+            for lo in (0, MID):
+                cols = slice(lo, lo + MID)
+                nc.vector.tensor_tensor(second[t][:, cols], a[t][0][:, cols], a[t][1][:, cols], ADD)
 
-        def low_terms(out, t):
-            mix(out, second[t][:, :S], t, 1, h_c0[t][:])
+        def low_terms(out, t, cols):
+            mix(out[:, cols], second[t][:, cols], t, 1, h_c0[t][:, cols])
 
         got = sb.tile([P, 2, S], F32, name="got")
-        gated = sb.tile([P, 2, S], F32, name="gated")
-        low_late = sb.tile([P, 2 * S], F32, name="low_late")
-        fwd = {}
+        gated = sb.tile([P, 2, 2 * S], F32, name="gated")
 
-        def blocks_on_scalar(t):
-            return BLOCKS // 2 if t == PACK - 1 else BLOCKS
+        def flip(out, in_, start, stop):
+            nc.tensor.matmul(out, lhsT=in_, rhs=ident[:], start=start, stop=stop, is_transpose=True)
 
-        def fetch(t, d):
-            nodes = blocks_on_scalar(t) * P
-            fwd[t, d] = bank((7, 0, 2, 6)[(2 * t + d) % 4], f"fwd{t}_{d}")
+        def fetch(t, d, blocks, place):
+            nodes = blocks * P
             nc.scalar.activation(got[:, d, :nodes], second[t][:].indirect(lists[d][:, : nodes // 16]), COPY)
-            turn(fwd[t, d], got[:, d, :], True, True, blocks_on_scalar(t))
+            for b in range(blocks):
+                flip(place(b), got[:, d, block(b)], True, True)
 
-        def weigh(t, d):
-            if d == 0:
-                ee[t] = bank((1, 3, 4, 5)[t], f"ee{t}")
-            out = low_late[:, 64 : 64 + S] if (t, d) == (1, 1) else gated[:, d, :]
-            for b in range(blocks_on_scalar(t)):
-                nc.scalar.activation(out[:, block(b)], fwd[t, d][:, block(b)], COPY, scale=gate_t[:, d, b : b + 1])
-            turn(ee[t], out, d == 0, d == 1, blocks_on_scalar(t))
+        def weigh(d, b, out, in_):
+            nc.scalar.activation(out, in_, COPY, scale=gate_t[:, d, b : b + 1])
 
-        def second_round_step(t):
-            fetch(t, 0)
-            if t > 0:
-                weigh(t - 1, 1)
-            fetch(t, 1)
-            weigh(t, 0)
-            if t == PACK - 1:
-                weigh(t, 1)
-
-        low = [plain(f"low{u}") for u in range(2)]
-
-        def finish_half(u):
-            mix(y[:, u, :], ee[u][:], u, 2, low[u][:])
-            nc.sync.dma_start(y_rows[:, u, :], y[:, u, :])
-
-        for t in range(2):
-            fused(a[t][0], h[t], 0)
-            for part in range(2):
-                fused(a[t][1], h[t], 1, part * MID, (part + 1) * MID)
-            for part in range(2):
-                first_sum(t, part * MID, (part + 1) * MID)
-            if t == 0:
+        every = slice(0, S)
+        lower, upper = slice(0, MID), slice(MID, S)
+        copy_h(1)
+        scale_h(0)
+        copy_h(2)
+        scale_h(1)
+        copy_h(3)
+        scale_h(2)
+        pair_fwd = [[bank((7, 0, 1, 5)[2 * d + half], f"pair_fwd{d}_{half}") for half in range(2)] for d in range(2)]
+        for u in range(2):
+            first_round(u)
+            for d in range(2):
+                fetch(u, d, BLOCKS, lambda b: pair_fwd[d][b // 2][:, block(2 * (b % 2) + u)])
+            if u == 0:
                 turn_gate(0)
                 turn_gate(1)
-            second_round_step(t)
-        fused(a[2][0], h[2], 0)
-        fused(a[2][1], h[2], 1)
-        fused(a[3][0], h[3], 0)
-        first_sum(2)
-        second_round_step(2)
-        fused(a[3][1], h[3], 1)
-        low_terms(low[0][:], 0)
-        first_sum(3)
-        second_round_step(3)
-        low_terms(low[1][:], 1)
-        nc.vector.tensor_scalar(h_c0[3][:], h[3][:, :S], c(3, 0), None, MULT)
-        finish_half(0)
-        finish_half(1)
+                scale_h(3)
+        low_half = [plain(f"low_half{u}") for u in range(2)]
+        low_pair = sb.tile([P, 2, S], F32, name="low_pair")
+        for u in range(2):
+            low_terms(low_half[u], u, every)
+            nc.sync.dma_start(low_pair[64 * u : 64 * u + 64], low_half[u][:])
 
-        low2, low3 = low_late[:, :S], low_late[:, S:]
-        low_terms(low2, 2)
-        last = [low[1][:, d * MID : (d + 1) * MID] for d in range(2)]
+        ee = [bank(6, "ee0"), bank(4, "ee1")]
+
+        def weigh_pair(d, out):
+            for b in range(BLOCKS):
+                weigh(
+                    d, b,
+                    out[:, 2 * b * P : 2 * (b + 1) * P].rearrange("n (t u m) -> n t u m", t=2, u=2),
+                    pair_fwd[d][b // 2][:, 2 * (b % 2) * P : 2 * (b % 2 + 1) * P].rearrange("n (u m t) -> n t u m", u=2, t=2),
+                )
+                for t in range(2):
+                    flip(ee[t][:, block(b)], out[:, block(2 * b + t)], d == 0 and b == 0, d == 1 and b == BLOCKS - 1)
+
         for d in range(2):
-            nc.vector.tensor_tensor(last[d], second[3][:].indirect(lists[d][:, MID // 16 :]), gates[d][:, MID:], MULT)
-        low_terms(low3, 3)
-        ee3_high = low[0][:, :MID]
-        nc.vector.tensor_tensor(ee3_high, last[0], last[1], ADD)
-        mix(y[:, 2, :], ee[2][:], 2, 2, low2)
-        nc.sync.dma_start(y_rows[:, 2, :], y[:, 2, :])
-        mix(y[:, 3, MID:], ee3_high, 3, 2, low3[:, MID:])
-        mix(y[:, 3, :MID], ee[3][:, :MID], 3, 2, low3[:, :MID])
-        nc.sync.dma_start(y_rows[:, 3, :], y[:, 3, :])
+            weigh_pair(d, gated[:, d, :])
+        first_round(2)
+        fwd2 = [bank(2 + d, f"fwd2_{d}") for d in range(2)]
+        for d in range(2):
+            fetch(2, d, BLOCKS, lambda b: fwd2[d][:, block(b)])
+        first_round(3)
+        ee.append(bank(7, "ee2"))
+        fwd3 = [bank(d, f"fwd3_{d}") for d in range(2)]
+        for d in range(2):
+            for b in range(BLOCKS):
+                weigh(d, b, gated[:, d, block(b)], fwd2[d][:, block(b)])
+                flip(ee[2][:, block(b)], gated[:, d, block(b)], d == 0 and b == 0, d == 1 and b == BLOCKS - 1)
+            fetch(3, d, BLOCKS // 2, lambda b: fwd3[d][:, block(b)])
+        ee_last = [bank(2, "ee_last0"), bank(5, "ee_last1")]
+        for d in range(2):
+            for b in (1, 0):
+                weigh(d, b, gated[:, d, block(BLOCKS + b)], fwd3[d][:, block(b)])
+                flip(ee_last[b][:, :P], gated[:, d, block(BLOCKS + b)], d == 0, d == 1)
+
+        low2, low3 = plain("low2"), plain("low3")
+        last = [low_half[0][:, d * MID : (d + 1) * MID] for d in range(2)]
+        for d in range(2):
+            nc.vector.tensor_tensor(last[d], second[3][:].indirect(lists[d][:, MID // 16 :]), gates[d][:, upper], MULT)
+        low_terms(low3, 3, upper)
+        ee3_upper = low_half[1][:, lower]
+        nc.vector.tensor_tensor(ee3_upper, last[0], last[1], ADD)
+        for t in range(2):
+            mix(y[:, t, :], ee[t][:], t, 2, low_pair[:, t, :])
+        nc.sync.dma_start(y_rows[:, :2, :], y[:, :2, :])
+        mix(y[:, 3, upper], ee3_upper, 3, 2, low3[:, upper])
+        low_terms(low2, 2, upper)
+        low_terms(low3, 3, lower)
+        mix(y[:, 2, upper], ee[2][:, upper], 2, 2, low2[:, upper])
+        nc.sync.dma_start(y_rows[:, 2:, upper], y[:, 2:, upper])
+        low_terms(low2, 2, lower)
+        mix(y[:, 3, block(1)], ee_last[1][:, :P], 3, 2, low3[:, block(1)])
+        mix(y[:, 2, lower], ee[2][:, lower], 2, 2, low2[:, lower])
+        mix(y[:, 3, block(0)], ee_last[0][:, :P], 3, 2, low3[:, block(0)])
+        nc.sync.dma_start(y_rows[:, 2:, lower], y[:, 2:, lower])
 
         yb = sb.tile([P, S, PACK], BF16, name="yb", align_bytes=64)
         yq = sb.tile([P, S], U32, name="yq", align_bytes=64)
@@ -252,11 +285,12 @@ def tile_picked_ygpr_none_po_kernel(
             )
 
         round_block(3, nc.scalar.copy)
-        round_block(2, nc.vector.tensor_copy)
-        round_block(0, nc.scalar.copy)
-        round_block(1, nc.vector.tensor_copy)
+        round_block(2, nc.scalar.copy)
+        round_block(1, nc.scalar.copy)
         quantise(MID, S)
-        quantise(0, MID)
+        round_block(0, nc.vector.tensor_copy)
+        quantise(P, MID)
+        quantise(0, P)
         nc.sync.dma_start(out_1[0].rearrange("p n t -> p (n t)").bitcast(I32), yq[:].bitcast(I32))
         for q in range(4):
             (nc.sync if q == 3 else nc.scalar).dma_start(out_2[0, 4 * q : 4 * q + 4, :].bitcast(I32), ys[32 * q : 32 * q + 4, :].bitcast(I32))

@@ -32,6 +32,7 @@ def tile_picked_ygpr_none_po_kernel(
     with ExitStack() as ctx:
         sb = ctx.enter_context(tc.tile_pool(name="sb", bufs=1))
         ps = ctx.enter_context(tc.psum_pool(name="ps", bufs=1))
+        shared = ctx.enter_context(tc.tile_pool(name="shared", bufs=1))
 
         def bank(n, name):
             return ps.tile([P, S], F32, tag=f"bank{n}", name=name)
@@ -91,8 +92,8 @@ def tile_picked_ygpr_none_po_kernel(
 
         xq = sb.tile([P, S], U32, name="xq", align_bytes=64)
         nc.vector.tensor_copy(xq[:], xw[:].bitcast(U32).indirect(picks[:]))
-        xq_scale = sb.tile([P, S], U8, name="xq_scale", align_bytes=64)
-        nc.vector.tensor_copy(xq_scale[:], xs[:].indirect(picks[:]))
+        xq_scale = sb.tile([P, S - P], U8, name="xq_scale", align_bytes=64)
+        nc.vector.tensor_copy(xq_scale[:], xs[:].indirect(picks[:, : (S - P) // 16]))
 
         wb_high = sb.tile([P, 2, P, PACK], BF16, name="wb_high", align_bytes=64)
         wq = sb.tile([P, N], U32, name="wq", align_bytes=64)
@@ -104,7 +105,7 @@ def tile_picked_ygpr_none_po_kernel(
             )
 
         def make_half_weights(u, copy):
-            wb_low = sb.tile([P, P, PACK], BF16, name=f"wb_low{u}", tag="wb_low", align_bytes=64)
+            wb_low = shared.tile([P, P, PACK], BF16, name=f"wb_low{u}", align_bytes=64, offset=P * u)
             copy(
                 wb_low[:].rearrange("p (m t) j -> p m j t", t=2),
                 w_raw[u][:].rearrange("p j (m t) -> p m j t", t=PACK)[:, :, :, 0:2],
@@ -117,25 +118,29 @@ def tile_picked_ygpr_none_po_kernel(
                 w_raw[u][:].rearrange("p j (m t) -> p m j t", t=PACK)[:, :, :, 2:4],
             )
 
-        def multiply(t, acc, cols):
+        def multiply(t, acc, lo, hi):
+            scale = xq_scale[:, lo:hi] if hi <= S - P else xq_scale_last[:]
             nc.tensor.matmul_mx(
-                out=acc[:, cols], lhsT=wq[:, block(t)].bitcast(FP8X4), lhsT_scale=ws[:, block(t)],
-                rhs=xq[:, cols].bitcast(FP8X4), rhs_scale=xq_scale[:, cols], start=True, stop=True,
+                out=acc[:, lo:hi], lhsT=wq[:, block(t)].bitcast(FP8X4), lhsT_scale=ws[:, block(t)],
+                rhs=xq[:, lo:hi].bitcast(FP8X4), rhs_scale=scale, start=True, stop=True,
             )
 
+        pieces = ((0, MID), (MID, S - P), (S - P, S))
         make_half_weights(0, nc.scalar.copy)
+        xq_scale_last = shared.tile([P, P], U8, name="xq_scale_last", align_bytes=64, offset=0)
+        nc.vector.tensor_copy(xq_scale_last[:], xs[:].indirect(picks[:, (S - P) // 16 :]))
         round_high(0)
-        for part in range(2):
-            cols = slice(part * MID, (part + 1) * MID)
-            acc = bank(part, f"h_ps0_{part}")
-            multiply(0, acc, cols)
-            (nc.scalar.copy if part == 0 else nc.vector.tensor_copy)(h[0][:, cols], acc[:, cols])
+        for n, (lo, hi) in enumerate(pieces):
+            acc = bank((0, 1, 5)[n], f"h_ps0_{n}")
+            multiply(0, acc, lo, hi)
+            nc.scalar.copy(h[0][:, lo:hi], acc[:, lo:hi])
         make_half_weights(1, nc.vector.tensor_copy)
         round_high(1)
         quantise_weights(2, 4, wb_high[:].rearrange("p t m j -> p (t m j)"))
         h_ps = [None] + [bank(t + 1, f"h_ps{t}") for t in range(1, PACK)]
         for t in range(1, PACK):
-            multiply(t, h_ps[t], slice(0, S))
+            for lo, hi in pieces:
+                multiply(t, h_ps[t], lo, hi)
 
         def copy_h(t):
             nc.scalar.copy(h[t][:, :S], h_ps[t][:])
@@ -159,21 +164,22 @@ def tile_picked_ygpr_none_po_kernel(
         y_rows = out_0.rearrange("(p t) n -> p t n", t=PACK)
         y = sb.tile([P, PACK, S], F32, name="y")
 
-        terms = sb.tile([P, 5 * MID], F32, name="terms")
-        term1 = plain("term1")
-        a = [[terms[:, (PACK - 1 - t) * MID : (PACK + 1 - t) * MID], term1[:]] for t in range(PACK)]
+        terms = [sb.tile([P, 2 * S], F32, name=f"terms{d}") for d in range(2)]
+        a = [[terms[d][:, at * MID : at * MID + S] for d in range(2)] for at in (2, 1, 0, 2)]
         h_c0 = [plain(f"h_c0_{t}")[:] for t in range(PACK)]
 
         def scale_h(t):
             scaled(h_c0[t], h[t][:, :S], t, 0)
 
+        def first_sum(t, cols):
+            nc.vector.tensor_tensor(second[t][:, cols], a[t][0][:, cols], a[t][1][:, cols], ADD)
+
         def first_round(t):
             fused(a[t][0], h[t], 0)
             for lo in (0, MID):
                 fused(a[t][1], h[t], 1, lo, lo + MID)
-            for lo in (0, MID):
-                cols = slice(lo, lo + MID)
-                nc.vector.tensor_tensor(second[t][:, cols], a[t][0][:, cols], a[t][1][:, cols], ADD)
+            for cols in (lower, upper):
+                first_sum(t, cols)
 
         def low_terms(out, t, cols):
             mix(out[:, cols], second[t][:, cols], t, 1, h_c0[t][:, cols])
@@ -230,11 +236,17 @@ def tile_picked_ygpr_none_po_kernel(
 
         for d in range(2):
             weigh_pair(d, gated[:, d, :])
-        first_round(2)
+        fused(a[2][0], h[2], 0)
+        fused(a[2][1], h[2], 1)
+        fused(a[3][0], h[3], 0)
+        first_sum(2, every)
         fwd2 = [bank(2 + d, f"fwd2_{d}") for d in range(2)]
         for d in range(2):
             fetch(2, d, BLOCKS, lambda b: fwd2[d][:, block(b)])
-        first_round(3)
+        fused(a[3][1], h[3], 1)
+        low2, low3 = plain("low2"), plain("low3")
+        low_terms(low2, 2, every)
+        first_sum(3, every)
         ee.append(bank(7, "ee2"))
         fwd3 = [bank(d, f"fwd3_{d}") for d in range(2)]
         for d in range(2):
@@ -248,22 +260,18 @@ def tile_picked_ygpr_none_po_kernel(
                 weigh(d, b, gated[:, d, block(BLOCKS + b)], fwd3[d][:, block(b)])
                 flip(ee_last[b][:, :P], gated[:, d, block(BLOCKS + b)], d == 0, d == 1)
 
-        low2, low3 = plain("low2"), plain("low3")
+        mix(y[:, 0, :], ee[0][:], 0, 2, low_pair[:, 0, :])
         last = [low_half[0][:, d * MID : (d + 1) * MID] for d in range(2)]
         for d in range(2):
             nc.vector.tensor_tensor(last[d], second[3][:].indirect(lists[d][:, MID // 16 :]), gates[d][:, upper], MULT)
-        low_terms(low3, 3, upper)
+        low_terms(low3, 3, every)
         ee3_upper = low_half[1][:, lower]
         nc.vector.tensor_tensor(ee3_upper, last[0], last[1], ADD)
-        for t in range(2):
-            mix(y[:, t, :], ee[t][:], t, 2, low_pair[:, t, :])
+        mix(y[:, 1, :], ee[1][:], 1, 2, low_pair[:, 1, :])
         nc.sync.dma_start(y_rows[:, :2, :], y[:, :2, :])
         mix(y[:, 3, upper], ee3_upper, 3, 2, low3[:, upper])
-        low_terms(low2, 2, upper)
-        low_terms(low3, 3, lower)
         mix(y[:, 2, upper], ee[2][:, upper], 2, 2, low2[:, upper])
         nc.sync.dma_start(y_rows[:, 2:, upper], y[:, 2:, upper])
-        low_terms(low2, 2, lower)
         mix(y[:, 3, block(1)], ee_last[1][:, :P], 3, 2, low3[:, block(1)])
         mix(y[:, 2, lower], ee[2][:, lower], 2, 2, low2[:, lower])
         mix(y[:, 3, block(0)], ee_last[0][:, :P], 3, 2, low3[:, block(0)])
@@ -273,10 +281,10 @@ def tile_picked_ygpr_none_po_kernel(
         yq = sb.tile([P, S], U32, name="yq", align_bytes=64)
         ys = sb.tile([P, S], U8, name="ys", align_bytes=64)
 
-        def round_block(b, copy):
+        def round_nodes(cols, copy):
             copy(
-                yb[:, block(b), :].rearrange("p (c i) t -> p c t i", i=4),
-                y[:, :, block(b)].rearrange("p t (c i) -> p c t i", i=4),
+                yb[:, cols, :].rearrange("p (c i) t -> p c t i", i=4),
+                y[:, :, cols].rearrange("p t (c i) -> p c t i", i=4),
             )
 
         def quantise(lo, hi):
@@ -284,13 +292,11 @@ def tile_picked_ygpr_none_po_kernel(
                 out=yq[:, lo:hi].bitcast(FP8X4), scales=ys[:, lo:hi], in_=yb[:, lo:hi, :].rearrange("p n t -> p (n t)")
             )
 
-        round_block(3, nc.scalar.copy)
-        round_block(2, nc.scalar.copy)
-        round_block(1, nc.scalar.copy)
+        round_nodes(upper, nc.scalar.copy)
+        round_nodes(block(1), nc.vector.tensor_copy)
+        round_nodes(block(0), nc.vector.tensor_copy)
         quantise(MID, S)
-        round_block(0, nc.vector.tensor_copy)
-        quantise(P, MID)
-        quantise(0, P)
+        quantise(0, MID)
         nc.sync.dma_start(out_1[0].rearrange("p n t -> p (n t)").bitcast(I32), yq[:].bitcast(I32))
         for q in range(4):
             (nc.sync if q == 3 else nc.scalar).dma_start(out_2[0, 4 * q : 4 * q + 4, :].bitcast(I32), ys[32 * q : 32 * q + 4, :].bitcast(I32))

@@ -95,7 +95,6 @@ def tile_picked_ygpr_none_po_kernel(
         xq_scale = sb.tile([P, S - P], U8, name="xq_scale", align_bytes=64)
         nc.vector.tensor_copy(xq_scale[:], xs[:].indirect(picks[:, : (S - P) // 16]))
 
-        wb_high = sb.tile([P, 2, P, PACK], BF16, name="wb_high", align_bytes=64)
         wq = sb.tile([P, N], U32, name="wq", align_bytes=64)
         ws = sb.tile([P, N], U8, name="ws", align_bytes=64)
 
@@ -105,18 +104,23 @@ def tile_picked_ygpr_none_po_kernel(
             )
 
         def make_half_weights(u, copy):
-            wb_low = shared.tile([P, P, PACK], BF16, name=f"wb_low{u}", align_bytes=64, offset=P * u)
+            wb_low = shared.tile([P, P, PACK], BF16, name=f"wb_low{u}", align_bytes=64, offset=(1024, 1216)[u])
             copy(
                 wb_low[:].rearrange("p (m t) j -> p m j t", t=2),
                 w_raw[u][:].rearrange("p j (m t) -> p m j t", t=PACK)[:, :, :, 0:2],
             )
             quantise_weights(u, u + 1, wb_low[:].rearrange("p m j -> p (m j)"))
 
-        def round_high(u):
-            nc.scalar.copy(
-                wb_high[:, :, 64 * u : 64 * u + 64, :].rearrange("p t m j -> p m j t"),
+        def make_high_weights(u, rounded, copy):
+            copy(
+                rounded[:].rearrange("p t m j -> p m j t"),
                 w_raw[u][:].rearrange("p j (m t) -> p m j t", t=PACK)[:, :, :, 2:4],
             )
+            for t in (2, 3):
+                cols = slice(t * P + 64 * u, t * P + 64 * u + 64)
+                nc.vector.quantize_mx(
+                    out=wq[:, cols].bitcast(FP8X4), scales=ws[:, cols], in_=rounded[:, t - 2].rearrange("p m j -> p (m j)")
+                )
 
         def multiply(t, acc, lo, hi):
             scale = xq_scale[:, lo:hi] if hi <= S - P else xq_scale_last[:]
@@ -127,16 +131,17 @@ def tile_picked_ygpr_none_po_kernel(
 
         pieces = ((0, MID), (MID, S - P), (S - P, S))
         make_half_weights(0, nc.scalar.copy)
-        xq_scale_last = shared.tile([P, P], U8, name="xq_scale_last", align_bytes=64, offset=0)
+        make_high_weights(0, sb.tile([P, 2, 64, PACK], BF16, name="wb_high0", align_bytes=64), nc.scalar.copy)
+        xq_scale_last = shared.tile([P, P], U8, name="xq_scale_last", align_bytes=64, offset=1088)
         nc.vector.tensor_copy(xq_scale_last[:], xs[:].indirect(picks[:, (S - P) // 16 :]))
-        round_high(0)
         for n, (lo, hi) in enumerate(pieces):
             acc = bank((0, 1, 5)[n], f"h_ps0_{n}")
             multiply(0, acc, lo, hi)
             nc.scalar.copy(h[0][:, lo:hi], acc[:, lo:hi])
         make_half_weights(1, nc.vector.tensor_copy)
-        round_high(1)
-        quantise_weights(2, 4, wb_high[:].rearrange("p t m j -> p (t m j)"))
+        make_high_weights(
+            1, shared.tile([P, 2, 64, PACK], BF16, name="wb_high1", align_bytes=64, offset=64), nc.vector.tensor_copy
+        )
         h_ps = [None] + [bank(t + 1, f"h_ps{t}") for t in range(1, PACK)]
         for t in range(1, PACK):
             for lo, hi in pieces:

@@ -68,15 +68,13 @@ def tile_picked_ygpr_none_po_kernel(
         for u in range(2):
             nc.sync.dma_start(w_raw[u][:], w_rows[:, :, u * HALF : (u + 1) * HALF])
         lists = [sb.tile([P, S // 16], U16, name=f"list{d}") for d in range(2)]
-        nc.sync.dma_start(lists[0][:], pos1)
-        nc.sync.dma_start(lists[1][:], pos2)
         gates = [sb.tile([P, S], F32, name=f"gate{d}") for d in range(2)]
-        for d in range(2):
-            nc.sync.dma_start(gates[d][:], gate[d])
         cf_half = [sb.tile([P, 2], F32, name=f"cf_half{u}") for u in range(2)]
-        with nc.allow_non_contiguous_dma(reason="two coefficients a partition"):
-            for u in range(2):
-                nc.sync.dma_start(cf_half[u][:], coef.rearrange("(u m t) c -> u m t c", u=2, t=PACK)[u, :, 0:2, 0:2])
+        for d, pos in enumerate((pos1, pos2)):
+            nc.sync.dma_start(lists[d][:], pos)
+            with nc.allow_non_contiguous_dma(reason="two coefficients a partition"):
+                nc.sync.dma_start(cf_half[d][:], coef.rearrange("(u m t) c -> u m t c", u=2, t=PACK)[d, :, 0:2, 0:2])
+            nc.sync.dma_start(gates[d][:], gate[d])
         cf = sb.tile([P, PACK * 3], F32, name="cf")
         nc.sync.dma_start(cf[:], coef.rearrange("(p t) c -> p (t c)", t=PACK))
 
@@ -155,7 +153,7 @@ def tile_picked_ygpr_none_po_kernel(
         def turn_gate(d):
             g_ps = bank(2 + d, f"gate_ps{d}")
             turn(g_ps, gates[d], True, True)
-            nc.vector.tensor_copy(gate_t[:, d, :], g_ps[:].rearrange("n (b j) -> n b j", b=BLOCKS)[:, :, 0])
+            nc.scalar.copy(gate_t[:, d, :], g_ps[:].rearrange("n (b j) -> n b j", b=BLOCKS)[:, :, 0])
 
         def fused(out, win, d, lo=0, hi=S):
             nc.vector.tensor_tensor(out[:, lo:hi], win[:].indirect(lists[d][:, lo // 16 : hi // 16]), gates[d][:, lo:hi], MULT)
@@ -171,7 +169,7 @@ def tile_picked_ygpr_none_po_kernel(
 
         terms = [sb.tile([P, 2 * S], F32, name=f"terms{d}") for d in range(2)]
         a = [[terms[d][:, at * MID : at * MID + S] for d in range(2)] for at in (2, 1, 0, 2)]
-        h_c0 = [plain(f"h_c0_{t}")[:] for t in range(PACK)]
+        h_c0 = [plain(f"h_c0_{t}")[:] for t in range(PACK - 1)] + [a[2][0]]
 
         def scale_h(t):
             scaled(h_c0[t], h[t][:, :S], t, 0)
@@ -189,7 +187,8 @@ def tile_picked_ygpr_none_po_kernel(
         def low_terms(out, t, cols):
             mix(out[:, cols], second[t][:, cols], t, 1, h_c0[t][:, cols])
 
-        got = sb.tile([P, 2, S], F32, name="got")
+        got = sb.tile([P, 6 * MID], F32, name="got")
+        got_at = ((0, 2), (1, 3), (2, 4), (4, 5))
         gated = sb.tile([P, 2, 2 * S], F32, name="gated")
 
         def flip(out, in_, start, stop):
@@ -197,57 +196,62 @@ def tile_picked_ygpr_none_po_kernel(
 
         def fetch(t, d, blocks, place):
             nodes = blocks * P
-            nc.scalar.activation(got[:, d, :nodes], second[t][:].indirect(lists[d][:, : nodes // 16]), COPY)
+            values = got[:, got_at[t][d] * MID : got_at[t][d] * MID + nodes]
+            nc.scalar.activation(values, second[t][:].indirect(lists[d][:, : nodes // 16]), COPY)
             for b in range(blocks):
-                flip(place(b), got[:, d, block(b)], True, True)
+                flip(place(b), values[:, block(b)], True, True)
 
         def weigh(d, b, out, in_):
             nc.scalar.activation(out, in_, COPY, scale=gate_t[:, d, b : b + 1])
 
         every = slice(0, S)
         lower, upper = slice(0, MID), slice(MID, S)
-        copy_h(1)
         scale_h(0)
-        copy_h(2)
+        for t in range(1, PACK):
+            copy_h(t)
         scale_h(1)
-        copy_h(3)
         scale_h(2)
-        pair_fwd = [[bank((7, 0, 1, 5)[2 * d + half], f"pair_fwd{d}_{half}") for half in range(2)] for d in range(2)]
+        turn_gate(0)
+        turn_gate(1)
+        ee = [bank(6, "ee0"), bank(4, "ee1")]
+
+        def turn_back(d, b):
+            for t in range(2):
+                flip(ee[t][:, block(b)], gated[:, d, block(2 * b + t)], d == 0 and b == 0, d == 1 and b == BLOCKS - 1)
+
+        def dealt(d, b):
+            return gated[:, d, 2 * b * P : 2 * (b + 1) * P].rearrange("n (t u m) -> n t u m", t=2, u=2)
+
+        fwd0 = [bank(7, "fwd0_0"), bank(0, "fwd1_0")]
+        fwd1 = [bank(1, "pair_fwd0"), bank(5, "pair_fwd1")]
         for u in range(2):
             first_round(u)
-            for d in range(2):
-                fetch(u, d, BLOCKS, lambda b: pair_fwd[d][b // 2][:, block(2 * (b % 2) + u)])
-            if u == 0:
-                turn_gate(0)
-                turn_gate(1)
-                scale_h(3)
+            fetch(u, 0, BLOCKS, lambda b: fwd0[u][:, block(b)])
+            fetch(u, 1, BLOCKS, lambda b: fwd1[b // 2][:, block(2 * (b % 2) + u)])
+            for b in range(BLOCKS):
+                weigh(0, b, dealt(0, b)[:, :, u, :], fwd0[u][:, block(b)].rearrange("n (m t) -> n t m", t=2))
+                if u == 1:
+                    turn_back(0, b)
+        for b in range(BLOCKS):
+            pair = fwd1[b // 2][:, 2 * (b % 2) * P : 2 * (b % 2 + 1) * P]
+            weigh(1, b, dealt(1, b), pair.rearrange("n (u m t) -> n t u m", u=2, t=2))
+            turn_back(1, b)
         low_half = [plain(f"low_half{u}") for u in range(2)]
         low_pair = sb.tile([P, 2, S], F32, name="low_pair")
-        for u in range(2):
+
+        def deal_low(u):
             low_terms(low_half[u], u, every)
             nc.sync.dma_start(low_pair[64 * u : 64 * u + 64], low_half[u][:])
 
-        ee = [bank(6, "ee0"), bank(4, "ee1")]
-
-        def weigh_pair(d, out):
-            for b in range(BLOCKS):
-                weigh(
-                    d, b,
-                    out[:, 2 * b * P : 2 * (b + 1) * P].rearrange("n (t u m) -> n t u m", t=2, u=2),
-                    pair_fwd[d][b // 2][:, 2 * (b % 2) * P : 2 * (b % 2 + 1) * P].rearrange("n (u m t) -> n t u m", u=2, t=2),
-                )
-                for t in range(2):
-                    flip(ee[t][:, block(b)], out[:, block(2 * b + t)], d == 0 and b == 0, d == 1 and b == BLOCKS - 1)
-
-        for d in range(2):
-            weigh_pair(d, gated[:, d, :])
+        deal_low(0)
         fused(a[2][0], h[2], 0)
         fused(a[2][1], h[2], 1)
-        fused(a[3][0], h[3], 0)
+        deal_low(1)
         first_sum(2, every)
         fwd2 = [bank(2 + d, f"fwd2_{d}") for d in range(2)]
         for d in range(2):
             fetch(2, d, BLOCKS, lambda b: fwd2[d][:, block(b)])
+        fused(a[3][0], h[3], 0)
         fused(a[3][1], h[3], 1)
         low2, low3 = plain("low2"), plain("low3")
         low_terms(low2, 2, every)
@@ -265,14 +269,15 @@ def tile_picked_ygpr_none_po_kernel(
                 weigh(d, b, gated[:, d, block(BLOCKS + b)], fwd3[d][:, block(b)])
                 flip(ee_last[b][:, :P], gated[:, d, block(BLOCKS + b)], d == 0, d == 1)
 
-        mix(y[:, 0, :], ee[0][:], 0, 2, low_pair[:, 0, :])
-        last = [low_half[0][:, d * MID : (d + 1) * MID] for d in range(2)]
+        nc.vector.tensor_scalar(h_c0[3], h[3][:, :S], c(3, 0), None, MULT)
+        last = [a[2][1][:, d * MID : (d + 1) * MID] for d in range(2)]
         for d in range(2):
             nc.vector.tensor_tensor(last[d], second[3][:].indirect(lists[d][:, MID // 16 :]), gates[d][:, upper], MULT)
         low_terms(low3, 3, every)
-        ee3_upper = low_half[1][:, lower]
+        ee3_upper = a[3][0][:, lower]
         nc.vector.tensor_tensor(ee3_upper, last[0], last[1], ADD)
-        mix(y[:, 1, :], ee[1][:], 1, 2, low_pair[:, 1, :])
+        for t in range(2):
+            mix(y[:, t, :], ee[t][:], t, 2, low_pair[:, t, :])
         nc.sync.dma_start(y_rows[:, :2, :], y[:, :2, :])
         mix(y[:, 3, upper], ee3_upper, 3, 2, low3[:, upper])
         mix(y[:, 2, upper], ee[2][:, upper], 2, 2, low2[:, upper])

@@ -258,11 +258,15 @@ def tile_picked_ygpr_none_po_kernel(
         first_sum(3, every)
         ee.append(bank(7, "ee2"))
         fwd3 = [bank(d, f"fwd3_{d}") for d in range(2)]
-        for d in range(2):
+        def weigh_tile2(d):
             for b in range(BLOCKS):
                 weigh(d, b, gated[:, d, block(b)], fwd2[d][:, block(b)])
                 flip(ee[2][:, block(b)], gated[:, d, block(b)], d == 0 and b == 0, d == 1 and b == BLOCKS - 1)
+
+        weigh_tile2(0)
+        for d in range(2):
             fetch(3, d, BLOCKS // 2, lambda b: fwd3[d][:, block(b)])
+        weigh_tile2(1)
         ee_last = [bank(2, "ee_last0"), bank(5, "ee_last1")]
         for d in range(2):
             for b in (1, 0):
@@ -305,8 +309,9 @@ def tile_picked_ygpr_none_po_kernel(
         round_nodes(upper, nc.scalar.copy)
         round_nodes(block(1), nc.vector.tensor_copy)
         round_nodes(block(0), nc.vector.tensor_copy)
+        quantise(P, MID)
+        quantise(0, P)
         quantise(MID, S)
-        quantise(0, MID)
         nc.sync.dma_start(out_1[0].rearrange("p n t -> p (n t)").bitcast(I32), yq[:].bitcast(I32))
         for q in range(4):
             (nc.sync if q == 3 else nc.scalar).dma_start(out_2[0, 4 * q : 4 * q + 4, :].bitcast(I32), ys[32 * q : 32 * q + 4, :].bitcast(I32))

@@ -23,6 +23,7 @@ HALF = N // 2
 SPARE = 8
 BLOCKS = S // P
 MID = S // 2
+LATE = 2 * S - 192
 
 
 def tile_picked_ygpr_none_po_kernel(
@@ -169,7 +170,7 @@ def tile_picked_ygpr_none_po_kernel(
 
         terms = [sb.tile([P, 2 * S], F32, name=f"terms{d}") for d in range(2)]
         a = [[terms[d][:, at * MID : at * MID + S] for d in range(2)] for at in (2, 1, 0, 2)]
-        h_c0 = [plain(f"h_c0_{t}")[:] for t in range(PACK - 1)] + [a[2][0]]
+        h_c0 = [plain("h_c0_0")[:], y[:, 1, :], plain("h_c0_2")[:], y[:, 1, :]]
 
         def scale_h(t):
             scaled(h_c0[t], h[t][:, :S], t, 0)
@@ -190,6 +191,8 @@ def tile_picked_ygpr_none_po_kernel(
         got = sb.tile([P, 6 * MID], F32, name="got")
         got_at = ((0, 2), (1, 3), (2, 4), (4, 5))
         gated = sb.tile([P, 2, 2 * S], F32, name="gated")
+        late = sb.tile([P, LATE + MID], F32, name="late")
+        pair_gated = (gated[:, 0, :], late[:, : 2 * S])
 
         def flip(out, in_, start, stop):
             nc.tensor.matmul(out, lhsT=in_, rhs=ident[:], start=start, stop=stop, is_transpose=True)
@@ -217,10 +220,10 @@ def tile_picked_ygpr_none_po_kernel(
 
         def turn_back(d, b):
             for t in range(2):
-                flip(ee[t][:, block(b)], gated[:, d, block(2 * b + t)], d == 0 and b == 0, d == 1 and b == BLOCKS - 1)
+                flip(ee[t][:, block(b)], pair_gated[d][:, block(2 * b + t)], d == 0 and b == 0, d == 1 and b == BLOCKS - 1)
 
         def dealt(d, b):
-            return gated[:, d, 2 * b * P : 2 * (b + 1) * P].rearrange("n (t u m) -> n t u m", t=2, u=2)
+            return pair_gated[d][:, 2 * b * P : 2 * (b + 1) * P].rearrange("n (t u m) -> n t u m", t=2, u=2)
 
         fwd0 = [bank(7, "fwd0_0"), bank(0, "fwd1_0")]
         fwd1 = [bank(1, "pair_fwd0"), bank(5, "pair_fwd1")]
@@ -244,16 +247,17 @@ def tile_picked_ygpr_none_po_kernel(
             nc.sync.dma_start(low_pair[64 * u : 64 * u + 64], low_half[u][:])
 
         deal_low(0)
+        deal_low(1)
         fused(a[2][0], h[2], 0)
         fused(a[2][1], h[2], 1)
-        deal_low(1)
+        nc.vector.tensor_scalar(h_c0[3], h[3][:, :S], c(3, 0), None, MULT)
         first_sum(2, every)
         fwd2 = [bank(2 + d, f"fwd2_{d}") for d in range(2)]
         for d in range(2):
             fetch(2, d, BLOCKS, lambda b: fwd2[d][:, block(b)])
         fused(a[3][0], h[3], 0)
         fused(a[3][1], h[3], 1)
-        low2, low3 = plain("low2"), plain("low3")
+        low2, low3 = plain("low2"), low_pair[:, 0, :]
         low_terms(low2, 2, every)
         first_sum(3, every)
         ee.append(bank(7, "ee2"))
@@ -273,16 +277,18 @@ def tile_picked_ygpr_none_po_kernel(
                 weigh(d, b, gated[:, d, block(BLOCKS + b)], fwd3[d][:, block(b)])
                 flip(ee_last[b][:, :P], gated[:, d, block(BLOCKS + b)], d == 0, d == 1)
 
-        nc.vector.tensor_scalar(h_c0[3], h[3][:, :S], c(3, 0), None, MULT)
-        last = [a[2][1][:, d * MID : (d + 1) * MID] for d in range(2)]
+        def finish_dealt(t):
+            mix(y[:, t, :], ee[t][:], t, 2, low_pair[:, t, :])
+            nc.sync.dma_start(y_rows[:, t, :], y[:, t, :])
+
+        finish_dealt(0)
+        last = [late[:, LATE + (0, -MID)[d] : LATE + (MID, 0)[d]] for d in range(2)]
         for d in range(2):
             nc.vector.tensor_tensor(last[d], second[3][:].indirect(lists[d][:, MID // 16 :]), gates[d][:, upper], MULT)
         low_terms(low3, 3, every)
         ee3_upper = a[3][0][:, lower]
         nc.vector.tensor_tensor(ee3_upper, last[0], last[1], ADD)
-        for t in range(2):
-            mix(y[:, t, :], ee[t][:], t, 2, low_pair[:, t, :])
-        nc.sync.dma_start(y_rows[:, :2, :], y[:, :2, :])
+        finish_dealt(1)
         mix(y[:, 3, upper], ee3_upper, 3, 2, low3[:, upper])
         mix(y[:, 2, upper], ee[2][:, upper], 2, 2, low2[:, upper])
         nc.sync.dma_start(y_rows[:, 2:, upper], y[:, 2:, upper])

@@ -290,12 +290,13 @@ def tile_picked_ygpr_none_po_kernel(
         nc.vector.tensor_tensor(ee3_upper, last[0], last[1], ADD)
         finish_dealt(1)
         mix(y[:, 3, upper], ee3_upper, 3, 2, low3[:, upper])
-        mix(y[:, 2, upper], ee[2][:, upper], 2, 2, low2[:, upper])
-        nc.sync.dma_start(y_rows[:, 2:, upper], y[:, 2:, upper])
-        mix(y[:, 3, block(1)], ee_last[1][:, :P], 3, 2, low3[:, block(1)])
-        mix(y[:, 2, lower], ee[2][:, lower], 2, 2, low2[:, lower])
-        mix(y[:, 3, block(0)], ee_last[0][:, :P], 3, 2, low3[:, block(0)])
-        nc.sync.dma_start(y_rows[:, 2:, lower], y[:, 2:, lower])
+        nc.sync.dma_start(y_rows[:, 3, upper], y[:, 3, upper])
+        for cols in (upper, lower):
+            mix(y[:, 2, cols], ee[2][:, cols], 2, 2, low2[:, cols])
+        nc.sync.dma_start(y_rows[:, 2, :], y[:, 2, :])
+        for b in (1, 0):
+            mix(y[:, 3, block(b)], ee_last[b][:, :P], 3, 2, low3[:, block(b)])
+        nc.sync.dma_start(y_rows[:, 3, lower], y[:, 3, lower])
 
         yb = sb.tile([P, S, PACK], BF16, name="yb", align_bytes=64)
         yq = sb.tile([P, S], U32, name="yq", align_bytes=64)
@@ -317,7 +318,9 @@ def tile_picked_ygpr_none_po_kernel(
         round_nodes(block(0), nc.vector.tensor_copy)
         quantise(P, MID)
         quantise(0, P)
+        words_out = out_1[0].rearrange("p n t -> p (n t)").bitcast(I32)
+        nc.sync.dma_start(words_out[:, lower], yq[:, lower].bitcast(I32))
         quantise(MID, S)
-        nc.sync.dma_start(out_1[0].rearrange("p n t -> p (n t)").bitcast(I32), yq[:].bitcast(I32))
+        nc.sync.dma_start(words_out[:, upper], yq[:, upper].bitcast(I32))
         for q in range(4):
             (nc.sync if q == 3 else nc.scalar).dma_start(out_2[0, 4 * q : 4 * q + 4, :].bitcast(I32), ys[32 * q : 32 * q + 4, :].bitcast(I32))

@@ -36,7 +36,7 @@ def tile_picked_ygpr_none_po_kernel(
         shared = ctx.enter_context(tc.tile_pool(name="shared", bufs=1))
 
         def bank(n, name):
-            return ps.tile([P, S], F32, tag=f"bank{n}", name=name)
+            return ps.tile([P, S], F32, name=name, offset=n * S * 4)
 
         def plain(name):
             return sb.tile([P, S], F32, name=name)
@@ -170,7 +170,8 @@ def tile_picked_ygpr_none_po_kernel(
 
         terms = [sb.tile([P, 2 * S], F32, name=f"terms{d}") for d in range(2)]
         a = [[terms[d][:, at * MID : at * MID + S] for d in range(2)] for at in (2, 1, 0, 2)]
-        h_c0 = [plain("h_c0_0")[:], y[:, 1, :], plain("h_c0_2")[:], y[:, 1, :]]
+        h_c0_late = plain("h_c0_late")
+        h_c0 = [plain("h_c0_0")[:], y[:, 1, :], h_c0_late[:], h_c0_late[:]]
 
         def scale_h(t):
             scaled(h_c0[t], h[t][:, :S], t, 0)
@@ -248,10 +249,7 @@ def tile_picked_ygpr_none_po_kernel(
 
         deal_low(0)
         deal_low(1)
-        fused(a[2][0], h[2], 0)
-        fused(a[2][1], h[2], 1)
-        nc.vector.tensor_scalar(h_c0[3], h[3][:, :S], c(3, 0), None, MULT)
-        first_sum(2, every)
+        first_round(2)
         fwd2 = [bank(2 + d, f"fwd2_{d}") for d in range(2)]
         for d in range(2):
             fetch(2, d, BLOCKS, lambda b: fwd2[d][:, block(b)])
@@ -259,6 +257,7 @@ def tile_picked_ygpr_none_po_kernel(
         fused(a[3][1], h[3], 1)
         low2, low3 = plain("low2"), low_pair[:, 0, :]
         low_terms(low2, 2, every)
+        nc.gpsimd.tensor_scalar(h_c0[3], h[3][:, :S], c(3, 0), -0.0, MULT, ADD)
         first_sum(3, every)
         ee.append(bank(7, "ee2"))
         fwd3 = [bank(d, f"fwd3_{d}") for d in range(2)]
@@ -287,7 +286,7 @@ def tile_picked_ygpr_none_po_kernel(
             nc.vector.tensor_tensor(last[d], second[3][:].indirect(lists[d][:, MID // 16 :]), gates[d][:, upper], MULT)
         low_terms(low3, 3, every)
         ee3_upper = a[3][0][:, lower]
-        nc.vector.tensor_tensor(ee3_upper, last[0], last[1], ADD)
+        nc.gpsimd.tensor_tensor(ee3_upper, last[0], last[1], ADD)
         finish_dealt(1)
         mix(y[:, 3, upper], ee3_upper, 3, 2, low3[:, upper])
         nc.sync.dma_start(y_rows[:, 3, upper], y[:, 3, upper])

from contextlib import ExitStack

import concourse.mybir as mybir
from concourse.masks import make_identity

K, T, S, N = 512, 1024, 512, 512
FLOPS = 2 * K * S * N

F32 = mybir.dt.float32
BF16 = mybir.dt.bfloat16
I32 = mybir.dt.int32
U32 = mybir.dt.uint32
U16 = mybir.dt.uint16
U8 = mybir.dt.uint8
FP8X4 = mybir.dt.float8_e4m3fn_x4
MULT = mybir.AluOpType.mult
ADD = mybir.AluOpType.add
COPY = mybir.ActivationFunctionType.Copy

P = 128
PACK = 4
HALF = N // 2
SPARE = 8
BLOCKS = S // P
MID = S // 2
LATE = 2 * S - 192


def tile_picked_ygpr_none_po_kernel(
    tc, x_words, x_scales, w1, gate, coef, offs, pos1, pos2, out_0, out_1, out_2
):
    nc = tc.nc
    with ExitStack() as ctx:
        sb = ctx.enter_context(tc.tile_pool(name="sb", bufs=1))
        ps = ctx.enter_context(tc.psum_pool(name="ps", bufs=1))
        shared = ctx.enter_context(tc.tile_pool(name="shared", bufs=1))

        def bank(n, name):
            return ps.tile([P, S], F32, name=name, offset=n * S * 4)

        def plain(name):
            return sb.tile([P, S], F32, name=name)

        def window(name):
            w = sb.tile([P, S + SPARE], F32, name=name)
            nc.gpsimd.memset(w[:, S:], 0.0)
            return w

        def block(b):
            return slice(b * P, (b + 1) * P)

        def turn(out, in_, start, stop, blocks=BLOCKS):
            for b in range(blocks):
                nc.tensor.matmul(
                    out[:, block(b)], lhsT=in_[:, block(b)], rhs=ident[:],
                    start=start and b == 0, stop=stop and b == blocks - 1, is_transpose=True,
                )

        xw = sb.tile([P, T], I32, name="xw")
        nc.sync.dma_start(xw[:], x_words[0].rearrange("p n t -> p (n t)").bitcast(I32))
        picks = sb.tile([P, S // 16], U16, name="picks")
        nc.sync.dma_start(picks[:], offs)
        xs = sb.tile([P, T], U8, name="xs")
        nc.gpsimd.memset(xs[:].bitcast(I32), 0)
        for q in range(4):
            nc.sync.dma_start(xs[32 * q : 32 * q + 4, :].bitcast(I32), x_scales[0, 4 * q : 4 * q + 4, :].bitcast(I32))
        w_rows = w1.rearrange("(p j) c -> p j c", j=PACK)
        w_raw = [sb.tile([P, PACK, HALF], F32, name=f"w_raw{u}") for u in range(2)]
        for u in range(2):
            nc.sync.dma_start(w_raw[u][:], w_rows[:, :, u * HALF : (u + 1) * HALF])
        lists = [sb.tile([P, S // 16], U16, name=f"list{d}") for d in range(2)]
        gates = [sb.tile([P, S], F32, name=f"gate{d}") for d in range(2)]
        cf_half = [sb.tile([P, 2], F32, name=f"cf_half{u}") for u in range(2)]
        for d, pos in enumerate((pos1, pos2)):
            nc.sync.dma_start(lists[d][:], pos)
            with nc.allow_non_contiguous_dma(reason="two coefficients a partition"):
                nc.sync.dma_start(cf_half[d][:], coef.rearrange("(u m t) c -> u m t c", u=2, t=PACK)[d, :, 0:2, 0:2])
            nc.sync.dma_start(gates[d][:], gate[d])
        cf = sb.tile([P, PACK * 3], F32, name="cf")
        nc.sync.dma_start(cf[:], coef.rearrange("(p t) c -> p (t c)", t=PACK))

        def c(t, depth):
            if t < 2 and depth < 2:
                return cf_half[t][:, depth : depth + 1]
            return cf[:, 3 * t + depth : 3 * t + depth + 1]

        ident = sb.tile([P, P], F32, name="ident")
        make_identity(nc, ident[:])
        h = [window(f"h{t}") for t in range(PACK)]
        second = [window(f"second{t}") for t in range(PACK)]

        xq = sb.tile([P, S], U32, name="xq", align_bytes=64)
        nc.vector.tensor_copy(xq[:], xw[:].bitcast(U32).indirect(picks[:]))
        xq_scale = sb.tile([P, S - P], U8, name="xq_scale", align_bytes=64)
        nc.vector.tensor_copy(xq_scale[:], xs[:].indirect(picks[:, : (S - P) // 16]))

        wq = sb.tile([P, N], U32, name="wq", align_bytes=64)
        ws = sb.tile([P, N], U8, name="ws", align_bytes=64)

        def quantise_weights(lo, hi, rounded):
            nc.vector.quantize_mx(
                out=wq[:, lo * P : hi * P].bitcast(FP8X4), scales=ws[:, lo * P : hi * P], in_=rounded
            )

        def make_half_weights(u, copy):
            wb_low = shared.tile([P, P, PACK], BF16, name=f"wb_low{u}", align_bytes=64, offset=(1024, 1216)[u])
            copy(
                wb_low[:].rearrange("p (m t) j -> p m j t", t=2),
                w_raw[u][:].rearrange("p j (m t) -> p m j t", t=PACK)[:, :, :, 0:2],
            )
            quantise_weights(u, u + 1, wb_low[:].rearrange("p m j -> p (m j)"))

        def make_high_weights(u, rounded, copy):
            copy(
                rounded[:].rearrange("p t m j -> p m j t"),
                w_raw[u][:].rearrange("p j (m t) -> p m j t", t=PACK)[:, :, :, 2:4],
            )
            for t in (2, 3):
                cols = slice(t * P + 64 * u, t * P + 64 * u + 64)
                nc.vector.quantize_mx(
                    out=wq[:, cols].bitcast(FP8X4), scales=ws[:, cols], in_=rounded[:, t - 2].rearrange("p m j -> p (m j)")
                )

        def multiply(t, acc, lo, hi):
            scale = xq_scale[:, lo:hi] if hi <= S - P else xq_scale_last[:]
            nc.tensor.matmul_mx(
                out=acc[:, lo:hi], lhsT=wq[:, block(t)].bitcast(FP8X4), lhsT_scale=ws[:, block(t)],
                rhs=xq[:, lo:hi].bitcast(FP8X4), rhs_scale=scale, start=True, stop=True,
            )

        pieces = ((0, MID), (MID, S - P), (S - P, S))
        make_half_weights(0, nc.scalar.copy)
        make_high_weights(0, sb.tile([P, 2, 64, PACK], BF16, name="wb_high0", align_bytes=64), nc.scalar.copy)
        xq_scale_last = shared.tile([P, P], U8, name="xq_scale_last", align_bytes=64, offset=1088)
        nc.vector.tensor_copy(xq_scale_last[:], xs[:].indirect(picks[:, (S - P) // 16 :]))
        for n, (lo, hi) in enumerate(pieces):
            acc = bank((0, 1, 5)[n], f"h_ps0_{n}")
            multiply(0, acc, lo, hi)
            nc.scalar.copy(h[0][:, lo:hi], acc[:, lo:hi])
        make_half_weights(1, nc.vector.tensor_copy)
        make_high_weights(
            1, shared.tile([P, 2, 64, PACK], BF16, name="wb_high1", align_bytes=64, offset=64), nc.vector.tensor_copy
        )
        h_ps = [None] + [bank(t + 1, f"h_ps{t}") for t in range(1, PACK)]
        for t in range(1, PACK):
            for lo, hi in pieces:
                multiply(t, h_ps[t], lo, hi)

        def copy_h(t):
            nc.scalar.copy(h[t][:, :S], h_ps[t][:])

        gate_t = sb.tile([P, 2, BLOCKS], F32, name="gate_t")

        def turn_gate(d):
            g_ps = bank(2 + d, f"gate_ps{d}")
            turn(g_ps, gates[d], True, True)
            nc.scalar.copy(gate_t[:, d, :], g_ps[:].rearrange("n (b j) -> n b j", b=BLOCKS)[:, :, 0])

        def fused(out, win, d, lo=0, hi=S):
            nc.vector.tensor_tensor(out[:, lo:hi], win[:].indirect(lists[d][:, lo // 16 : hi // 16]), gates[d][:, lo:hi], MULT)

        def scaled(out, in_, t, depth):
            nc.scalar.activation(out, in_, COPY, scale=c(t, depth))

        def mix(out, in0, t, depth, in1):
            nc.vector.scalar_tensor_tensor(out, in0, c(t, depth), in1, MULT, ADD)

        y_rows = out_0.rearrange("(p t) n -> p t n", t=PACK)
        y = sb.tile([P, PACK, S], F32, name="y")

        terms = [sb.tile([P, 2 * S], F32, name=f"terms{d}") for d in range(2)]
        a = [[terms[d][:, at * MID : at * MID + S] for d in range(2)] for at in (2, 1, 0, 2)]
        h_c0_late = plain("h_c0_late")
        h_c0 = [plain("h_c0_0")[:], y[:, 1, :], h_c0_late[:], h_c0_late[:]]

        def scale_h(t):
            scaled(h_c0[t], h[t][:, :S], t, 0)

        def first_sum(t, cols):
            nc.vector.tensor_tensor(second[t][:, cols], a[t][0][:, cols], a[t][1][:, cols], ADD)

        def first_round(t):
            fused(a[t][0], h[t], 0)
            for lo in (0, MID):
                fused(a[t][1], h[t], 1, lo, lo + MID)
            for cols in (lower, upper):
                first_sum(t, cols)

        def low_terms(out, t, cols):
            mix(out[:, cols], second[t][:, cols], t, 1, h_c0[t][:, cols])

        got = sb.tile([P, 6 * MID], F32, name="got")
        got_at = ((0, 2), (1, 3), (2, 4), (4, 5))
        gated = sb.tile([P, 2, 2 * S], F32, name="gated")
        late = sb.tile([P, LATE + MID], F32, name="late")
        pair_gated = (gated[:, 0, :], late[:, : 2 * S])

        def flip(out, in_, start, stop):
            nc.tensor.matmul(out, lhsT=in_, rhs=ident[:], start=start, stop=stop, is_transpose=True)

        def fetch(t, d, blocks, place):
            nodes = blocks * P
            values = got[:, got_at[t][d] * MID : got_at[t][d] * MID + nodes]
            nc.scalar.activation(values, second[t][:].indirect(lists[d][:, : nodes // 16]), COPY)
            for b in range(blocks):
                flip(place(b), values[:, block(b)], True, True)

        def weigh(d, b, out, in_):
            nc.scalar.activation(out, in_, COPY, scale=gate_t[:, d, b : b + 1])

        every = slice(0, S)
        lower, upper = slice(0, MID), slice(MID, S)
        scale_h(0)
        for t in range(1, PACK):
            copy_h(t)
        scale_h(1)
        scale_h(2)
        turn_gate(0)
        turn_gate(1)
        ee = [bank(6, "ee0"), bank(4, "ee1")]

        def turn_back(d, b):
            for t in range(2):
                flip(ee[t][:, block(b)], pair_gated[d][:, block(2 * b + t)], d == 0 and b == 0, d == 1 and b == BLOCKS - 1)

        def dealt(d, b):
            return pair_gated[d][:, 2 * b * P : 2 * (b + 1) * P].rearrange("n (t u m) -> n t u m", t=2, u=2)

        fwd0 = [bank(7, "fwd0_0"), bank(0, "fwd1_0")]
        fwd1 = [bank(1, "pair_fwd0"), bank(5, "pair_fwd1")]
        for u in range(2):
            first_round(u)
            fetch(u, 0, BLOCKS, lambda b: fwd0[u][:, block(b)])
            fetch(u, 1, BLOCKS, lambda b: fwd1[b // 2][:, block(2 * (b % 2) + u)])
            for b in range(BLOCKS):
                weigh(0, b, dealt(0, b)[:, :, u, :], fwd0[u][:, block(b)].rearrange("n (m t) -> n t m", t=2))
                if u == 1:
                    turn_back(0, b)
        for b in range(BLOCKS):
            pair = fwd1[b // 2][:, 2 * (b % 2) * P : 2 * (b % 2 + 1) * P]
            weigh(1, b, dealt(1, b), pair.rearrange("n (u m t) -> n t u m", u=2, t=2))
            turn_back(1, b)
        low_half = [plain(f"low_half{u}") for u in range(2)]
        low_pair = sb.tile([P, 2, S], F32, name="low_pair")

        def deal_low(u):
            low_terms(low_half[u], u, every)
            nc.sync.dma_start(low_pair[64 * u : 64 * u + 64], low_half[u][:])

        deal_low(0)
        deal_low(1)
        first_round(2)
        fwd2 = [bank(2 + d, f"fwd2_{d}") for d in range(2)]
        for d in range(2):
            fetch(2, d, BLOCKS, lambda b: fwd2[d][:, block(b)])
        fused(a[3][0], h[3], 0)
        fused(a[3][1], h[3], 1)
        low2, low3 = plain("low2"), low_pair[:, 0, :]
        low_terms(low2, 2, every)
        nc.gpsimd.tensor_scalar(h_c0[3], h[3][:, :S], c(3, 0), -0.0, MULT, ADD)
        first_sum(3, every)
        ee.append(bank(7, "ee2"))
        fwd3 = [bank(d, f"fwd3_{d}") for d in range(2)]
        def weigh_tile2(d):
            for b in range(BLOCKS):
                weigh(d, b, gated[:, d, block(b)], fwd2[d][:, block(b)])
                flip(ee[2][:, block(b)], gated[:, d, block(b)], d == 0 and b == 0, d == 1 and b == BLOCKS - 1)

        weigh_tile2(0)
        for d in range(2):
            fetch(3, d, BLOCKS // 2, lambda b: fwd3[d][:, block(b)])
        weigh_tile2(1)
        ee_last = [bank(2, "ee_last0"), bank(5, "ee_last1")]
        for d in range(2):
            for b in (1, 0):
                weigh(d, b, gated[:, d, block(BLOCKS + b)], fwd3[d][:, block(b)])
                flip(ee_last[b][:, :P], gated[:, d, block(BLOCKS + b)], d == 0, d == 1)

        def finish_dealt(t):
            mix(y[:, t, :], ee[t][:], t, 2, low_pair[:, t, :])
            nc.sync.dma_start(y_rows[:, t, :], y[:, t, :])

        finish_dealt(0)
        last = [late[:, LATE + (0, -MID)[d] : LATE + (MID, 0)[d]] for d in range(2)]
        for d in range(2):
            nc.vector.tensor_tensor(last[d], second[3][:].indirect(lists[d][:, MID // 16 :]), gates[d][:, upper], MULT)
        low_terms(low3, 3, every)
        ee3_upper = a[3][0][:, lower]
        nc.gpsimd.tensor_tensor(ee3_upper, last[0], last[1], ADD)
        finish_dealt(1)
        mix(y[:, 3, upper], ee3_upper, 3, 2, low3[:, upper])
        nc.sync.dma_start(y_rows[:, 3, upper], y[:, 3, upper])
        for cols in (upper, lower):
            mix(y[:, 2, cols], ee[2][:, cols], 2, 2, low2[:, cols])
        nc.sync.dma_start(y_rows[:, 2, :], y[:, 2, :])
        for b in (1, 0):
            mix(y[:, 3, block(b)], ee_last[b][:, :P], 3, 2, low3[:, block(b)])
        nc.sync.dma_start(y_rows[:, 3, lower], y[:, 3, lower])

        yb = sb.tile([P, S, PACK], BF16, name="yb", align_bytes=64)
        yq = sb.tile([P, S], U32, name="yq", align_bytes=64)
        ys = sb.tile([P, S], U8, name="ys", align_bytes=64)

        def round_nodes(cols, copy):
            copy(
                yb[:, cols, :].rearrange("p (c i) t -> p c t i", i=4),
                y[:, :, cols].rearrange("p t (c i) -> p c t i", i=4),
            )

        def quantise(lo, hi):
            nc.vector.quantize_mx(
                out=yq[:, lo:hi].bitcast(FP8X4), scales=ys[:, lo:hi], in_=yb[:, lo:hi, :].rearrange("p n t -> p (n t)")
            )

        round_nodes(upper, nc.scalar.copy)
        round_nodes(block(1), nc.vector.tensor_copy)
        round_nodes(block(0), nc.vector.tensor_copy)
        quantise(P, MID)
        quantise(0, P)
        words_out = out_1[0].rearrange("p n t -> p (n t)").bitcast(I32)
        nc.sync.dma_start(words_out[:, lower], yq[:, lower].bitcast(I32))
        quantise(MID, S)
        nc.sync.dma_start(words_out[:, upper], yq[:, upper].bitcast(I32))
        for q in range(4):
            (nc.sync if q == 3 else nc.scalar).dma_start(out_2[0, 4 * q : 4 * q + 4, :].bitcast(I32), ys[32 * q : 32 * q + 4, :].bitcast(I32))
